import numpy as np
import ml_dtypes


def mxq(x, axis, fmt="e4m3"):
    dtype, down = {"e4m3": (ml_dtypes.float8_e4m3fn, 7), "e5m2": (ml_dtypes.float8_e5m2, 14)}[fmt]
    v = np.moveaxis(np.asarray(x, np.float32).astype(ml_dtypes.bfloat16).astype(np.float64), axis, -1)
    blocks = v.reshape(v.shape[:-1] + (-1, 32))
    amax = np.abs(blocks).max(-1, keepdims=True)
    byte = np.maximum(np.where(amax > 0, np.frexp(amax)[1] - 1 + 127, 0) - down, 1)
    scale = np.exp2(byte - 127.0)
    codes = (blocks / scale).astype(np.float32).astype(dtype).astype(np.float64)
    return np.moveaxis((codes * scale).reshape(v.shape), -1, axis)


WIDE = False


def mx_kscale(k):
    if not WIDE:
        return np.ones(k)
    levels = np.array([24, -24, 12, -12, 0])
    if k % 512:
        return np.exp2(np.random.permutation(np.resize(levels, k // 32))).repeat(32)
    a = np.empty((k // 512, 16))
    for p in range(k // 512):
        a[p, :8] = np.random.permutation(np.resize(levels, 8))
        for g in range(8):
            far = levels[np.abs(levels - a[p, g]) >= 10]
            a[p, g + 8] = far[np.random.randint(len(far))]
    return np.exp2(a.ravel()).repeat(32)


def f64(x):
    return np.asarray(x).astype(np.float64)


def striped(idx):
    return np.tile(idx.reshape(-1, 16).T, (8, 1)).astype(np.uint16)


def unstriped(offs):
    return offs[:16].T.reshape(-1).astype(np.int64)


E2M1 = np.array([0.0, 0.5, 1.0, 1.5, 2.0, 3.0, 4.0, 6.0, -0.0, -0.5, -1.0, -1.5, -2.0, -3.0, -4.0, -6.0])


def pack_weight(w, fmt):
    k, n = w.shape
    w = f64(np.asarray(w, np.float32).astype(ml_dtypes.bfloat16)).reshape(k // 32, 32, n)
    amax = np.abs(w).max(1)
    if fmt == "e4m3":
        byte = np.frexp(amax)[1] - 1 + 127 - 7
    else:
        mant, ex = np.frexp(amax / 6.0)
        byte = np.where(mant > 0.5, ex, ex - 1) + 127
    byte = np.clip(np.where(amax > 0, byte, 1), 1, 254)
    scaled = (w * np.exp2(127.0 - byte)[:, None, :]).reshape(k, n).astype(np.float32)
    by_word = np.ascontiguousarray(scaled.reshape(k // 512, 128, 4, n).transpose(0, 1, 3, 2))
    if fmt == "e4m3":
        words = by_word.astype(ml_dtypes.float8_e4m3fn).view(np.uint8)
    else:
        c = by_word.astype(ml_dtypes.float4_e2m1fn).view(np.uint8) & 0xF
        words = (c[..., 0::2] | (c[..., 1::2] << 4)).reshape(k // 512, 128, 2 * n)
    return np.ascontiguousarray(words), np.ascontiguousarray(byte.astype(np.uint8).reshape(k // 512, 16, n))


def unpack_weight(words, scales, fmt):
    g, _, n = scales.shape
    words = np.ascontiguousarray(words).reshape(g, 128, n, -1)
    if fmt == "e4m3":
        vals = words.view(ml_dtypes.float8_e4m3fn).astype(np.float64)
    else:
        nib = np.empty((g, 128, n, 4), np.uint8)
        nib[..., 0::2] = words & 0xF
        nib[..., 1::2] = words >> 4
        vals = E2M1[nib]
    vals = vals * np.repeat(np.exp2(scales.astype(np.float64) - 127.0), 8, axis=1)[..., None]
    return vals.transpose(0, 1, 3, 2).reshape(g * 512, n)


def pack_table4(v):
    words, scales = pack_weight(v, "e2m1")
    g, t = words.shape[0] // 2, v.shape[1]
    return np.ascontiguousarray(words.reshape(g, 2, 128, t, 2).transpose(0, 2, 3, 1, 4).reshape(g, 128, t, 4)), scales


def unpack_table4(words, scales):
    g, _, t, _ = words.shape
    return unpack_weight(words.reshape(g, 128, t, 2, 2).transpose(0, 3, 1, 2, 4).reshape(2 * g, 128, 2 * t), scales, "e2m1")


def planes(y):
    n, m = y.shape
    v = y.astype(np.float32).astype(ml_dtypes.bfloat16).astype(np.float64).reshape(n // 32, 32, m)
    top = np.abs(v).max(1)
    byte = np.clip(np.where(top > 0, np.frexp(top)[1] - 1 + 127 - 7, 1), 1, 254)
    codes = (v * np.exp2(127.0 - byte)[:, None, :]).reshape(n, m).astype(np.float32).astype(ml_dtypes.float8_e4m3fn).view(np.uint8)
    words = codes.reshape(n // 512, 128, 4, m).transpose(0, 1, 3, 2)
    return np.ascontiguousarray(words), np.ascontiguousarray(byte.astype(np.uint8).reshape(n // 512, 16, m))


def gelu(f):
    return 0.5 * f * (1.0 + np.tanh(np.sqrt(2.0 / np.pi) * (f + 0.044715 * f**3)))


K, R, N, T, J = 1024, 512, 512, 2048, 1024


def setup_inputs():
    n = np.random.standard_normal
    s = mx_kscale(K)[:, None]
    u = mx_kscale(R)[:, None]
    p_tab = pack_table4(n((K, T)) * s)
    p_wt = pack_weight(n((K, R)) / np.sqrt(2 * K) / s, "e4m3")
    return {
        "tab_words": p_tab[0],
        "tab_scales": p_tab[1],
        "ws": (n((K, R)) / np.sqrt(2 * K) / s).astype(np.float32),
        "wt_words": p_wt[0],
        "wt_scales": p_wt[1],
        "sm": (np.random.uniform(0.5, 2.0, R) * u[:, 0]).astype(np.float32),
        "wd": (n((R, N)) / np.sqrt(R) / u).astype(np.float32),
        "gT": (n((N, T))).astype(np.float32),
        "wgo": np.tile(np.random.uniform(0.5, 2.0, J), (128, 1)).astype(np.float32),
        "offs": striped(np.random.permutation(T)[:J]),
        "offs2": striped(np.random.permutation(T)[:J]),
    }


def reference(tab_words, tab_scales, ws, wt_words, wt_scales, sm, wd, gT, wgo, offs, offs2):
    idx = unstriped(offs)
    idx2 = unstriped(offs2)
    tab_ = unpack_table4(tab_words, tab_scales)[:, idx]
    tabb_ = unpack_table4(tab_words, tab_scales)[:, idx2]
    ws_ = mxq(f64(ws), 0, "e4m3")
    wt_ = unpack_weight(wt_words, wt_scales, "e4m3")
    a = ws_.T @ tab_ + wt_.T @ tabb_
    h = f64(sm)[:, None] * gelu(a)
    h_ = mxq(h, 0, "e4m3")
    wd_ = mxq(f64(wd), 0, "e4m3")
    y = wd_.T @ h_
    out = np.zeros((N, T))
    out[:, idx2] = f64(wgo)[0] * (y * f64(gT)[:, idx])
    return (out,) + planes(out)

@@ -1,0 +1,284 @@
+from contextlib import ExitStack
+
+import concourse.mybir as mybir
+
+K, R, N, T, J = 1024, 512, 512, 2048, 1024
+FLOPS = 2 * J * R * (2 * K + N)
+
+F32 = mybir.dt.float32
+BF16 = mybir.dt.bfloat16
+I32 = mybir.dt.int32
+U32 = mybir.dt.uint32
+U16 = mybir.dt.uint16
+U8 = mybir.dt.uint8
+FP8X4 = mybir.dt.float8_e4m3fn_x4
+FP4X4 = mybir.dt.float4_e2m1fn_x4
+MULT = mybir.AluOpType.mult
+GELU = mybir.ActivationFunctionType.Gelu_apprx_tanh
+COPY = mybir.ActivationFunctionType.Copy
+
+P = 128
+PACK = 4
+QUADS = 4
+HALF = 512
+HALVES = J // HALF
+LIST_ROWS = 16
+OUT_CHUNKS = (256, 512, 512, 512, 256)
+VECTOR_CHUNKS = 3
+ORDER = (2, 0, 1, 3)
+
+
+def tile_list_msg_gelu_gateP_kernel(tc, tab_words, tab_scales, ws, wt_words, wt_scales, sm, wd, gT, wgo, offs, offs2, out_0, out_1, out_2):
+    nc = tc.nc
+
+    with ExitStack() as ctx:
+        keep = ctx.enter_context(tc.tile_pool(name="keep", bufs=1))
+        psum = ctx.enter_context(tc.psum_pool(name="psum", bufs=1))
+
+        def tile(name, shape, dtype, tag=None):
+            return keep.tile(shape, dtype, name=name, tag=tag or name, align_bytes=64)
+
+        src_list = tile("src_list", [P, J // LIST_ROWS], U16)
+        dst_list = tile("dst_list", [P, J // LIST_ROWS], U16)
+        lists = (src_list, dst_list)
+        nc.sync.dma_start(src_list[:], offs)
+        nc.sync.dma_start(dst_list[:], offs2)
+
+        first, second, third, last = ORDER
+        tab_s = tile("tab_s", [P, T], U8, tag="gate%d" % last)
+        wt_s_raw = tile("wt_s_raw", [P, 2 * R], U8)
+        moved = tile("moved", [P, HALVES, 2 * HALF], U8)
+        nc.vector.memset(tab_s[:].bitcast(I32), 0)
+        nc.vector.memset(wt_s_raw[:].bitcast(I32), 0)
+        nc.vector.memset(moved[:].bitcast(I32), 0)
+        tab_w = tile("tab_w", [P, T], I32)
+        nc.sync.dma_start(out=tab_w[:], in_=tab_words[0].rearrange("p t i -> p (t i)").bitcast(I32))
+        for q in range(QUADS):
+            nc.sync.dma_start(
+                out=tab_s[32 * q : 32 * q + 8, :].bitcast(I32),
+                in_=tab_scales[:, 4 * q : 4 * q + 4, :].bitcast(I32),
+            )
+        ws_raw = []
+        for a in range(2):
+            raw = tile("ws_raw%d" % a, [P, PACK, R], F32, tag="gate%d" % ORDER[a])
+            nc.sync.dma_start(out=raw[:], in_=ws[512 * a : 512 * (a + 1), :].rearrange("(p j) r -> p j r", j=PACK))
+            ws_raw.append(raw)
+        wt_w_raw = tile("wt_w_raw", [P, 2, R], I32, tag="gate%d" % third)
+        nc.sync.dma_start(out=wt_w_raw[:], in_=wt_words.rearrange("a p r i -> p a (r i)").bitcast(I32))
+        for q in range(QUADS):
+            nc.sync.dma_start(
+                out=wt_s_raw[32 * q : 32 * q + 4, :].bitcast(I32).rearrange("q (a r) -> q a r", a=2),
+                in_=wt_scales[:, 4 * q : 4 * q + 4, :].bitcast(I32).rearrange("a q r -> q a r"),
+            )
+        wd_raw = tile("wd_raw", [P, PACK, N], F32)
+        nc.sync.dma_start(out=wd_raw[:], in_=wd.rearrange("(p j) n -> p j n", j=PACK))
+        sm_t = tile("sm_t", [P, PACK], F32)
+        nc.sync.dma_start(out=sm_t[:], in_=sm.rearrange("(p t) -> p t", t=PACK))
+        wgo_t = tile("wgo_t", [P, J], F32)
+        nc.sync.dma_start(out=wgo_t[:], in_=wgo)
+
+        pages = {}
+        for t in ORDER[:3]:
+            pages[t] = tile("page%d" % t, [P, T], F32)
+            nc.vector.memset(pages[t][:], 0.0)
+
+        def round_and_deal(dst, raw):
+            nc.scalar.copy(
+                out=dst.rearrange("p (t m j) -> p m j t", t=PACK, j=PACK),
+                in_=raw[:].rearrange("p j (m t) -> p m j t", t=PACK),
+            )
+
+        def list_cols(h):
+            return slice(h * HALF // LIST_ROWS, (h + 1) * HALF // LIST_ROWS)
+
+        def gather_scales(h, tag=None):
+            packed = tile("v_s%d" % h, [P, 2, HALF], U8, tag=tag)
+            for u in range(2):
+                nc.vector.tensor_copy(packed[:, u, :], tab_s[:].indirect(lists[u][:, list_cols(h)]))
+            rows = packed[:].rearrange("p u n -> p (u n)").bitcast(I32)
+            for q in range(QUADS):
+                nc.sync.dma_start(out=moved[32 * q : 32 * q + 4, h, :].bitcast(I32), in_=rows[32 * q + 4 : 32 * q + 8, :])
+            return [[packed[:, u, :] for u in range(2)], [moved[:, h, u * HALF : (u + 1) * HALF] for u in range(2)]]
+
+        def gather_words(h, tag=None):
+            pairs = tile("pairs%d" % h, [P, 2, HALF], U32, tag=tag)
+            for u in range(2):
+                nc.vector.tensor_copy(pairs[:, u, :], tab_w[:].bitcast(U32).indirect(lists[u][:, list_cols(h)]))
+            return pairs
+
+        def part_words(h, pairs):
+            parted = tile("v_w%d" % h, [P, 2, 2, 2 * HALF], U8)
+            for u in range(2):
+                nc.vector.tensor_copy(
+                    parted[:, u].bitcast(U16),
+                    pairs[:, u, :].bitcast(U16).rearrange("p (n d) -> p d n", d=2),
+                )
+            return parted
+
+        v_s = [gather_scales(0)]
+        v_w = [part_words(0, gather_words(0))]
+
+        wt_w = tile("wt_w", [P, 2, R], I32)
+        wt_s = tile("wt_s", [P, 2, R], U8)
+        nc.vector.tensor_copy(
+            wt_w[:].rearrange("p a (t m) -> p a m t", t=PACK), wt_w_raw[:].rearrange("p a (m t) -> p a m t", t=PACK)
+        )
+        nc.vector.tensor_copy(
+            wt_s[:].rearrange("p a (t m) -> p a m t", t=PACK), wt_s_raw[:].rearrange("p (a m t) -> p a m t", a=2, t=PACK)
+        )
+
+        ws_w = tile("ws_w", [P, 2, R], U32)
+        ws_s = tile("ws_s", [P, 2, R], U8)
+        ws_bf = tile("ws_bf", [P, 2, PACK * R], BF16)
+        for a in range(2):
+            round_and_deal(ws_bf[:, a, :], ws_raw[a])
+        nc.vector.quantize_mx(
+            out=ws_w[:].rearrange("p a r -> p (a r)").bitcast(FP8X4),
+            scales=ws_s[:].rearrange("p a r -> p (a r)"),
+            in_=ws_bf[:].rearrange("p a r -> p (a r)"),
+        )
+
+        pairs1 = gather_words(1, "ws_bf")
+        v_s.append(gather_scales(1, "tab_w"))
+        v_w.append(part_words(1, pairs1))
+
+        wd_bf = tile("wd_bf", [P, PACK * N], BF16)
+        round_and_deal(wd_bf[:], wd_raw)
+        wd_w = tile("wd_w", [P, N], U32)
+        wd_s = tile("wd_s", [P, N], U8)
+        nc.vector.quantize_mx(out=wd_w[:].bitcast(FP8X4), scales=wd_s[:], in_=wd_bf[:])
+
+        gates = {}
+        g_rows = gT.rearrange("(p t) c -> t p c", t=PACK)
+        for t in ORDER:
+            gates[t] = tile("gate%d" % t, [P, T], F32)
+            nc.sync.dma_start(out=gates[t][:], in_=g_rows[t])
+
+        def first_stage(h):
+            act = tile("act%d" % h, [P, PACK, HALF], F32, tag="act")
+            planes = tile("h_planes%d" % h, [P, PACK, HALF], BF16)
+            for t in range(PACK):
+                acc = psum.tile([P, HALF], F32, name="a%d%d" % (h, t), tag="bank%d" % (PACK * h + t))
+                m_cols = slice(t * P, (t + 1) * P)
+                steps = [(a, u) for a in range(2) for u in (1, 0)]
+                for i, (a, u) in enumerate(steps):
+                    w_w, w_s = ((ws_w, ws_s), (wt_w, wt_s))[u]
+                    nc.tensor.matmul_mx(
+                        out=acc[:],
+                        lhsT=w_w[:, a, m_cols].bitcast(FP8X4),
+                        lhsT_scale=w_s[:, a, m_cols],
+                        rhs=v_w[h][:, u, a, :].bitcast(FP4X4),
+                        rhs_scale=v_s[h][a][u],
+                        start=(i == 0),
+                        stop=(i == len(steps) - 1),
+                    )
+                nc.scalar.activation(out=act[:, t, :], in_=acc[:], func=GELU)
+                nc.scalar.activation(out=planes[:, t, :], in_=act[:, t, :], func=COPY, scale=sm_t[:, t : t + 1])
+            return planes
+
+        def weave(h, planes):
+            woven = tile("h_bf%d" % h, [P, HALF, PACK], BF16)
+            nc.scalar.copy(
+                out=woven[:].rearrange("p (c i) t -> p c t i", i=4),
+                in_=planes[:].rearrange("p t (c i) -> p c t i", i=4),
+            )
+            return woven
+
+        def quantise_hidden(h, woven, tag):
+            h_w = tile("h_w%d" % h, [P, HALF], U32, tag=tag)
+            h_s = tile("h_s%d" % h, [P, HALF], U8)
+            nc.vector.quantize_mx(out=h_w[:].bitcast(FP8X4), scales=h_s[:], in_=woven[:].rearrange("p c t -> p (c t)"))
+            return h_w, h_s
+
+        def second_stage(h, t, hidden):
+            acc = psum.tile([P, HALF], F32, name="y%d%d" % (h, t), tag="bank%d" % (PACK * h + t))
+            m_cols = slice(t * P, (t + 1) * P)
+            nc.tensor.matmul_mx(
+                out=acc[:],
+                lhsT=wd_w[:, m_cols].bitcast(FP8X4),
+                lhsT_scale=wd_s[:, m_cols],
+                rhs=hidden[0][:].bitcast(FP8X4),
+                rhs_scale=hidden[1][:],
+                start=True,
+                stop=True,
+            )
+            return acc
+
+        factors = {}
+
+        def gather_gate(t, tag=None):
+            factors[t] = tile("factor%d" % t, [P, J], F32, tag=tag)
+            nc.vector.tensor_tensor(factors[t][:], gates[t][:].indirect(src_list[:]), wgo_t[:], MULT)
+
+        out_rows = out_0.rearrange("(p t) c -> t p c", t=PACK)
+        out_bf = tile("out_bf", [P, T, PACK], BF16)
+        starts = [sum(OUT_CHUNKS[:i]) for i in range(len(OUT_CHUNKS) + 1)]
+        chunks = [slice(starts[i], starts[i + 1]) for i in range(len(OUT_CHUNKS))]
+        split = starts[VECTOR_CHUNKS]
+
+        def copy_out(name, accs, tag=None):
+            y = tile(name, [P, len(accs) * HALF], F32, tag=tag)
+            for i, acc in enumerate(accs):
+                nc.scalar.copy(out=y[:, i * HALF : (i + 1) * HALF], in_=acc[:])
+            return y
+
+        def scatter(t, y, h=None):
+            offsets = dst_list[:] if h is None else dst_list[:, list_cols(h)]
+            factor = factors[t][:] if h is None else factors[t][:, h * HALF : (h + 1) * HALF]
+            nc.vector.tensor_tensor(pages[t][:].indirect(offsets), y[:], factor, MULT)
+
+        def finish_page(t):
+            nc.sync.dma_start(out=out_rows[t], in_=pages[t][:])
+            if t != last:
+                for cols in (slice(0, split), slice(split, T)):
+                    nc.scalar.copy(out=out_bf[:, cols, t], in_=pages[t][:, cols])
+
+        woven0 = weave(0, first_stage(0))
+        planes1 = first_stage(1)
+        gather_gate(first)
+        gather_gate(second)
+
+        hidden0 = quantise_hidden(0, woven0, "gate%d" % second)
+        y_first0 = copy_out("y_first0", [second_stage(0, first, hidden0)], "act")
+        woven1 = weave(1, planes1)
+        y_second0 = copy_out("y_second0", [second_stage(0, second, hidden0)])
+        gather_gate(third, "h_bf0")
+        scatter(first, y_first0, 0)
+        hidden1 = quantise_hidden(1, woven1, "act")
+        scatter(second, y_second0, 0)
+        y_first1 = copy_out("y_first1", [second_stage(1, first, hidden1)])
+        y_second1 = copy_out("y_second1", [second_stage(1, second, hidden1)])
+        y_third = copy_out("y_third", [second_stage(0, third, hidden0), second_stage(1, third, hidden1)])
+        y_last = copy_out("y_last", [second_stage(0, last, hidden0), second_stage(1, last, hidden1)])
+        pages[last] = tile("page%d" % last, [P, T], F32, tag="act")
+        nc.gpsimd.memset(pages[last][:], 0.0)
+
+        scatter(first, y_first1, 1)
+        finish_page(first)
+        scatter(second, y_second1, 1)
+        finish_page(second)
+        scatter(third, y_third)
+        finish_page(third)
+        gather_gate(last, "page%d" % first)
+        scatter(last, y_last)
+        finish_page(last)
+        for cols in chunks[VECTOR_CHUNKS:]:
+            nc.scalar.copy(out=out_bf[:, cols, last], in_=pages[last][:, cols])
+
+        out_w = tile("out_w", [P, T], U32)
+        out_s = tile("out_s", [P, T], U8)
+        code_rows = out_1[0].rearrange("p t i -> p (t i)").bitcast(I32)
+        for i in range(len(chunks) + 1):
+            if i < VECTOR_CHUNKS:
+                nc.vector.tensor_copy(out_bf[:, chunks[i], last], pages[last][:, chunks[i]])
+            if i > 0:
+                cols = chunks[i - 1]
+                nc.vector.quantize_mx(
+                    out=out_w[:, cols].bitcast(FP8X4),
+                    scales=out_s[:, cols],
+                    in_=out_bf[:, cols, :].rearrange("p c t -> p (c t)"),
+                )
+                nc.sync.dma_start(out=code_rows[:, cols], in_=out_w[:, cols].bitcast(I32))
+        for q in range(QUADS):
+            queue = nc.scalar if q % 2 else nc.sync
+            queue.dma_start(out=out_2[0, 4 * q : 4 * q + 4, :].bitcast(I32), in_=out_s[32 * q : 32 * q + 4, :].bitcast(I32))

@@ -25,6 +25,7 @@ HALVES = J // HALF
 LIST_ROWS = 16
 OUT_CHUNKS = (256, 512, 512, 512, 256)
 VECTOR_CHUNKS = 3
+TABLE_PIECE = 512
 ORDER = (2, 0, 1, 3)
 
 
@@ -45,22 +46,29 @@ def tile_list_msg_gelu_gateP_kernel(tc, tab_words, tab_scales, ws, wt_words, wt_
         nc.sync.dma_start(dst_list[:], offs2)
 
         first, second, third, last = ORDER
-        tab_s = tile("tab_s", [P, T], U8, tag="gate%d" % last)
-        wt_s_raw = tile("wt_s_raw", [P, 2 * R], U8)
-        moved = tile("moved", [P, HALVES, 2 * HALF], U8)
-        nc.vector.memset(tab_s[:].bitcast(I32), 0)
-        nc.vector.memset(wt_s_raw[:].bitcast(I32), 0)
-        nc.vector.memset(moved[:].bitcast(I32), 0)
+        tab_s = tile("tab_s", [P, T], U8, tag="gate%d" % first)
+        wt_s_raw = tile("wt_s_raw", [P, 2 * R], U8, tag="gate%d" % last)
+        moved = tile("moved", [P, 2 * J], U8)
+        nc.gpsimd.memset(tab_s[:].bitcast(I32), 0)
+        nc.gpsimd.memset(wt_s_raw[:].bitcast(I32), 0)
+        nc.gpsimd.memset(moved[:].bitcast(I32), 0)
         tab_w = tile("tab_w", [P, T], I32)
-        nc.sync.dma_start(out=tab_w[:], in_=tab_words[0].rearrange("p t i -> p (t i)").bitcast(I32))
+        sm_t = tile("sm_t", [P, PACK], F32)
+        nc.sync.dma_start(out=sm_t[:], in_=sm.rearrange("(p t) -> p t", t=PACK))
+        tab_rows = tab_words[0].rearrange("p t i -> p (t i)").bitcast(I32)
+        for c in range(0, T, TABLE_PIECE):
+            nc.sync.dma_start(out=tab_w[:, c : c + TABLE_PIECE], in_=tab_rows[:, c : c + TABLE_PIECE])
         for q in range(QUADS):
             nc.sync.dma_start(
                 out=tab_s[32 * q : 32 * q + 8, :].bitcast(I32),
                 in_=tab_scales[:, 4 * q : 4 * q + 4, :].bitcast(I32),
             )
+        warm = tile("warm", [P, 2], F32)
+        nc.vector.memset(warm[:, 0:1], 0.0)
+        nc.scalar.activation(out=warm[:, 1:2], in_=warm[:, 0:1], func=GELU)
         ws_raw = []
         for a in range(2):
-            raw = tile("ws_raw%d" % a, [P, PACK, R], F32, tag="gate%d" % ORDER[a])
+            raw = tile("ws_raw%d" % a, [P, PACK, R], F32)
             nc.sync.dma_start(out=raw[:], in_=ws[512 * a : 512 * (a + 1), :].rearrange("(p j) r -> p j r", j=PACK))
             ws_raw.append(raw)
         wt_w_raw = tile("wt_w_raw", [P, 2, R], I32, tag="gate%d" % third)
@@ -70,17 +78,15 @@ def tile_list_msg_gelu_gateP_kernel(tc, tab_words, tab_scales, ws, wt_words, wt_
                 out=wt_s_raw[32 * q : 32 * q + 4, :].bitcast(I32).rearrange("q (a r) -> q a r", a=2),
                 in_=wt_scales[:, 4 * q : 4 * q + 4, :].bitcast(I32).rearrange("a q r -> q a r"),
             )
-        wd_raw = tile("wd_raw", [P, PACK, N], F32)
+        wd_raw = tile("wd_raw", [P, PACK, N], F32, tag="act")
         nc.sync.dma_start(out=wd_raw[:], in_=wd.rearrange("(p j) n -> p j n", j=PACK))
-        sm_t = tile("sm_t", [P, PACK], F32)
-        nc.sync.dma_start(out=sm_t[:], in_=sm.rearrange("(p t) -> p t", t=PACK))
         wgo_t = tile("wgo_t", [P, J], F32)
         nc.sync.dma_start(out=wgo_t[:], in_=wgo)
 
         pages = {}
-        for t in ORDER[:3]:
+        for t in ORDER:
             pages[t] = tile("page%d" % t, [P, T], F32)
-            nc.vector.memset(pages[t][:], 0.0)
+            nc.gpsimd.memset(pages[t][:], 0.0)
 
         def round_and_deal(dst, raw):
             nc.scalar.copy(
@@ -90,15 +96,6 @@ def tile_list_msg_gelu_gateP_kernel(tc, tab_words, tab_scales, ws, wt_words, wt_
 
         def list_cols(h):
             return slice(h * HALF // LIST_ROWS, (h + 1) * HALF // LIST_ROWS)
-
-        def gather_scales(h, tag=None):
-            packed = tile("v_s%d" % h, [P, 2, HALF], U8, tag=tag)
-            for u in range(2):
-                nc.vector.tensor_copy(packed[:, u, :], tab_s[:].indirect(lists[u][:, list_cols(h)]))
-            rows = packed[:].rearrange("p u n -> p (u n)").bitcast(I32)
-            for q in range(QUADS):
-                nc.sync.dma_start(out=moved[32 * q : 32 * q + 4, h, :].bitcast(I32), in_=rows[32 * q + 4 : 32 * q + 8, :])
-            return [[packed[:, u, :] for u in range(2)], [moved[:, h, u * HALF : (u + 1) * HALF] for u in range(2)]]
 
         def gather_words(h, tag=None):
             pairs = tile("pairs%d" % h, [P, 2, HALF], U32, tag=tag)
@@ -115,8 +112,14 @@ def tile_list_msg_gelu_gateP_kernel(tc, tab_words, tab_scales, ws, wt_words, wt_
                 )
             return parted
 
-        v_s = [gather_scales(0)]
-        v_w = [part_words(0, gather_words(0))]
+        pairs0 = gather_words(0, "gate%d" % second)
+        packed = tile("packed", [P, 2 * J], U8)
+        for u in range(2):
+            nc.vector.tensor_copy(packed[:, u * J : (u + 1) * J], tab_s[:].indirect(lists[u][:]))
+        for q in range(QUADS):
+            nc.sync.dma_start(out=moved[32 * q : 32 * q + 4, :].bitcast(I32), in_=packed[32 * q + 4 : 32 * q + 8, :].bitcast(I32))
+        v_s = (packed, moved)
+        v_w = [part_words(0, pairs0)]
 
         wt_w = tile("wt_w", [P, 2, R], I32)
         wt_s = tile("wt_s", [P, 2, R], U8)
@@ -138,9 +141,7 @@ def tile_list_msg_gelu_gateP_kernel(tc, tab_words, tab_scales, ws, wt_words, wt_
             in_=ws_bf[:].rearrange("p a r -> p (a r)"),
         )
 
-        pairs1 = gather_words(1, "ws_bf")
-        v_s.append(gather_scales(1, "tab_w"))
-        v_w.append(part_words(1, pairs1))
+        v_w.append(part_words(1, gather_words(1, "ws_bf")))
 
         wd_bf = tile("wd_bf", [P, PACK * N], BF16)
         round_and_deal(wd_bf[:], wd_raw)
@@ -157,6 +158,10 @@ def tile_list_msg_gelu_gateP_kernel(tc, tab_words, tab_scales, ws, wt_words, wt_
         def first_stage(h):
             act = tile("act%d" % h, [P, PACK, HALF], F32, tag="act")
             planes = tile("h_planes%d" % h, [P, PACK, HALF], BF16)
+
+            def smooth(t):
+                nc.scalar.activation(out=planes[:, t, :], in_=act[:, t, :], func=COPY, scale=sm_t[:, t : t + 1])
+
             for t in range(PACK):
                 acc = psum.tile([P, HALF], F32, name="a%d%d" % (h, t), tag="bank%d" % (PACK * h + t))
                 m_cols = slice(t * P, (t + 1) * P)
@@ -168,17 +173,19 @@ def tile_list_msg_gelu_gateP_kernel(tc, tab_words, tab_scales, ws, wt_words, wt_
                         lhsT=w_w[:, a, m_cols].bitcast(FP8X4),
                         lhsT_scale=w_s[:, a, m_cols],
                         rhs=v_w[h][:, u, a, :].bitcast(FP4X4),
-                        rhs_scale=v_s[h][a][u],
+                        rhs_scale=v_s[a][:, u * J + h * HALF : u * J + (h + 1) * HALF],
                         start=(i == 0),
                         stop=(i == len(steps) - 1),
                     )
                 nc.scalar.activation(out=act[:, t, :], in_=acc[:], func=GELU)
-                nc.scalar.activation(out=planes[:, t, :], in_=act[:, t, :], func=COPY, scale=sm_t[:, t : t + 1])
+                if t > 0:
+                    smooth(t - 1)
+            smooth(PACK - 1)
             return planes
 
-        def weave(h, planes):
+        def weave(h, planes, copy):
             woven = tile("h_bf%d" % h, [P, HALF, PACK], BF16)
-            nc.scalar.copy(
+            copy(
                 out=woven[:].rearrange("p (c i) t -> p c t i", i=4),
                 in_=planes[:].rearrange("p t (c i) -> p c t i", i=4),
             )
@@ -233,25 +240,24 @@ def tile_list_msg_gelu_gateP_kernel(tc, tab_words, tab_scales, ws, wt_words, wt_
                 for cols in (slice(0, split), slice(split, T)):
                     nc.scalar.copy(out=out_bf[:, cols, t], in_=pages[t][:, cols])
 
-        woven0 = weave(0, first_stage(0))
+        planes0 = first_stage(0)
         planes1 = first_stage(1)
         gather_gate(first)
         gather_gate(second)
 
-        hidden0 = quantise_hidden(0, woven0, "gate%d" % second)
+        woven0 = weave(0, planes0, nc.vector.tensor_copy)
+        hidden0 = quantise_hidden(0, woven0, None)
         y_first0 = copy_out("y_first0", [second_stage(0, first, hidden0)], "act")
-        woven1 = weave(1, planes1)
-        y_second0 = copy_out("y_second0", [second_stage(0, second, hidden0)])
+        woven1 = weave(1, planes1, nc.scalar.copy)
+        y_second0 = copy_out("y_second0", [second_stage(0, second, hidden0)], "h_planes1")
         gather_gate(third, "h_bf0")
         scatter(first, y_first0, 0)
-        hidden1 = quantise_hidden(1, woven1, "act")
+        hidden1 = quantise_hidden(1, woven1, None)
         scatter(second, y_second0, 0)
         y_first1 = copy_out("y_first1", [second_stage(1, first, hidden1)])
         y_second1 = copy_out("y_second1", [second_stage(1, second, hidden1)])
         y_third = copy_out("y_third", [second_stage(0, third, hidden0), second_stage(1, third, hidden1)])
         y_last = copy_out("y_last", [second_stage(0, last, hidden0), second_stage(1, last, hidden1)])
-        pages[last] = tile("page%d" % last, [P, T], F32, tag="act")
-        nc.gpsimd.memset(pages[last][:], 0.0)
 
         scatter(first, y_first1, 1)
         finish_page(first)

@@ -64,7 +64,7 @@ def tile_list_msg_gelu_gateP_kernel(tc, tab_words, tab_scales, ws, wt_words, wt_
                 in_=tab_scales[:, 4 * q : 4 * q + 4, :].bitcast(I32),
             )
         warm = tile("warm", [P, 2], F32)
-        nc.vector.memset(warm[:, 0:1], 0.0)
+        nc.gpsimd.memset(warm[:, 0:1], 0.0)
         nc.scalar.activation(out=warm[:, 1:2], in_=warm[:, 0:1], func=GELU)
         ws_raw = []
         for a in range(2):
@@ -163,7 +163,7 @@ def tile_list_msg_gelu_gateP_kernel(tc, tab_words, tab_scales, ws, wt_words, wt_
                 nc.scalar.activation(out=planes[:, t, :], in_=act[:, t, :], func=COPY, scale=sm_t[:, t : t + 1])
 
             for t in range(PACK):
-                acc = psum.tile([P, HALF], F32, name="a%d%d" % (h, t), tag="bank%d" % (PACK * h + t))
+                acc = psum.tile([P, HALF], F32, name="a%d%d" % (h, t), tag="bank%d" % t)
                 m_cols = slice(t * P, (t + 1) * P)
                 steps = [(a, u) for a in range(2) for u in (1, 0)]
                 for i, (a, u) in enumerate(steps):
@@ -198,7 +198,8 @@ def tile_list_msg_gelu_gateP_kernel(tc, tab_words, tab_scales, ws, wt_words, wt_
             return h_w, h_s
 
         def second_stage(h, t, hidden):
-            acc = psum.tile([P, HALF], F32, name="y%d%d" % (h, t), tag="bank%d" % (PACK * h + t))
+            bank = PACK + t if h else PACK - 2 + ORDER.index(t) % 2
+            acc = psum.tile([P, HALF], F32, name="y%d%d" % (h, t), tag="bank%d" % bank)
             m_cols = slice(t * P, (t + 1) * P)
             nc.tensor.matmul_mx(
                 out=acc[:],

@@ -47,7 +47,7 @@ def tile_list_msg_gelu_gateP_kernel(tc, tab_words, tab_scales, ws, wt_words, wt_
 
         first, second, third, last = ORDER
         tab_s = tile("tab_s", [P, T], U8, tag="gate%d" % first)
-        wt_s_raw = tile("wt_s_raw", [P, 2 * R], U8, tag="gate%d" % last)
+        wt_s_raw = tile("wt_s_raw", [P, 2 * R], U8)
         moved = tile("moved", [P, 2 * J], U8)
         nc.gpsimd.memset(tab_s[:].bitcast(I32), 0)
         nc.gpsimd.memset(wt_s_raw[:].bitcast(I32), 0)
@@ -66,27 +66,25 @@ def tile_list_msg_gelu_gateP_kernel(tc, tab_words, tab_scales, ws, wt_words, wt_
         warm = tile("warm", [P, 2], F32)
         nc.gpsimd.memset(warm[:, 0:1], 0.0)
         nc.scalar.activation(out=warm[:, 1:2], in_=warm[:, 0:1], func=GELU)
-        ws_raw = []
-        for a in range(2):
-            raw = tile("ws_raw%d" % a, [P, PACK, R], F32)
-            nc.sync.dma_start(out=raw[:], in_=ws[512 * a : 512 * (a + 1), :].rearrange("(p j) r -> p j r", j=PACK))
-            ws_raw.append(raw)
-        wt_w_raw = tile("wt_w_raw", [P, 2, R], I32, tag="gate%d" % third)
+        wt_w_raw = tile("wt_w_raw", [P, 2, R], I32, tag="gate%d" % second)
         nc.sync.dma_start(out=wt_w_raw[:], in_=wt_words.rearrange("a p r i -> p a (r i)").bitcast(I32))
         for q in range(QUADS):
             nc.sync.dma_start(
                 out=wt_s_raw[32 * q : 32 * q + 4, :].bitcast(I32).rearrange("q (a r) -> q a r", a=2),
                 in_=wt_scales[:, 4 * q : 4 * q + 4, :].bitcast(I32).rearrange("a q r -> q a r"),
             )
-        wd_raw = tile("wd_raw", [P, PACK, N], F32, tag="act")
-        nc.sync.dma_start(out=wd_raw[:], in_=wd.rearrange("(p j) n -> p j n", j=PACK))
-        wgo_t = tile("wgo_t", [P, J], F32)
-        nc.sync.dma_start(out=wgo_t[:], in_=wgo)
+
+        def load_rows(name, rows, tag=None):
+            raw = tile(name, [P, PACK, rows.shape[1]], F32, tag=tag)
+            nc.sync.dma_start(out=raw[:], in_=rows.rearrange("(p j) r -> p j r", j=PACK))
+            return raw
+
+        ws_raw = [load_rows("ws_raw0", ws[:512, :])]
 
         pages = {}
-        for t in ORDER:
+        for t in (first, second):
             pages[t] = tile("page%d" % t, [P, T], F32)
-            nc.gpsimd.memset(pages[t][:], 0.0)
+            nc.vector.memset(pages[t][:], 0.0)
 
         def round_and_deal(dst, raw):
             nc.scalar.copy(
@@ -97,29 +95,34 @@ def tile_list_msg_gelu_gateP_kernel(tc, tab_words, tab_scales, ws, wt_words, wt_
         def list_cols(h):
             return slice(h * HALF // LIST_ROWS, (h + 1) * HALF // LIST_ROWS)
 
-        def gather_words(h, tag=None):
-            pairs = tile("pairs%d" % h, [P, 2, HALF], U32, tag=tag)
-            for u in range(2):
-                nc.vector.tensor_copy(pairs[:, u, :], tab_w[:].bitcast(U32).indirect(lists[u][:, list_cols(h)]))
-            return pairs
+        def gather_words(u, h, pairs):
+            nc.vector.tensor_copy(pairs, tab_w[:].bitcast(U32).indirect(lists[u][:, list_cols(h)]))
 
-        def part_words(h, pairs):
-            parted = tile("v_w%d" % h, [P, 2, 2, 2 * HALF], U8)
-            for u in range(2):
-                nc.vector.tensor_copy(
-                    parted[:, u].bitcast(U16),
-                    pairs[:, u, :].bitcast(U16).rearrange("p (n d) -> p d n", d=2),
-                )
+        def part_words(u, h, pairs):
+            parted = tile("v_w%d%d" % (u, h), [P, 2, 2 * HALF], U8)
+            nc.vector.tensor_copy(parted[:].bitcast(U16), pairs.bitcast(U16).rearrange("p (n d) -> p d n", d=2))
             return parted
 
-        pairs0 = gather_words(0, "gate%d" % second)
-        packed = tile("packed", [P, 2 * J], U8)
-        for u in range(2):
-            nc.vector.tensor_copy(packed[:, u * J : (u + 1) * J], tab_s[:].indirect(lists[u][:]))
-        for q in range(QUADS):
-            nc.sync.dma_start(out=moved[32 * q : 32 * q + 4, :].bitcast(I32), in_=packed[32 * q + 4 : 32 * q + 8, :].bitcast(I32))
-        v_s = (packed, moved)
-        v_w = [part_words(0, pairs0)]
+        def gather_scales(u, tag=None):
+            packed = tile("packed%d" % u, [P, J], U8, tag=tag)
+            nc.vector.tensor_copy(packed[:], tab_s[:].indirect(lists[u][:]))
+            for q in range(QUADS):
+                nc.sync.dma_start(
+                    out=moved[32 * q : 32 * q + 4, u * J : (u + 1) * J].bitcast(I32),
+                    in_=packed[32 * q + 4 : 32 * q + 8, :].bitcast(I32),
+                )
+            return packed[:], moved[:, u * J : (u + 1) * J]
+
+        v_w, v_s = {}, {}
+        dst_pairs = tile("dst_pairs", [P, HALF], U32)
+        gather_words(1, 0, dst_pairs[:])
+        v_s[1] = gather_scales(1)
+        v_w[1, 0] = part_words(1, 0, dst_pairs[:])
+
+        ws_raw.append(load_rows("ws_raw1", ws[512:, :], "gate%d" % third))
+        wd_raw = load_rows("wd_raw", wd, "act")
+        wgo_t = tile("wgo_t", [P, J], F32)
+        nc.sync.dma_start(out=wgo_t[:], in_=wgo)
 
         wt_w = tile("wt_w", [P, 2, R], I32)
         wt_s = tile("wt_s", [P, 2, R], U8)
@@ -130,9 +133,13 @@ def tile_list_msg_gelu_gateP_kernel(tc, tab_words, tab_scales, ws, wt_words, wt_
             wt_s[:].rearrange("p a (t m) -> p a m t", t=PACK), wt_s_raw[:].rearrange("p (a m t) -> p a m t", a=2, t=PACK)
         )
 
+        src_pairs = tile("src_pairs", [P, HALF], U32, tag="gate%d" % second)
+        v_s[0] = gather_scales(0, "wt_s_raw")
+        gather_words(0, 0, src_pairs[:])
+
         ws_w = tile("ws_w", [P, 2, R], U32)
         ws_s = tile("ws_s", [P, 2, R], U8)
-        ws_bf = tile("ws_bf", [P, 2, PACK * R], BF16)
+        ws_bf = tile("ws_bf", [P, 2, PACK * R], BF16, tag="gate%d" % last)
         for a in range(2):
             round_and_deal(ws_bf[:, a, :], ws_raw[a])
         nc.vector.quantize_mx(
@@ -141,7 +148,13 @@ def tile_list_msg_gelu_gateP_kernel(tc, tab_words, tab_scales, ws, wt_words, wt_
             in_=ws_bf[:].rearrange("p a r -> p (a r)"),
         )
 
-        v_w.append(part_words(1, gather_words(1, "ws_bf")))
+        v_w[0, 0] = part_words(0, 0, src_pairs[:])
+
+        pairs1 = tile("pairs1", [P, 2, HALF], U32, tag="gate%d" % last)
+        for u in (1, 0):
+            gather_words(u, 1, pairs1[:, u, :])
+        for u in (1, 0):
+            v_w[u, 1] = part_words(u, 1, pairs1[:, u, :])
 
         wd_bf = tile("wd_bf", [P, PACK * N], BF16)
         round_and_deal(wd_bf[:], wd_raw)
@@ -162,22 +175,26 @@ def tile_list_msg_gelu_gateP_kernel(tc, tab_words, tab_scales, ws, wt_words, wt_
             def smooth(t):
                 nc.scalar.activation(out=planes[:, t, :], in_=act[:, t, :], func=COPY, scale=sm_t[:, t : t + 1])
 
-            for t in range(PACK):
-                acc = psum.tile([P, HALF], F32, name="a%d%d" % (h, t), tag="bank%d" % t)
+            accs = [psum.tile([P, HALF], F32, name="a%d%d" % (h, t), tag="bank%d" % t) for t in range(PACK)]
+
+            def one_pass(t, u, a):
+                w_w, w_s = ((ws_w, ws_s), (wt_w, wt_s))[u]
                 m_cols = slice(t * P, (t + 1) * P)
-                steps = [(a, u) for a in range(2) for u in (1, 0)]
-                for i, (a, u) in enumerate(steps):
-                    w_w, w_s = ((ws_w, ws_s), (wt_w, wt_s))[u]
-                    nc.tensor.matmul_mx(
-                        out=acc[:],
-                        lhsT=w_w[:, a, m_cols].bitcast(FP8X4),
-                        lhsT_scale=w_s[:, a, m_cols],
-                        rhs=v_w[h][:, u, a, :].bitcast(FP4X4),
-                        rhs_scale=v_s[a][:, u * J + h * HALF : u * J + (h + 1) * HALF],
-                        start=(i == 0),
-                        stop=(i == len(steps) - 1),
-                    )
-                nc.scalar.activation(out=act[:, t, :], in_=acc[:], func=GELU)
+                nc.tensor.matmul_mx(
+                    out=accs[t][:],
+                    lhsT=w_w[:, a, m_cols].bitcast(FP8X4),
+                    lhsT_scale=w_s[:, a, m_cols],
+                    rhs=v_w[u, h][:, a, :].bitcast(FP4X4),
+                    rhs_scale=v_s[u][a][:, h * HALF : (h + 1) * HALF],
+                    start=(u, a) == (1, 0),
+                    stop=(u, a) == (0, 1),
+                )
+
+            for t in range(PACK):
+                for u in (1, 0):
+                    for a in range(2):
+                        one_pass(t, u, a)
+                nc.scalar.activation(out=act[:, t, :], in_=accs[t][:], func=GELU)
                 if t > 0:
                     smooth(t - 1)
             smooth(PACK - 1)
@@ -259,6 +276,9 @@ def tile_list_msg_gelu_gateP_kernel(tc, tab_words, tab_scales, ws, wt_words, wt_
         y_second1 = copy_out("y_second1", [second_stage(1, second, hidden1)])
         y_third = copy_out("y_third", [second_stage(0, third, hidden0), second_stage(1, third, hidden1)])
         y_last = copy_out("y_last", [second_stage(0, last, hidden0), second_stage(1, last, hidden1)])
+        for t, tag in ((third, "h_w1"), (last, "h_s1")):
+            pages[t] = tile("page%d" % t, [P, T], F32, tag=tag)
+            nc.gpsimd.memset(pages[t][:], 0.0)
 
         scatter(first, y_first1, 1)
         finish_page(first)

@@ -23,9 +23,9 @@ QUADS = 4
 HALF = 512
 HALVES = J // HALF
 LIST_ROWS = 16
-OUT_CHUNKS = (256, 512, 512, 512, 256)
-VECTOR_CHUNKS = 3
-TABLE_PIECE = 512
+OUT_CHUNKS = (512, 512, 512, 512)
+VECTOR_CHUNKS = 2
+RUN = 8
 ORDER = (2, 0, 1, 3)
 
 
@@ -46,27 +46,26 @@ def tile_list_msg_gelu_gateP_kernel(tc, tab_words, tab_scales, ws, wt_words, wt_
         nc.sync.dma_start(dst_list[:], offs2)
 
         first, second, third, last = ORDER
-        tab_s = tile("tab_s", [P, T], U8, tag="gate%d" % first)
-        wt_s_raw = tile("wt_s_raw", [P, 2 * R], U8)
-        moved = tile("moved", [P, 2 * J], U8)
-        nc.gpsimd.memset(tab_s[:].bitcast(I32), 0)
-        nc.gpsimd.memset(wt_s_raw[:].bitcast(I32), 0)
-        nc.gpsimd.memset(moved[:].bitcast(I32), 0)
+        tab_s = tile("tab_s", [P, T], U8, tag="act")
+        nc.sync.dma_start(
+            out=tab_s[96:128, :].bitcast(I32),
+            in_=tab_scales.bitcast(I32).rearrange("a b t -> b a t"),
+        )
+        nc.vector.memset(tab_s[0:96, :].bitcast(I32), 0)
         tab_w = tile("tab_w", [P, T], I32)
-        sm_t = tile("sm_t", [P, PACK], F32)
-        nc.sync.dma_start(out=sm_t[:], in_=sm.rearrange("(p t) -> p t", t=PACK))
-        tab_rows = tab_words[0].rearrange("p t i -> p (t i)").bitcast(I32)
-        for c in range(0, T, TABLE_PIECE):
-            nc.sync.dma_start(out=tab_w[:, c : c + TABLE_PIECE], in_=tab_rows[:, c : c + TABLE_PIECE])
-        for q in range(QUADS):
-            nc.sync.dma_start(
-                out=tab_s[32 * q : 32 * q + 8, :].bitcast(I32),
-                in_=tab_scales[:, 4 * q : 4 * q + 4, :].bitcast(I32),
-            )
+        nc.sync.dma_start(out=tab_w[:], in_=tab_words[0].rearrange("p t i -> p (t i)").bitcast(I32))
         warm = tile("warm", [P, 2], F32)
         nc.gpsimd.memset(warm[:, 0:1], 0.0)
         nc.scalar.activation(out=warm[:, 1:2], in_=warm[:, 0:1], func=GELU)
-        wt_w_raw = tile("wt_w_raw", [P, 2, R], I32, tag="gate%d" % second)
+
+        ws_raw = []
+        for a in range(2):
+            raw = tile("ws_raw%d" % a, [P, PACK, R], F32)
+            nc.sync.dma_start(out=raw[:], in_=ws[512 * a : 512 * (a + 1), :].rearrange("(p j) r -> p j r", j=PACK))
+            ws_raw.append(raw)
+        wt_w_raw = tile("wt_w_raw", [P, 2, R], I32)
+        wt_s_raw = tile("wt_s_raw", [P, 2 * R], U8)
+        nc.gpsimd.memset(wt_s_raw[:].bitcast(I32), 0)
         nc.sync.dma_start(out=wt_w_raw[:], in_=wt_words.rearrange("a p r i -> p a (r i)").bitcast(I32))
         for q in range(QUADS):
             nc.sync.dma_start(
@@ -74,23 +73,16 @@ def tile_list_msg_gelu_gateP_kernel(tc, tab_words, tab_scales, ws, wt_words, wt_
                 in_=wt_scales[:, 4 * q : 4 * q + 4, :].bitcast(I32).rearrange("a q r -> q a r"),
             )
 
-        def load_rows(name, rows, tag=None):
-            raw = tile(name, [P, PACK, rows.shape[1]], F32, tag=tag)
-            nc.sync.dma_start(out=raw[:], in_=rows.rearrange("(p j) r -> p j r", j=PACK))
-            return raw
-
-        ws_raw = [load_rows("ws_raw0", ws[:512, :])]
-
+        moved = tile("moved", [P, 2, 2 * J], U8)
+        nc.gpsimd.memset(moved[:].rearrange("p a c -> p (a c)").bitcast(I32), 0)
         pages = {}
-        for t in (first, second):
+        for t, engine in ((first, nc.vector), (second, nc.gpsimd)):
             pages[t] = tile("page%d" % t, [P, T], F32)
-            nc.vector.memset(pages[t][:], 0.0)
-
-        def round_and_deal(dst, raw):
-            nc.scalar.copy(
-                out=dst.rearrange("p (t m j) -> p m j t", t=PACK, j=PACK),
-                in_=raw[:].rearrange("p j (m t) -> p m j t", t=PACK),
-            )
+            engine.memset(pages[t][:], 0.0)
+        sm_t = tile("sm_t", [P, PACK, RUN], F32)
+        sm_rows = sm.rearrange("(q t i o) -> t q i o", t=PACK, i=RUN, o=1)
+        for t in range(PACK):
+            nc.gpsimd.dma_start(out=sm_t[:, t, 0:1], in_=sm_rows[t])
 
         def list_cols(h):
             return slice(h * HALF // LIST_ROWS, (h + 1) * HALF // LIST_ROWS)
@@ -103,69 +95,74 @@ def tile_list_msg_gelu_gateP_kernel(tc, tab_words, tab_scales, ws, wt_words, wt_
             nc.vector.tensor_copy(parted[:].bitcast(U16), pairs.bitcast(U16).rearrange("p (n d) -> p d n", d=2))
             return parted
 
-        def gather_scales(u, tag=None):
-            packed = tile("packed%d" % u, [P, J], U8, tag=tag)
-            nc.vector.tensor_copy(packed[:], tab_s[:].indirect(lists[u][:]))
-            for q in range(QUADS):
-                nc.sync.dma_start(
-                    out=moved[32 * q : 32 * q + 4, u * J : (u + 1) * J].bitcast(I32),
-                    in_=packed[32 * q + 4 : 32 * q + 8, :].bitcast(I32),
-                )
-            return packed[:], moved[:, u * J : (u + 1) * J]
+        packed = tile("packed", [P, 2 * J], U8)
+        for u in (1, 0):
+            nc.vector.tensor_copy(packed[:, u * J : (u + 1) * J], tab_s[:].indirect(lists[u][:]))
+        for q in range(QUADS):
+            nc.sync.dma_start(
+                out=moved[32 * q : 32 * q + 4, :, :].bitcast(I32),
+                in_=packed[96 + 8 * q : 104 + 8 * q, :].bitcast(I32),
+            )
+        v_s = [[moved[:, a, u * J : (u + 1) * J] for a in range(2)] for u in range(2)]
 
-        v_w, v_s = {}, {}
-        dst_pairs = tile("dst_pairs", [P, HALF], U32)
-        gather_words(1, 0, dst_pairs[:])
-        v_s[1] = gather_scales(1)
-        v_w[1, 0] = part_words(1, 0, dst_pairs[:])
+        wd_raw = tile("wd_raw", [P, PACK, N], F32, tag="act")
+        wd_rows = wd.rearrange("(q j i) n -> j q i n", j=PACK, i=RUN)
+        for j in range(PACK):
+            nc.sync.dma_start(out=wd_raw[:, j, :], in_=wd_rows[j])
 
-        ws_raw.append(load_rows("ws_raw1", ws[512:, :], "gate%d" % third))
-        wd_raw = load_rows("wd_raw", wd, "act")
-        wgo_t = tile("wgo_t", [P, J], F32)
-        nc.sync.dma_start(out=wgo_t[:], in_=wgo)
+        v_w = {}
+        pairs0 = tile("pairs0", [P, 2, HALF], U32)
+        for u in (1, 0):
+            gather_words(u, 0, pairs0[:, u, :])
+        for u in (1, 0):
+            v_w[u, 0] = part_words(u, 0, pairs0[:, u, :])
 
         wt_w = tile("wt_w", [P, 2, R], I32)
         wt_s = tile("wt_s", [P, 2, R], U8)
         nc.vector.tensor_copy(
-            wt_w[:].rearrange("p a (t m) -> p a m t", t=PACK), wt_w_raw[:].rearrange("p a (m t) -> p a m t", t=PACK)
+            wt_w[:].rearrange("p a (t q i) -> p a t q i", t=PACK, i=RUN),
+            wt_w_raw[:].rearrange("p a (q t i) -> p a t q i", t=PACK, i=RUN),
         )
         nc.vector.tensor_copy(
-            wt_s[:].rearrange("p a (t m) -> p a m t", t=PACK), wt_s_raw[:].rearrange("p (a m t) -> p a m t", a=2, t=PACK)
+            wt_s[:].bitcast(I32).rearrange("p a (t q i) -> p a t q i", t=PACK, i=RUN // 4),
+            wt_s_raw[:].bitcast(I32).rearrange("p (a q t i) -> p a t q i", a=2, t=PACK, i=RUN // 4),
         )
 
-        src_pairs = tile("src_pairs", [P, HALF], U32, tag="gate%d" % second)
-        v_s[0] = gather_scales(0, "wt_s_raw")
-        gather_words(0, 0, src_pairs[:])
-
         ws_w = tile("ws_w", [P, 2, R], U32)
-        ws_s = tile("ws_s", [P, 2, R], U8)
-        ws_bf = tile("ws_bf", [P, 2, PACK * R], BF16, tag="gate%d" % last)
+        ws_s = tile("ws_s", [P, 2, R], U8, tag="wt_s_raw")
+        ws_bf = tile("ws_bf", [P, 2, PACK * R], BF16)
         for a in range(2):
-            round_and_deal(ws_bf[:, a, :], ws_raw[a])
+            nc.scalar.copy(
+                out=ws_bf[:, a, :].rearrange("p (t q i j) -> p q t j i", t=PACK, i=RUN, j=PACK),
+                in_=ws_raw[a][:].rearrange("p j (q t i) -> p q t j i", t=PACK, i=RUN),
+            )
         nc.vector.quantize_mx(
             out=ws_w[:].rearrange("p a r -> p (a r)").bitcast(FP8X4),
             scales=ws_s[:].rearrange("p a r -> p (a r)"),
             in_=ws_bf[:].rearrange("p a r -> p (a r)"),
         )
 
-        v_w[0, 0] = part_words(0, 0, src_pairs[:])
-
-        pairs1 = tile("pairs1", [P, 2, HALF], U32, tag="gate%d" % last)
+        pairs1 = tile("pairs1", [P, 2, HALF], U32, tag="ws_bf")
         for u in (1, 0):
             gather_words(u, 1, pairs1[:, u, :])
         for u in (1, 0):
             v_w[u, 1] = part_words(u, 1, pairs1[:, u, :])
 
         wd_bf = tile("wd_bf", [P, PACK * N], BF16)
-        round_and_deal(wd_bf[:], wd_raw)
+        nc.scalar.copy(
+            out=wd_bf[:].rearrange("p (t m j) -> p m j t", t=PACK, j=PACK),
+            in_=wd_raw[:].rearrange("p j (m t) -> p m j t", t=PACK),
+        )
         wd_w = tile("wd_w", [P, N], U32)
         wd_s = tile("wd_s", [P, N], U8)
         nc.vector.quantize_mx(out=wd_w[:].bitcast(FP8X4), scales=wd_s[:], in_=wd_bf[:])
 
+        wgo_t = tile("wgo_t", [P, J], F32, tag="pairs0")
+        nc.sync.dma_start(out=wgo_t[:], in_=wgo)
         gates = {}
         g_rows = gT.rearrange("(p t) c -> t p c", t=PACK)
-        for t in ORDER:
-            gates[t] = tile("gate%d" % t, [P, T], F32)
+        for t, tag in zip(ORDER, ("wt_w_raw", "ws_raw1", "ws_bf", "wd_bf")):
+            gates[t] = tile("gate%d" % t, [P, T], F32, tag=tag)
             nc.sync.dma_start(out=gates[t][:], in_=g_rows[t])
 
         def first_stage(h):
@@ -173,7 +170,7 @@ def tile_list_msg_gelu_gateP_kernel(tc, tab_words, tab_scales, ws, wt_words, wt_
             planes = tile("h_planes%d" % h, [P, PACK, HALF], BF16)
 
             def smooth(t):
-                nc.scalar.activation(out=planes[:, t, :], in_=act[:, t, :], func=COPY, scale=sm_t[:, t : t + 1])
+                nc.scalar.activation(out=planes[:, t, :], in_=act[:, t, :], func=COPY, scale=sm_t[:, t, 0:1])
 
             accs = [psum.tile([P, HALF], F32, name="a%d%d" % (h, t), tag="bank%d" % t) for t in range(PACK)]
 
@@ -215,7 +212,7 @@ def tile_list_msg_gelu_gateP_kernel(tc, tab_words, tab_scales, ws, wt_words, wt_
             return h_w, h_s
 
         def second_stage(h, t, hidden):
-            bank = PACK + t if h else PACK - 2 + ORDER.index(t) % 2
+            bank = PACK + t
             acc = psum.tile([P, HALF], F32, name="y%d%d" % (h, t), tag="bank%d" % bank)
             m_cols = slice(t * P, (t + 1) * P)
             nc.tensor.matmul_mx(
@@ -235,6 +232,12 @@ def tile_list_msg_gelu_gateP_kernel(tc, tab_words, tab_scales, ws, wt_words, wt_
             factors[t] = tile("factor%d" % t, [P, J], F32, tag=tag)
             nc.vector.tensor_tensor(factors[t][:], gates[t][:].indirect(src_list[:]), wgo_t[:], MULT)
 
+        def gather_gate_half(t, h, tag):
+            factors[t, h] = tile("factor%d%d" % (t, h), [P, HALF], F32, tag=tag)
+            nc.vector.tensor_tensor(
+                factors[t, h][:], gates[t][:].indirect(src_list[:, list_cols(h)]), wgo_t[:, h * HALF : (h + 1) * HALF], MULT
+            )
+
         out_rows = out_0.rearrange("(p t) c -> t p c", t=PACK)
         out_bf = tile("out_bf", [P, T, PACK], BF16)
         starts = [sum(OUT_CHUNKS[:i]) for i in range(len(OUT_CHUNKS) + 1)]
@@ -249,7 +252,10 @@ def tile_list_msg_gelu_gateP_kernel(tc, tab_words, tab_scales, ws, wt_words, wt_
 
         def scatter(t, y, h=None):
             offsets = dst_list[:] if h is None else dst_list[:, list_cols(h)]
-            factor = factors[t][:] if h is None else factors[t][:, h * HALF : (h + 1) * HALF]
+            if (t, h) in factors:
+                factor = factors[t, h][:]
+            else:
+                factor = factors[t][:] if h is None else factors[t][:, h * HALF : (h + 1) * HALF]
             nc.vector.tensor_tensor(pages[t][:].indirect(offsets), y[:], factor, MULT)
 
         def finish_page(t):
@@ -259,23 +265,26 @@ def tile_list_msg_gelu_gateP_kernel(tc, tab_words, tab_scales, ws, wt_words, wt_
                     nc.scalar.copy(out=out_bf[:, cols, t], in_=pages[t][:, cols])
 
         planes0 = first_stage(0)
-        planes1 = first_stage(1)
+        woven0 = weave(0, planes0, nc.scalar.copy)
         gather_gate(first)
         gather_gate(second)
-
-        woven0 = weave(0, planes0, nc.vector.tensor_copy)
         hidden0 = quantise_hidden(0, woven0, None)
-        y_first0 = copy_out("y_first0", [second_stage(0, first, hidden0)], "act")
-        woven1 = weave(1, planes1, nc.scalar.copy)
-        y_second0 = copy_out("y_second0", [second_stage(0, second, hidden0)], "h_planes1")
-        gather_gate(third, "h_bf0")
+        gather_gate_half(third, 0, "h_bf0")
+        y_first0 = copy_out("y_first0", [second_stage(0, first, hidden0)])
+        y_second0 = copy_out("y_second0", [second_stage(0, second, hidden0)])
         scatter(first, y_first0, 0)
-        hidden1 = quantise_hidden(1, woven1, None)
         scatter(second, y_second0, 0)
+        planes1 = first_stage(1)
+        woven1 = weave(1, planes1, nc.scalar.copy)
+        hidden1 = quantise_hidden(1, woven1, None)
+        gather_gate_half(third, 1, "h_bf1")
         y_first1 = copy_out("y_first1", [second_stage(1, first, hidden1)])
         y_second1 = copy_out("y_second1", [second_stage(1, second, hidden1)])
-        y_third = copy_out("y_third", [second_stage(0, third, hidden0), second_stage(1, third, hidden1)])
-        y_last = copy_out("y_last", [second_stage(0, last, hidden0), second_stage(1, last, hidden1)])
+        y_third0 = copy_out("y_third0", [second_stage(0, third, hidden0)], "h_planes1")
+        y_third1 = copy_out("y_third1", [second_stage(1, third, hidden1)])
+        y_last = tile("y_last", [P, J], F32, tag="act")
+        for h, hidden in enumerate((hidden0, hidden1)):
+            nc.scalar.copy(out=y_last[:, h * HALF : (h + 1) * HALF], in_=second_stage(h, last, hidden)[:])
         for t, tag in ((third, "h_w1"), (last, "h_s1")):
             pages[t] = tile("page%d" % t, [P, T], F32, tag=tag)
             nc.gpsimd.memset(pages[t][:], 0.0)
@@ -284,7 +293,8 @@ def tile_list_msg_gelu_gateP_kernel(tc, tab_words, tab_scales, ws, wt_words, wt_
         finish_page(first)
         scatter(second, y_second1, 1)
         finish_page(second)
-        scatter(third, y_third)
+        scatter(third, y_third0, 0)
+        scatter(third, y_third1, 1)
         finish_page(third)
         gather_gate(last, "page%d" % first)
         scatter(last, y_last)

@@ -25,7 +25,6 @@ HALVES = J // HALF
 LIST_ROWS = 16
 OUT_CHUNKS = (512, 512, 512, 512)
 VECTOR_CHUNKS = 2
-RUN = 8
 ORDER = (2, 0, 1, 3)
 
 
@@ -65,8 +64,10 @@ def tile_list_msg_gelu_gateP_kernel(tc, tab_words, tab_scales, ws, wt_words, wt_
             ws_raw.append(raw)
         wt_w_raw = tile("wt_w_raw", [P, 2, R], I32)
         wt_s_raw = tile("wt_s_raw", [P, 2 * R], U8)
-        nc.gpsimd.memset(wt_s_raw[:].bitcast(I32), 0)
+        nc.vector.memset(wt_s_raw[:].bitcast(I32), 0)
         nc.sync.dma_start(out=wt_w_raw[:], in_=wt_words.rearrange("a p r i -> p a (r i)").bitcast(I32))
+        sm_t = tile("sm_t", [P, PACK], F32)
+        nc.sync.dma_start(out=sm_t[:], in_=sm.rearrange("(p t) -> p t", t=PACK))
         for q in range(QUADS):
             nc.sync.dma_start(
                 out=wt_s_raw[32 * q : 32 * q + 4, :].bitcast(I32).rearrange("q (a r) -> q a r", a=2),
@@ -74,15 +75,20 @@ def tile_list_msg_gelu_gateP_kernel(tc, tab_words, tab_scales, ws, wt_words, wt_
             )
 
         moved = tile("moved", [P, 2, 2 * J], U8)
-        nc.gpsimd.memset(moved[:].rearrange("p a c -> p (a c)").bitcast(I32), 0)
+        nc.vector.memset(moved[:].rearrange("p a c -> p (a c)").bitcast(I32), 0)
         pages = {}
-        for t, engine in ((first, nc.vector), (second, nc.gpsimd)):
-            pages[t] = tile("page%d" % t, [P, T], F32)
-            engine.memset(pages[t][:], 0.0)
-        sm_t = tile("sm_t", [P, PACK, RUN], F32)
-        sm_rows = sm.rearrange("(q t i o) -> t q i o", t=PACK, i=RUN, o=1)
-        for t in range(PACK):
-            nc.gpsimd.dma_start(out=sm_t[:, t, 0:1], in_=sm_rows[t])
+
+        def clear_page(t, tag=None):
+            pages[t] = tile("page%d" % t, [P, T], F32, tag=tag)
+            nc.vector.memset(pages[t][:], 0.0)
+
+        clear_page(first)
+
+        def round_and_deal(dst, raw):
+            nc.scalar.copy(
+                out=dst.rearrange("p (t m j) -> p m j t", t=PACK, j=PACK),
+                in_=raw[:].rearrange("p j (m t) -> p m j t", t=PACK),
+            )
 
         def list_cols(h):
             return slice(h * HALF // LIST_ROWS, (h + 1) * HALF // LIST_ROWS)
@@ -106,9 +112,7 @@ def tile_list_msg_gelu_gateP_kernel(tc, tab_words, tab_scales, ws, wt_words, wt_
         v_s = [[moved[:, a, u * J : (u + 1) * J] for a in range(2)] for u in range(2)]
 
         wd_raw = tile("wd_raw", [P, PACK, N], F32, tag="act")
-        wd_rows = wd.rearrange("(q j i) n -> j q i n", j=PACK, i=RUN)
-        for j in range(PACK):
-            nc.sync.dma_start(out=wd_raw[:, j, :], in_=wd_rows[j])
+        nc.sync.dma_start(out=wd_raw[:], in_=wd.rearrange("(p j) n -> p j n", j=PACK))
 
         v_w = {}
         pairs0 = tile("pairs0", [P, 2, HALF], U32)
@@ -120,22 +124,17 @@ def tile_list_msg_gelu_gateP_kernel(tc, tab_words, tab_scales, ws, wt_words, wt_
         wt_w = tile("wt_w", [P, 2, R], I32)
         wt_s = tile("wt_s", [P, 2, R], U8)
         nc.vector.tensor_copy(
-            wt_w[:].rearrange("p a (t q i) -> p a t q i", t=PACK, i=RUN),
-            wt_w_raw[:].rearrange("p a (q t i) -> p a t q i", t=PACK, i=RUN),
+            wt_w[:].rearrange("p a (t m) -> p a m t", t=PACK), wt_w_raw[:].rearrange("p a (m t) -> p a m t", t=PACK)
         )
         nc.vector.tensor_copy(
-            wt_s[:].bitcast(I32).rearrange("p a (t q i) -> p a t q i", t=PACK, i=RUN // 4),
-            wt_s_raw[:].bitcast(I32).rearrange("p (a q t i) -> p a t q i", a=2, t=PACK, i=RUN // 4),
+            wt_s[:].rearrange("p a (t m) -> p a m t", t=PACK), wt_s_raw[:].rearrange("p (a m t) -> p a m t", a=2, t=PACK)
         )
 
         ws_w = tile("ws_w", [P, 2, R], U32)
         ws_s = tile("ws_s", [P, 2, R], U8, tag="wt_s_raw")
         ws_bf = tile("ws_bf", [P, 2, PACK * R], BF16)
         for a in range(2):
-            nc.scalar.copy(
-                out=ws_bf[:, a, :].rearrange("p (t q i j) -> p q t j i", t=PACK, i=RUN, j=PACK),
-                in_=ws_raw[a][:].rearrange("p j (q t i) -> p q t j i", t=PACK, i=RUN),
-            )
+            round_and_deal(ws_bf[:, a, :], ws_raw[a])
         nc.vector.quantize_mx(
             out=ws_w[:].rearrange("p a r -> p (a r)").bitcast(FP8X4),
             scales=ws_s[:].rearrange("p a r -> p (a r)"),
@@ -149,10 +148,7 @@ def tile_list_msg_gelu_gateP_kernel(tc, tab_words, tab_scales, ws, wt_words, wt_
             v_w[u, 1] = part_words(u, 1, pairs1[:, u, :])
 
         wd_bf = tile("wd_bf", [P, PACK * N], BF16)
-        nc.scalar.copy(
-            out=wd_bf[:].rearrange("p (t m j) -> p m j t", t=PACK, j=PACK),
-            in_=wd_raw[:].rearrange("p j (m t) -> p m j t", t=PACK),
-        )
+        round_and_deal(wd_bf[:], wd_raw)
         wd_w = tile("wd_w", [P, N], U32)
         wd_s = tile("wd_s", [P, N], U8)
         nc.vector.quantize_mx(out=wd_w[:].bitcast(FP8X4), scales=wd_s[:], in_=wd_bf[:])
@@ -170,7 +166,7 @@ def tile_list_msg_gelu_gateP_kernel(tc, tab_words, tab_scales, ws, wt_words, wt_
             planes = tile("h_planes%d" % h, [P, PACK, HALF], BF16)
 
             def smooth(t):
-                nc.scalar.activation(out=planes[:, t, :], in_=act[:, t, :], func=COPY, scale=sm_t[:, t, 0:1])
+                nc.scalar.activation(out=planes[:, t, :], in_=act[:, t, :], func=COPY, scale=sm_t[:, t : t + 1])
 
             accs = [psum.tile([P, HALF], F32, name="a%d%d" % (h, t), tag="bank%d" % t) for t in range(PACK)]
 
@@ -232,12 +228,6 @@ def tile_list_msg_gelu_gateP_kernel(tc, tab_words, tab_scales, ws, wt_words, wt_
             factors[t] = tile("factor%d" % t, [P, J], F32, tag=tag)
             nc.vector.tensor_tensor(factors[t][:], gates[t][:].indirect(src_list[:]), wgo_t[:], MULT)
 
-        def gather_gate_half(t, h, tag):
-            factors[t, h] = tile("factor%d%d" % (t, h), [P, HALF], F32, tag=tag)
-            nc.vector.tensor_tensor(
-                factors[t, h][:], gates[t][:].indirect(src_list[:, list_cols(h)]), wgo_t[:, h * HALF : (h + 1) * HALF], MULT
-            )
-
         out_rows = out_0.rearrange("(p t) c -> t p c", t=PACK)
         out_bf = tile("out_bf", [P, T, PACK], BF16)
         starts = [sum(OUT_CHUNKS[:i]) for i in range(len(OUT_CHUNKS) + 1)]
@@ -252,10 +242,7 @@ def tile_list_msg_gelu_gateP_kernel(tc, tab_words, tab_scales, ws, wt_words, wt_
 
         def scatter(t, y, h=None):
             offsets = dst_list[:] if h is None else dst_list[:, list_cols(h)]
-            if (t, h) in factors:
-                factor = factors[t, h][:]
-            else:
-                factor = factors[t][:] if h is None else factors[t][:, h * HALF : (h + 1) * HALF]
+            factor = factors[t][:] if h is None else factors[t][:, h * HALF : (h + 1) * HALF]
             nc.vector.tensor_tensor(pages[t][:].indirect(offsets), y[:], factor, MULT)
 
         def finish_page(t):
@@ -266,10 +253,10 @@ def tile_list_msg_gelu_gateP_kernel(tc, tab_words, tab_scales, ws, wt_words, wt_
 
         planes0 = first_stage(0)
         woven0 = weave(0, planes0, nc.scalar.copy)
-        gather_gate(first)
-        gather_gate(second)
-        hidden0 = quantise_hidden(0, woven0, None)
-        gather_gate_half(third, 0, "h_bf0")
+        for t in (first, second, third):
+            gather_gate(t)
+        hidden0 = quantise_hidden(0, woven0, "ws_bf")
+        clear_page(second, "h_bf0")
         y_first0 = copy_out("y_first0", [second_stage(0, first, hidden0)])
         y_second0 = copy_out("y_second0", [second_stage(0, second, hidden0)])
         scatter(first, y_first0, 0)
@@ -277,27 +264,24 @@ def tile_list_msg_gelu_gateP_kernel(tc, tab_words, tab_scales, ws, wt_words, wt_
         planes1 = first_stage(1)
         woven1 = weave(1, planes1, nc.scalar.copy)
         hidden1 = quantise_hidden(1, woven1, None)
-        gather_gate_half(third, 1, "h_bf1")
+        clear_page(third, "h_bf1")
         y_first1 = copy_out("y_first1", [second_stage(1, first, hidden1)])
         y_second1 = copy_out("y_second1", [second_stage(1, second, hidden1)])
-        y_third0 = copy_out("y_third0", [second_stage(0, third, hidden0)], "h_planes1")
-        y_third1 = copy_out("y_third1", [second_stage(1, third, hidden1)])
-        y_last = tile("y_last", [P, J], F32, tag="act")
-        for h, hidden in enumerate((hidden0, hidden1)):
-            nc.scalar.copy(out=y_last[:, h * HALF : (h + 1) * HALF], in_=second_stage(h, last, hidden)[:])
-        for t, tag in ((third, "h_w1"), (last, "h_s1")):
-            pages[t] = tile("page%d" % t, [P, T], F32, tag=tag)
-            nc.gpsimd.memset(pages[t][:], 0.0)
+        y_later = {}
+        for t, tag in ((third, "h_planes1"), (last, "act")):
+            y_later[t] = tile("y_later%d" % t, [P, J], F32, tag=tag)
+            for h, hidden in enumerate((hidden0, hidden1)):
+                nc.scalar.copy(out=y_later[t][:, h * HALF : (h + 1) * HALF], in_=second_stage(h, t, hidden)[:])
 
         scatter(first, y_first1, 1)
         finish_page(first)
         scatter(second, y_second1, 1)
         finish_page(second)
-        scatter(third, y_third0, 0)
-        scatter(third, y_third1, 1)
+        scatter(third, y_later[third])
         finish_page(third)
-        gather_gate(last, "page%d" % first)
-        scatter(last, y_last)
+        gather_gate(last, "y_second1")
+        pages[last] = pages[first]
+        scatter(last, y_later[last])
         finish_page(last)
         for cols in chunks[VECTOR_CHUNKS:]:
             nc.scalar.copy(out=out_bf[:, cols, last], in_=pages[last][:, cols])

@@ -23,8 +23,9 @@ QUADS = 4
 HALF = 512
 HALVES = J // HALF
 LIST_ROWS = 16
-OUT_CHUNKS = (512, 512, 512, 512)
-VECTOR_CHUNKS = 2
+OUT_CHUNKS = (512, 512, 256, 512, 256)
+VECTOR_CHUNKS = 3
+SIDE = T // 2
 ORDER = (2, 0, 1, 3)
 
 
@@ -78,11 +79,11 @@ def tile_list_msg_gelu_gateP_kernel(tc, tab_words, tab_scales, ws, wt_words, wt_
         nc.vector.memset(moved[:].rearrange("p a c -> p (a c)").bitcast(I32), 0)
         pages = {}
 
-        def clear_page(t, tag=None):
+        def clear_page(t, engine, tag=None):
             pages[t] = tile("page%d" % t, [P, T], F32, tag=tag)
-            nc.vector.memset(pages[t][:], 0.0)
+            engine.memset(pages[t][:], 0.0)
 
-        clear_page(first)
+        clear_page(first, nc.vector)
 
         def round_and_deal(dst, raw):
             nc.scalar.copy(
@@ -157,7 +158,7 @@ def tile_list_msg_gelu_gateP_kernel(tc, tab_words, tab_scales, ws, wt_words, wt_
         nc.sync.dma_start(out=wgo_t[:], in_=wgo)
         gates = {}
         g_rows = gT.rearrange("(p t) c -> t p c", t=PACK)
-        for t, tag in zip(ORDER, ("wt_w_raw", "ws_raw1", "ws_bf", "wd_bf")):
+        for t, tag in zip(ORDER, ("wt_w_raw", "ws_raw1", "tab_w", "wd_bf")):
             gates[t] = tile("gate%d" % t, [P, T], F32, tag=tag)
             nc.sync.dma_start(out=gates[t][:], in_=g_rows[t])
 
@@ -229,10 +230,14 @@ def tile_list_msg_gelu_gateP_kernel(tc, tab_words, tab_scales, ws, wt_words, wt_
             nc.vector.tensor_tensor(factors[t][:], gates[t][:].indirect(src_list[:]), wgo_t[:], MULT)
 
         out_rows = out_0.rearrange("(p t) c -> t p c", t=PACK)
-        out_bf = tile("out_bf", [P, T, PACK], BF16)
+        out_bf = [tile("out_bf%d" % c, [P, SIDE, PACK], BF16) for c in range(2)]
+        twins = [tile("twins%d" % c, [P, 2, SIDE, 2], BF16, tag=tag) for c, tag in enumerate(("ws_raw1", "ws_raw0"))]
         starts = [sum(OUT_CHUNKS[:i]) for i in range(len(OUT_CHUNKS) + 1)]
         chunks = [slice(starts[i], starts[i + 1]) for i in range(len(OUT_CHUNKS))]
-        split = starts[VECTOR_CHUNKS]
+
+        def woven_out(cols):
+            side, start = divmod(cols.start, SIDE)
+            return out_bf[side][:, start : start + cols.stop - cols.start, :]
 
         def copy_out(name, accs, tag=None):
             y = tile(name, [P, len(accs) * HALF], F32, tag=tag)
@@ -247,16 +252,27 @@ def tile_list_msg_gelu_gateP_kernel(tc, tab_words, tab_scales, ws, wt_words, wt_
 
         def finish_page(t):
             nc.sync.dma_start(out=out_rows[t], in_=pages[t][:])
-            if t != last:
-                for cols in (slice(0, split), slice(split, T)):
-                    nc.scalar.copy(out=out_bf[:, cols, t], in_=pages[t][:, cols])
+            for c in range(2 if t != last else 0):
+                source = pages[t][:, c * SIDE : (c + 1) * SIDE]
+                if t == first:
+                    nc.scalar.copy(out=twins[c][:, 1, :, :], in_=source.unsqueeze(2).to_broadcast([P, SIDE, 2]))
+                else:
+                    nc.scalar.copy(out=twins[c][:, 0, :, t], in_=source)
+                if t == third:
+                    nc.scalar.copy(
+                        out=out_bf[c][:].bitcast(U32),
+                        in_=twins[c][:].bitcast(U32).rearrange("p u c o -> p c (u o)"),
+                    )
 
+        clear_page(second, nc.gpsimd, "ws_bf")
         planes0 = first_stage(0)
         woven0 = weave(0, planes0, nc.scalar.copy)
-        for t in (first, second, third):
-            gather_gate(t)
-        hidden0 = quantise_hidden(0, woven0, "ws_bf")
-        clear_page(second, "h_bf0")
+        gather_gate(first)
+        clear_page(third, nc.gpsimd, "wt_w_raw")
+        gather_gate(second)
+        gather_gate(third)
+        hidden0 = quantise_hidden(0, woven0, "tab_w")
+        gather_gate(last, "h_bf0")
         y_first0 = copy_out("y_first0", [second_stage(0, first, hidden0)])
         y_second0 = copy_out("y_second0", [second_stage(0, second, hidden0)])
         scatter(first, y_first0, 0)
@@ -264,40 +280,33 @@ def tile_list_msg_gelu_gateP_kernel(tc, tab_words, tab_scales, ws, wt_words, wt_
         planes1 = first_stage(1)
         woven1 = weave(1, planes1, nc.scalar.copy)
         hidden1 = quantise_hidden(1, woven1, None)
-        clear_page(third, "h_bf1")
-        y_first1 = copy_out("y_first1", [second_stage(1, first, hidden1)])
-        y_second1 = copy_out("y_second1", [second_stage(1, second, hidden1)])
-        y_later = {}
-        for t, tag in ((third, "h_planes1"), (last, "act")):
-            y_later[t] = tile("y_later%d" % t, [P, J], F32, tag=tag)
-            for h, hidden in enumerate((hidden0, hidden1)):
-                nc.scalar.copy(out=y_later[t][:, h * HALF : (h + 1) * HALF], in_=second_stage(h, t, hidden)[:])
-
-        scatter(first, y_first1, 1)
-        finish_page(first)
-        scatter(second, y_second1, 1)
-        finish_page(second)
-        scatter(third, y_later[third])
-        finish_page(third)
-        gather_gate(last, "y_second1")
+        y_third0 = copy_out("y_third0", [second_stage(0, third, hidden0)], "h_planes1")
+        scatter(third, y_third0, 0)
+        later = {t: copy_out("y_later%d" % t, [second_stage(1, t, hidden1)]) for t in (first, second, third)}
+        y_last = tile("y_last", [P, J], F32, tag="act")
+        for h, hidden in enumerate((hidden0, hidden1)):
+            nc.scalar.copy(out=y_last[:, h * HALF : (h + 1) * HALF], in_=second_stage(h, last, hidden)[:])
+        for t in (first, second, third):
+            scatter(t, later[t], 1)
+            finish_page(t)
         pages[last] = pages[first]
-        scatter(last, y_later[last])
+        scatter(last, y_last)
         finish_page(last)
         for cols in chunks[VECTOR_CHUNKS:]:
-            nc.scalar.copy(out=out_bf[:, cols, last], in_=pages[last][:, cols])
+            nc.scalar.copy(out=woven_out(cols)[:, :, last], in_=pages[last][:, cols])
 
         out_w = tile("out_w", [P, T], U32)
         out_s = tile("out_s", [P, T], U8)
         code_rows = out_1[0].rearrange("p t i -> p (t i)").bitcast(I32)
         for i in range(len(chunks) + 1):
             if i < VECTOR_CHUNKS:
-                nc.vector.tensor_copy(out_bf[:, chunks[i], last], pages[last][:, chunks[i]])
+                nc.vector.tensor_copy(woven_out(chunks[i])[:, :, last], pages[last][:, chunks[i]])
             if i > 0:
                 cols = chunks[i - 1]
                 nc.vector.quantize_mx(
                     out=out_w[:, cols].bitcast(FP8X4),
                     scales=out_s[:, cols],
-                    in_=out_bf[:, cols, :].rearrange("p c t -> p (c t)"),
+                    in_=woven_out(cols).rearrange("p c t -> p (c t)"),
                 )
                 nc.sync.dma_start(out=code_rows[:, cols], in_=out_w[:, cols].bitcast(I32))
         for q in range(QUADS):

@@ -46,7 +46,7 @@ def tile_list_msg_gelu_gateP_kernel(tc, tab_words, tab_scales, ws, wt_words, wt_
         nc.sync.dma_start(dst_list[:], offs2)
 
         first, second, third, last = ORDER
-        tab_s = tile("tab_s", [P, T], U8, tag="act")
+        tab_s = tile("tab_s", [P, T], U8)
         nc.sync.dma_start(
             out=tab_s[96:128, :].bitcast(I32),
             in_=tab_scales.bitcast(I32).rearrange("a b t -> b a t"),
@@ -74,6 +74,8 @@ def tile_list_msg_gelu_gateP_kernel(tc, tab_words, tab_scales, ws, wt_words, wt_
                 out=wt_s_raw[32 * q : 32 * q + 4, :].bitcast(I32).rearrange("q (a r) -> q a r", a=2),
                 in_=wt_scales[:, 4 * q : 4 * q + 4, :].bitcast(I32).rearrange("a q r -> q a r"),
             )
+        wd_raw = tile("wd_raw", [P, PACK, N], F32, tag="act")
+        nc.sync.dma_start(out=wd_raw[:], in_=wd.rearrange("(p j) n -> p j n", j=PACK))
 
         moved = tile("moved", [P, 2, 2 * J], U8)
         nc.vector.memset(moved[:].rearrange("p a c -> p (a c)").bitcast(I32), 0)
@@ -111,9 +113,6 @@ def tile_list_msg_gelu_gateP_kernel(tc, tab_words, tab_scales, ws, wt_words, wt_
                 in_=packed[96 + 8 * q : 104 + 8 * q, :].bitcast(I32),
             )
         v_s = [[moved[:, a, u * J : (u + 1) * J] for a in range(2)] for u in range(2)]
-
-        wd_raw = tile("wd_raw", [P, PACK, N], F32, tag="act")
-        nc.sync.dma_start(out=wd_raw[:], in_=wd.rearrange("(p j) n -> p j n", j=PACK))
 
         v_w = {}
         pairs0 = tile("pairs0", [P, 2, HALF], U32)
@@ -154,11 +153,11 @@ def tile_list_msg_gelu_gateP_kernel(tc, tab_words, tab_scales, ws, wt_words, wt_
         wd_s = tile("wd_s", [P, N], U8)
         nc.vector.quantize_mx(out=wd_w[:].bitcast(FP8X4), scales=wd_s[:], in_=wd_bf[:])
 
-        wgo_t = tile("wgo_t", [P, J], F32, tag="pairs0")
+        wgo_t = tile("wgo_t", [P, J], F32, tag="tab_s")
         nc.sync.dma_start(out=wgo_t[:], in_=wgo)
         gates = {}
         g_rows = gT.rearrange("(p t) c -> t p c", t=PACK)
-        for t, tag in zip(ORDER, ("wt_w_raw", "ws_raw1", "tab_w", "wd_bf")):
+        for t, tag in zip(ORDER, ("ws_raw0", "ws_raw1", "packed", "wt_w_raw")):
             gates[t] = tile("gate%d" % t, [P, T], F32, tag=tag)
             nc.sync.dma_start(out=gates[t][:], in_=g_rows[t])
 
@@ -231,7 +230,7 @@ def tile_list_msg_gelu_gateP_kernel(tc, tab_words, tab_scales, ws, wt_words, wt_
 
         out_rows = out_0.rearrange("(p t) c -> t p c", t=PACK)
         out_bf = [tile("out_bf%d" % c, [P, SIDE, PACK], BF16) for c in range(2)]
-        twins = [tile("twins%d" % c, [P, 2, SIDE, 2], BF16, tag=tag) for c, tag in enumerate(("ws_raw1", "ws_raw0"))]
+        twins = [tile("twins%d" % c, [P, 2, SIDE, 2], BF16, tag=tag) for c, tag in enumerate(("ws_raw1", "wt_w_raw"))]
         starts = [sum(OUT_CHUNKS[:i]) for i in range(len(OUT_CHUNKS) + 1)]
         chunks = [slice(starts[i], starts[i + 1]) for i in range(len(OUT_CHUNKS))]
 
@@ -264,18 +263,18 @@ def tile_list_msg_gelu_gateP_kernel(tc, tab_words, tab_scales, ws, wt_words, wt_
                         in_=twins[c][:].bitcast(U32).rearrange("p u c o -> p c (u o)"),
                     )
 
-        clear_page(second, nc.gpsimd, "ws_bf")
         planes0 = first_stage(0)
         woven0 = weave(0, planes0, nc.scalar.copy)
         gather_gate(first)
-        clear_page(third, nc.gpsimd, "wt_w_raw")
+        clear_page(second, nc.gpsimd, "ws_raw0")
         gather_gate(second)
         gather_gate(third)
-        hidden0 = quantise_hidden(0, woven0, "tab_w")
+        hidden0 = quantise_hidden(0, woven0, "packed")
         gather_gate(last, "h_bf0")
         y_first0 = copy_out("y_first0", [second_stage(0, first, hidden0)])
         y_second0 = copy_out("y_second0", [second_stage(0, second, hidden0)])
         scatter(first, y_first0, 0)
+        clear_page(third, nc.gpsimd, "y_first0")
         scatter(second, y_second0, 0)
         planes1 = first_stage(1)
         woven1 = weave(1, planes1, nc.scalar.copy)

@@ -23,8 +23,8 @@ QUADS = 4
 HALF = 512
 HALVES = J // HALF
 LIST_ROWS = 16
-OUT_CHUNKS = (512, 512, 256, 512, 256)
-VECTOR_CHUNKS = 3
+OUT_CHUNKS = (512, 512, 512, 256, 256)
+VECTOR_CHUNKS = 2
 SIDE = T // 2
 ORDER = (2, 0, 1, 3)
 
@@ -52,17 +52,19 @@ def tile_list_msg_gelu_gateP_kernel(tc, tab_words, tab_scales, ws, wt_words, wt_
             in_=tab_scales.bitcast(I32).rearrange("a b t -> b a t"),
         )
         nc.vector.memset(tab_s[0:96, :].bitcast(I32), 0)
-        tab_w = tile("tab_w", [P, T], I32)
-        nc.sync.dma_start(out=tab_w[:], in_=tab_words[0].rearrange("p t i -> p (t i)").bitcast(I32))
         warm = tile("warm", [P, 2], F32)
         nc.gpsimd.memset(warm[:, 0:1], 0.0)
         nc.scalar.activation(out=warm[:, 1:2], in_=warm[:, 0:1], func=GELU)
 
-        ws_raw = []
-        for a in range(2):
+        def load_ws(a):
             raw = tile("ws_raw%d" % a, [P, PACK, R], F32)
             nc.sync.dma_start(out=raw[:], in_=ws[512 * a : 512 * (a + 1), :].rearrange("(p j) r -> p j r", j=PACK))
-            ws_raw.append(raw)
+            return raw
+
+        ws_raw = [load_ws(0)]
+        tab_w = tile("tab_w", [P, T], I32)
+        nc.sync.dma_start(out=tab_w[:], in_=tab_words[0].rearrange("p t i -> p (t i)").bitcast(I32))
+        ws_raw.append(load_ws(1))
         wt_w_raw = tile("wt_w_raw", [P, 2, R], I32)
         wt_s_raw = tile("wt_s_raw", [P, 2 * R], U8)
         nc.vector.memset(wt_s_raw[:].bitcast(I32), 0)
@@ -84,8 +86,6 @@ def tile_list_msg_gelu_gateP_kernel(tc, tab_words, tab_scales, ws, wt_words, wt_
         def clear_page(t, engine, tag=None):
             pages[t] = tile("page%d" % t, [P, T], F32, tag=tag)
             engine.memset(pages[t][:], 0.0)
-
-        clear_page(first, nc.vector)
 
         def round_and_deal(dst, raw):
             nc.scalar.copy(
@@ -149,7 +149,7 @@ def tile_list_msg_gelu_gateP_kernel(tc, tab_words, tab_scales, ws, wt_words, wt_
 
         wd_bf = tile("wd_bf", [P, PACK * N], BF16)
         round_and_deal(wd_bf[:], wd_raw)
-        wd_w = tile("wd_w", [P, N], U32)
+        wd_w = tile("wd_w", [P, N], U32, tag="ws_bf")
         wd_s = tile("wd_s", [P, N], U8)
         nc.vector.quantize_mx(out=wd_w[:].bitcast(FP8X4), scales=wd_s[:], in_=wd_bf[:])
 
@@ -249,20 +249,24 @@ def tile_list_msg_gelu_gateP_kernel(tc, tab_words, tab_scales, ws, wt_words, wt_
             factor = factors[t][:] if h is None else factors[t][:, h * HALF : (h + 1) * HALF]
             nc.vector.tensor_tensor(pages[t][:].indirect(offsets), y[:], factor, MULT)
 
+        def weave_twins(c, part):
+            nc.scalar.copy(
+                out=out_bf[c][:, part, :].bitcast(U32),
+                in_=twins[c][:, :, part, :].bitcast(U32).rearrange("p u c o -> p c (u o)"),
+            )
+
         def finish_page(t):
             nc.sync.dma_start(out=out_rows[t], in_=pages[t][:])
             for c in range(2 if t != last else 0):
                 source = pages[t][:, c * SIDE : (c + 1) * SIDE]
-                if t == first:
+                if (t, c) == (first, 0):
                     nc.scalar.copy(out=twins[c][:, 1, :, :], in_=source.unsqueeze(2).to_broadcast([P, SIDE, 2]))
                 else:
-                    nc.scalar.copy(out=twins[c][:, 0, :, t], in_=source)
-                if t == third:
-                    nc.scalar.copy(
-                        out=out_bf[c][:].bitcast(U32),
-                        in_=twins[c][:].bitcast(U32).rearrange("p u c o -> p c (u o)"),
-                    )
+                    nc.scalar.copy(out=twins[c][:, t // 2, :, t % 2], in_=source)
+                if (t, c) == (third, 0):
+                    weave_twins(0, slice(0, SIDE))
 
+        clear_page(first, nc.gpsimd, "wd_bf")
         planes0 = first_stage(0)
         woven0 = weave(0, planes0, nc.scalar.copy)
         gather_gate(first)
@@ -292,7 +296,9 @@ def tile_list_msg_gelu_gateP_kernel(tc, tab_words, tab_scales, ws, wt_words, wt_
         scatter(last, y_last)
         finish_page(last)
         for cols in chunks[VECTOR_CHUNKS:]:
-            nc.scalar.copy(out=woven_out(cols)[:, :, last], in_=pages[last][:, cols])
+            part = slice(cols.start - SIDE, cols.stop - SIDE)
+            nc.scalar.copy(out=twins[1][:, last // 2, part, last % 2], in_=pages[last][:, cols])
+            weave_twins(1, part)
 
         out_w = tile("out_w", [P, T], U32)
         out_s = tile("out_s", [P, T], U8)

@@ -1,6 +1,7 @@
 from contextlib import ExitStack
 
 import concourse.mybir as mybir
+from concourse.masks import make_identity
 
 K, R, N, T, J = 1024, 512, 512, 2048, 1024
 FLOPS = 2 * J * R * (2 * K + N)
@@ -42,19 +43,22 @@ def tile_list_msg_gelu_gateP_kernel(tc, tab_words, tab_scales, ws, wt_words, wt_
         src_list = tile("src_list", [P, J // LIST_ROWS], U16)
         dst_list = tile("dst_list", [P, J // LIST_ROWS], U16)
         lists = (src_list, dst_list)
-        nc.sync.dma_start(src_list[:], offs)
-        nc.sync.dma_start(dst_list[:], offs2)
-
         first, second, third, last = ORDER
-        tab_s = tile("tab_s", [P, T], U8)
+        wt_s = tile("wt_s", [P, 2, R], U8)
+        nc.vector.memset(wt_s[:].rearrange("p a r -> p (a r)").bitcast(I32), 0)
+        tab_s = tile("tab_s", [P, T], U8, tag="act")
+        nc.sync.dma_start(src_list[:], offs)
         nc.sync.dma_start(
             out=tab_s[96:128, :].bitcast(I32),
             in_=tab_scales.bitcast(I32).rearrange("a b t -> b a t"),
         )
+        nc.sync.dma_start(dst_list[:], offs2)
         nc.vector.memset(tab_s[0:96, :].bitcast(I32), 0)
         warm = tile("warm", [P, 2], F32)
         nc.gpsimd.memset(warm[:, 0:1], 0.0)
         nc.scalar.activation(out=warm[:, 1:2], in_=warm[:, 0:1], func=GELU)
+        identity = tile("identity", [P, P], F32)
+        make_identity(nc, identity[:])
 
         def load_ws(a):
             raw = tile("ws_raw%d" % a, [P, PACK, R], F32)
@@ -64,20 +68,14 @@ def tile_list_msg_gelu_gateP_kernel(tc, tab_words, tab_scales, ws, wt_words, wt_
         ws_raw = [load_ws(0)]
         tab_w = tile("tab_w", [P, T], I32)
         nc.sync.dma_start(out=tab_w[:], in_=tab_words[0].rearrange("p t i -> p (t i)").bitcast(I32))
-        ws_raw.append(load_ws(1))
-        wt_w_raw = tile("wt_w_raw", [P, 2, R], I32)
-        wt_s_raw = tile("wt_s_raw", [P, 2 * R], U8)
-        nc.vector.memset(wt_s_raw[:].bitcast(I32), 0)
-        nc.sync.dma_start(out=wt_w_raw[:], in_=wt_words.rearrange("a p r i -> p a (r i)").bitcast(I32))
         sm_t = tile("sm_t", [P, PACK], F32)
         nc.sync.dma_start(out=sm_t[:], in_=sm.rearrange("(p t) -> p t", t=PACK))
         for q in range(QUADS):
             nc.sync.dma_start(
-                out=wt_s_raw[32 * q : 32 * q + 4, :].bitcast(I32).rearrange("q (a r) -> q a r", a=2),
+                out=wt_s[32 * q : 32 * q + 4, :, :].bitcast(I32),
                 in_=wt_scales[:, 4 * q : 4 * q + 4, :].bitcast(I32).rearrange("a q r -> q a r"),
             )
-        wd_raw = tile("wd_raw", [P, PACK, N], F32, tag="act")
-        nc.sync.dma_start(out=wd_raw[:], in_=wd.rearrange("(p j) n -> p j n", j=PACK))
+        ws_raw.append(load_ws(1))
 
         moved = tile("moved", [P, 2, 2 * J], U8)
         nc.vector.memset(moved[:].rearrange("p a c -> p (a c)").bitcast(I32), 0)
@@ -105,92 +103,93 @@ def tile_list_msg_gelu_gateP_kernel(tc, tab_words, tab_scales, ws, wt_words, wt_
             return parted
 
         packed = tile("packed", [P, 2 * J], U8)
-        for u in (1, 0):
+        for u in range(2):
             nc.vector.tensor_copy(packed[:, u * J : (u + 1) * J], tab_s[:].indirect(lists[u][:]))
         for q in range(QUADS):
             nc.sync.dma_start(
                 out=moved[32 * q : 32 * q + 4, :, :].bitcast(I32),
                 in_=packed[96 + 8 * q : 104 + 8 * q, :].bitcast(I32),
             )
+        wd_raw = tile("wd_raw", [P, PACK, N], F32, tag="act")
+        nc.sync.dma_start(out=wd_raw[:], in_=wd.rearrange("(p j) n -> p j n", j=PACK))
         v_s = [[moved[:, a, u * J : (u + 1) * J] for a in range(2)] for u in range(2)]
 
         v_w = {}
         pairs0 = tile("pairs0", [P, 2, HALF], U32)
-        for u in (1, 0):
+        for u in range(2):
             gather_words(u, 0, pairs0[:, u, :])
-        for u in (1, 0):
+        for u in range(2):
             v_w[u, 0] = part_words(u, 0, pairs0[:, u, :])
 
-        wt_w = tile("wt_w", [P, 2, R], I32)
-        wt_s = tile("wt_s", [P, 2, R], U8)
-        nc.vector.tensor_copy(
-            wt_w[:].rearrange("p a (t m) -> p a m t", t=PACK), wt_w_raw[:].rearrange("p a (m t) -> p a m t", t=PACK)
-        )
-        nc.vector.tensor_copy(
-            wt_s[:].rearrange("p a (t m) -> p a m t", t=PACK), wt_s_raw[:].rearrange("p (a m t) -> p a m t", a=2, t=PACK)
-        )
-
         ws_w = tile("ws_w", [P, 2, R], U32)
-        ws_s = tile("ws_s", [P, 2, R], U8, tag="wt_s_raw")
+        ws_s = tile("ws_s", [P, 2, R], U8)
         ws_bf = tile("ws_bf", [P, 2, PACK * R], BF16)
         for a in range(2):
-            round_and_deal(ws_bf[:, a, :], ws_raw[a])
-        nc.vector.quantize_mx(
-            out=ws_w[:].rearrange("p a r -> p (a r)").bitcast(FP8X4),
-            scales=ws_s[:].rearrange("p a r -> p (a r)"),
-            in_=ws_bf[:].rearrange("p a r -> p (a r)"),
-        )
+            nc.scalar.copy(
+                out=ws_bf[:, a, :].rearrange("p (c i j) -> p c j i", i=4, j=PACK),
+                in_=ws_raw[a][:].rearrange("p j (c i) -> p c j i", i=4),
+            )
+        wt_w = tile("wt_w", [P, 2, R], I32, tag="ws_raw0")
+        nc.sync.dma_start(out=wt_w[:], in_=wt_words.rearrange("a p r i -> p a (r i)").bitcast(I32))
+        for a in range(2):
+            nc.vector.quantize_mx(out=ws_w[:, a, :].bitcast(FP8X4), scales=ws_s[:, a, :], in_=ws_bf[:, a, :])
 
         pairs1 = tile("pairs1", [P, 2, HALF], U32, tag="ws_bf")
-        for u in (1, 0):
+        for u in range(2):
             gather_words(u, 1, pairs1[:, u, :])
-        for u in (1, 0):
+        for u in range(2):
             v_w[u, 1] = part_words(u, 1, pairs1[:, u, :])
 
         wd_bf = tile("wd_bf", [P, PACK * N], BF16)
         round_and_deal(wd_bf[:], wd_raw)
-        wd_w = tile("wd_w", [P, N], U32, tag="ws_bf")
+        wd_w = tile("wd_w", [P, N], U32)
         wd_s = tile("wd_s", [P, N], U8)
         nc.vector.quantize_mx(out=wd_w[:].bitcast(FP8X4), scales=wd_s[:], in_=wd_bf[:])
 
-        wgo_t = tile("wgo_t", [P, J], F32, tag="tab_s")
+        wgo_t = tile("wgo_t", [P, J], F32, tag="pairs0")
         nc.sync.dma_start(out=wgo_t[:], in_=wgo)
         gates = {}
         g_rows = gT.rearrange("(p t) c -> t p c", t=PACK)
-        for t, tag in zip(ORDER, ("ws_raw0", "ws_raw1", "packed", "wt_w_raw")):
+
+        def load_gate(t, tag):
             gates[t] = tile("gate%d" % t, [P, T], F32, tag=tag)
             nc.sync.dma_start(out=gates[t][:], in_=g_rows[t])
 
+        for t, tag in zip(ORDER[:3], ("packed", "ws_raw1", "ws_bf")):
+            load_gate(t, tag)
+
         def first_stage(h):
-            act = tile("act%d" % h, [P, PACK, HALF], F32, tag="act")
-            planes = tile("h_planes%d" % h, [P, PACK, HALF], BF16)
+            act = tile("act%d" % h, [P, PACK, PACK, P], F32, tag="act")
+            accs = [psum.tile([P, R], F32, name="a%d%d" % (h, i), tag="bank%d" % (PACK * h + i)) for i in range(PACK)]
 
-            def smooth(t):
-                nc.scalar.activation(out=planes[:, t, :], in_=act[:, t, :], func=COPY, scale=sm_t[:, t : t + 1])
-
-            accs = [psum.tile([P, HALF], F32, name="a%d%d" % (h, t), tag="bank%d" % t) for t in range(PACK)]
-
-            def one_pass(t, u, a):
+            def one_pass(i, u, a):
                 w_w, w_s = ((ws_w, ws_s), (wt_w, wt_s))[u]
-                m_cols = slice(t * P, (t + 1) * P)
                 nc.tensor.matmul_mx(
-                    out=accs[t][:],
-                    lhsT=w_w[:, a, m_cols].bitcast(FP8X4),
-                    lhsT_scale=w_s[:, a, m_cols],
-                    rhs=v_w[u, h][:, a, :].bitcast(FP4X4),
-                    rhs_scale=v_s[u][a][:, h * HALF : (h + 1) * HALF],
-                    start=(u, a) == (1, 0),
+                    out=accs[i][:],
+                    lhsT=v_w[u, h][:, a, 2 * i * P : 2 * (i + 1) * P].bitcast(FP4X4),
+                    lhsT_scale=v_s[u][a][:, h * HALF + i * P : h * HALF + (i + 1) * P],
+                    rhs=w_w[:, a, :].bitcast(FP8X4),
+                    rhs_scale=w_s[:, a, :],
+                    start=(u, a) == (0, 0),
                     stop=(u, a) == (0, 1),
                 )
 
+            for i in range(PACK):
+                one_pass(i, 0, 0)
+            for i in range(PACK):
+                for u, a in ((1, 0), (1, 1), (0, 1)):
+                    one_pass(i, u, a)
+                nc.scalar.activation(out=act[:, i, :, :], in_=accs[i][:].rearrange("p (m t) -> p t m", t=PACK), func=GELU)
+            return act
+
+        def turn_and_smooth(h, act):
+            planes = tile("h_planes%d" % h, [P, PACK, HALF], BF16)
+            turned = [psum.tile([P, HALF], F32, name="t%d%d" % (h, t), tag="bank%d" % (PACK * (1 - h) + t)) for t in range(PACK)]
+            for i in range(PACK):
+                for t in range(PACK):
+                    nc.tensor.transpose(turned[t][:, i * P : (i + 1) * P], act[:, i, t, :], identity[:])
             for t in range(PACK):
-                for u in (1, 0):
-                    for a in range(2):
-                        one_pass(t, u, a)
-                nc.scalar.activation(out=act[:, t, :], in_=accs[t][:], func=GELU)
-                if t > 0:
-                    smooth(t - 1)
-            smooth(PACK - 1)
+                nc.scalar.activation(out=planes[:, t, :], in_=turned[t][:], func=COPY, scale=sm_t[:, t : t + 1])
             return planes
 
         def weave(h, planes, copy):
@@ -208,7 +207,7 @@ def tile_list_msg_gelu_gateP_kernel(tc, tab_words, tab_scales, ws, wt_words, wt_
             return h_w, h_s
 
         def second_stage(h, t, hidden):
-            bank = PACK + t
+            bank = PACK + ORDER.index(t)
             acc = psum.tile([P, HALF], F32, name="y%d%d" % (h, t), tag="bank%d" % bank)
             m_cols = slice(t * P, (t + 1) * P)
             nc.tensor.matmul_mx(
@@ -230,7 +229,7 @@ def tile_list_msg_gelu_gateP_kernel(tc, tab_words, tab_scales, ws, wt_words, wt_
 
         out_rows = out_0.rearrange("(p t) c -> t p c", t=PACK)
         out_bf = [tile("out_bf%d" % c, [P, SIDE, PACK], BF16) for c in range(2)]
-        twins = [tile("twins%d" % c, [P, 2, SIDE, 2], BF16, tag=tag) for c, tag in enumerate(("ws_raw1", "wt_w_raw"))]
+        twins = [tile("twins%d" % c, [P, 2, SIDE, 2], BF16, tag=tag) for c, tag in enumerate(("ws_raw0", "pairs0"))]
         starts = [sum(OUT_CHUNKS[:i]) for i in range(len(OUT_CHUNKS) + 1)]
         chunks = [slice(starts[i], starts[i + 1]) for i in range(len(OUT_CHUNKS))]
 
@@ -267,20 +266,22 @@ def tile_list_msg_gelu_gateP_kernel(tc, tab_words, tab_scales, ws, wt_words, wt_
                     weave_twins(0, slice(0, SIDE))
 
         clear_page(first, nc.gpsimd, "wd_bf")
-        planes0 = first_stage(0)
+        planes0 = turn_and_smooth(0, first_stage(0))
         woven0 = weave(0, planes0, nc.scalar.copy)
         gather_gate(first)
-        clear_page(second, nc.gpsimd, "ws_raw0")
+        load_gate(last, "packed")
         gather_gate(second)
+        clear_page(second, nc.gpsimd, "ws_raw1")
         gather_gate(third)
-        hidden0 = quantise_hidden(0, woven0, "packed")
+        hidden0 = quantise_hidden(0, woven0, "ws_bf")
         gather_gate(last, "h_bf0")
+        act1 = first_stage(1)
         y_first0 = copy_out("y_first0", [second_stage(0, first, hidden0)])
         y_second0 = copy_out("y_second0", [second_stage(0, second, hidden0)])
         scatter(first, y_first0, 0)
         clear_page(third, nc.gpsimd, "y_first0")
         scatter(second, y_second0, 0)
-        planes1 = first_stage(1)
+        planes1 = turn_and_smooth(1, act1)
         woven1 = weave(1, planes1, nc.scalar.copy)
         hidden1 = quantise_hidden(1, woven1, None)
         y_third0 = copy_out("y_third0", [second_stage(0, third, hidden0)], "h_planes1")

@@ -22,11 +22,12 @@ P = 128
 PACK = 4
 QUADS = 4
 HALF = 512
-HALVES = J // HALF
+GROUP = HALF // 2
 LIST_ROWS = 16
-OUT_CHUNKS = (512, 512, 512, 256, 256)
+OUT_CHUNKS = (512, 512, 256, 512, 256)
 VECTOR_CHUNKS = 2
 SIDE = T // 2
+RUN = J // P
 ORDER = (2, 0, 1, 3)
 
 
@@ -35,6 +36,7 @@ def tile_list_msg_gelu_gateP_kernel(tc, tab_words, tab_scales, ws, wt_words, wt_
 
     with ExitStack() as ctx:
         keep = ctx.enter_context(tc.tile_pool(name="keep", bufs=1))
+        placed = ctx.enter_context(tc.tile_pool(name="placed", bufs=1))
         psum = ctx.enter_context(tc.psum_pool(name="psum", bufs=1))
 
         def tile(name, shape, dtype, tag=None):
@@ -65,6 +67,8 @@ def tile_list_msg_gelu_gateP_kernel(tc, tab_words, tab_scales, ws, wt_words, wt_
             nc.sync.dma_start(out=raw[:], in_=ws[512 * a : 512 * (a + 1), :].rearrange("(p j) r -> p j r", j=PACK))
             return raw
 
+        wgo_runs = tile("wgo_runs", [P, RUN], F32)
+        nc.sync.dma_start(out=wgo_runs[:], in_=wgo[0].rearrange("(p i) -> p i", i=RUN))
         ws_raw = [load_ws(0)]
         tab_w = tile("tab_w", [P, T], I32)
         nc.sync.dma_start(out=tab_w[:], in_=tab_words[0].rearrange("p t i -> p (t i)").bitcast(I32))
@@ -77,19 +81,21 @@ def tile_list_msg_gelu_gateP_kernel(tc, tab_words, tab_scales, ws, wt_words, wt_
             )
         ws_raw.append(load_ws(1))
 
+        wgo_t = tile("wgo_t", [P, P, RUN], F32)
+        for b in range(RUN // PACK):
+            spread = psum.tile([P, PACK, P], F32, name="spread%d" % b, tag="bank%d" % (PACK + b))
+            for i in range(PACK):
+                column = wgo_runs[:, PACK * b + i : PACK * b + i + 1]
+                nc.tensor.transpose(spread[:, i, :], column.to_broadcast([P, P]), identity[:])
+            nc.scalar.copy(out=wgo_t[:, :, PACK * b : PACK * (b + 1)], in_=spread[:].rearrange("c i p -> c p i"))
+
         moved = tile("moved", [P, 2, 2 * J], U8)
         nc.vector.memset(moved[:].rearrange("p a c -> p (a c)").bitcast(I32), 0)
         pages = {}
 
-        def clear_page(t, engine, tag=None):
-            pages[t] = tile("page%d" % t, [P, T], F32, tag=tag)
-            engine.memset(pages[t][:], 0.0)
-
-        def round_and_deal(dst, raw):
-            nc.scalar.copy(
-                out=dst.rearrange("p (t m j) -> p m j t", t=PACK, j=PACK),
-                in_=raw[:].rearrange("p j (m t) -> p m j t", t=PACK),
-            )
+        def clear_page(t, page):
+            pages[t] = page
+            nc.gpsimd.memset(page[:], 0.0)
 
         def list_cols(h):
             return slice(h * HALF // LIST_ROWS, (h + 1) * HALF // LIST_ROWS)
@@ -110,15 +116,15 @@ def tile_list_msg_gelu_gateP_kernel(tc, tab_words, tab_scales, ws, wt_words, wt_
                 out=moved[32 * q : 32 * q + 4, :, :].bitcast(I32),
                 in_=packed[96 + 8 * q : 104 + 8 * q, :].bitcast(I32),
             )
-        wd_raw = tile("wd_raw", [P, PACK, N], F32, tag="act")
-        nc.sync.dma_start(out=wd_raw[:], in_=wd.rearrange("(p j) n -> p j n", j=PACK))
+        wt_w = tile("wt_w", [P, 2, R], I32, tag="act")
+        nc.sync.dma_start(out=wt_w[:], in_=wt_words.rearrange("a p r i -> p a (r i)").bitcast(I32))
         v_s = [[moved[:, a, u * J : (u + 1) * J] for a in range(2)] for u in range(2)]
 
         v_w = {}
         pairs0 = tile("pairs0", [P, 2, HALF], U32)
-        for u in range(2):
+        for u in (1, 0):
             gather_words(u, 0, pairs0[:, u, :])
-        for u in range(2):
+        for u in (1, 0):
             v_w[u, 0] = part_words(u, 0, pairs0[:, u, :])
 
         ws_w = tile("ws_w", [P, 2, R], U32)
@@ -129,25 +135,28 @@ def tile_list_msg_gelu_gateP_kernel(tc, tab_words, tab_scales, ws, wt_words, wt_
                 out=ws_bf[:, a, :].rearrange("p (c i j) -> p c j i", i=4, j=PACK),
                 in_=ws_raw[a][:].rearrange("p j (c i) -> p c j i", i=4),
             )
-        wt_w = tile("wt_w", [P, 2, R], I32, tag="ws_raw0")
-        nc.sync.dma_start(out=wt_w[:], in_=wt_words.rearrange("a p r i -> p a (r i)").bitcast(I32))
+        wd_raw = tile("wd_raw", [P, 2, PACK, N // 2], F32, tag="ws_raw0")
+        for b in range(2):
+            nc.sync.dma_start(out=wd_raw[:, b, :, :], in_=wd[:, b * N // 2 : (b + 1) * N // 2].rearrange("(p j) n -> p j n", j=PACK))
         for a in range(2):
             nc.vector.quantize_mx(out=ws_w[:, a, :].bitcast(FP8X4), scales=ws_s[:, a, :], in_=ws_bf[:, a, :])
 
         pairs1 = tile("pairs1", [P, 2, HALF], U32, tag="ws_bf")
-        for u in range(2):
+        for u in (1, 0):
             gather_words(u, 1, pairs1[:, u, :])
-        for u in range(2):
+        for u in (1, 0):
             v_w[u, 1] = part_words(u, 1, pairs1[:, u, :])
 
-        wd_bf = tile("wd_bf", [P, PACK * N], BF16)
-        round_and_deal(wd_bf[:], wd_raw)
+        wd_bf = placed.tile([P, PACK * N], BF16, name="wd_bf", align_bytes=64, offset=4 * T - PACK * N)
+        for b in range(2):
+            nc.scalar.copy(
+                out=wd_bf[:].rearrange("p (t b m j) -> p b m j t", t=PACK, b=2, j=PACK)[:, b],
+                in_=wd_raw[:, b, :, :].rearrange("p j (m t) -> p m j t", t=PACK),
+            )
         wd_w = tile("wd_w", [P, N], U32)
         wd_s = tile("wd_s", [P, N], U8)
         nc.vector.quantize_mx(out=wd_w[:].bitcast(FP8X4), scales=wd_s[:], in_=wd_bf[:])
 
-        wgo_t = tile("wgo_t", [P, J], F32, tag="pairs0")
-        nc.sync.dma_start(out=wgo_t[:], in_=wgo)
         gates = {}
         g_rows = gT.rearrange("(p t) c -> t p c", t=PACK)
 
@@ -155,81 +164,83 @@ def tile_list_msg_gelu_gateP_kernel(tc, tab_words, tab_scales, ws, wt_words, wt_
             gates[t] = tile("gate%d" % t, [P, T], F32, tag=tag)
             nc.sync.dma_start(out=gates[t][:], in_=g_rows[t])
 
-        for t, tag in zip(ORDER[:3], ("packed", "ws_raw1", "ws_bf")):
+        for t, tag in zip(ORDER[:3], ("pairs0", "ws_raw1", "ws_bf")):
             load_gate(t, tag)
 
-        def first_stage(h):
-            act = tile("act%d" % h, [P, PACK, PACK, P], F32, tag="act")
-            accs = [psum.tile([P, R], F32, name="a%d%d" % (h, i), tag="bank%d" % (PACK * h + i)) for i in range(PACK)]
-
-            def one_pass(i, u, a):
-                w_w, w_s = ((ws_w, ws_s), (wt_w, wt_s))[u]
-                nc.tensor.matmul_mx(
-                    out=accs[i][:],
-                    lhsT=v_w[u, h][:, a, 2 * i * P : 2 * (i + 1) * P].bitcast(FP4X4),
-                    lhsT_scale=v_s[u][a][:, h * HALF + i * P : h * HALF + (i + 1) * P],
-                    rhs=w_w[:, a, :].bitcast(FP8X4),
-                    rhs_scale=w_s[:, a, :],
-                    start=(u, a) == (0, 0),
-                    stop=(u, a) == (0, 1),
-                )
-
-            for i in range(PACK):
-                one_pass(i, 0, 0)
-            for i in range(PACK):
-                for u, a in ((1, 0), (1, 1), (0, 1)):
-                    one_pass(i, u, a)
+        def sums_and_gelu(h, g, act):
+            blocks = (2 * g, 2 * g + 1)
+            accs = {i: psum.tile([P, R], F32, name="a%d%d" % (h, i), tag="bank%d" % (PACK * h + i)) for i in blocks}
+            for u, (w_w, w_s) in ((1, (wt_w, wt_s)), (0, (ws_w, ws_s))):
+                for i in blocks:
+                    for a in range(2):
+                        nc.tensor.matmul_mx(
+                            out=accs[i][:],
+                            lhsT=v_w[u, h][:, a, 2 * i * P : 2 * (i + 1) * P].bitcast(FP4X4),
+                            lhsT_scale=v_s[u][a][:, h * HALF + i * P : h * HALF + (i + 1) * P],
+                            rhs=w_w[:, a, :].bitcast(FP8X4),
+                            rhs_scale=w_s[:, a, :],
+                            start=(u, a) == (1, 0),
+                            stop=(u, a) == (0, 1),
+                        )
+            for i in blocks:
                 nc.scalar.activation(out=act[:, i, :, :], in_=accs[i][:].rearrange("p (m t) -> p t m", t=PACK), func=GELU)
-            return act
 
-        def turn_and_smooth(h, act):
-            planes = tile("h_planes%d" % h, [P, PACK, HALF], BF16)
-            turned = [psum.tile([P, HALF], F32, name="t%d%d" % (h, t), tag="bank%d" % (PACK * (1 - h) + t)) for t in range(PACK)]
-            for i in range(PACK):
-                for t in range(PACK):
-                    nc.tensor.transpose(turned[t][:, i * P : (i + 1) * P], act[:, i, t, :], identity[:])
-            for t in range(PACK):
-                nc.scalar.activation(out=planes[:, t, :], in_=turned[t][:], func=COPY, scale=sm_t[:, t : t + 1])
-            return planes
+        def turn_and_smooth(h, g, act, pairs):
+            cols = slice(2 * g * P, 2 * (g + 1) * P)
+            for u in range(2):
+                turned = psum.tile([P, 2, 2, P], F32, name="t%d%d%d" % (h, g, u), tag="bank%d" % (PACK * (1 - h) + 2 * g + u))
+                for o in range(2):
+                    for i in range(2):
+                        nc.tensor.transpose(turned[:, o, i, :], act[:, 2 * g + i, 2 * u + o, :], identity[:])
+                for o in range(2):
+                    t = 2 * u + o
+                    nc.scalar.activation(
+                        out=pairs[:, u, cols, o], in_=turned[:, o, :, :].rearrange("p i m -> p (i m)"), func=COPY, scale=sm_t[:, t : t + 1]
+                    )
 
-        def weave(h, planes, copy):
-            woven = tile("h_bf%d" % h, [P, HALF, PACK], BF16)
-            copy(
-                out=woven[:].rearrange("p (c i) t -> p c t i", i=4),
-                in_=planes[:].rearrange("p t (c i) -> p c t i", i=4),
-            )
-            return woven
+        def weave(g, pairs, woven):
+            cols = slice(g * GROUP, (g + 1) * GROUP)
+            nc.scalar.copy(out=woven.bitcast(U32), in_=pairs[:, :, cols, :].bitcast(U32).rearrange("p u c o -> p c (u o)"))
 
-        def quantise_hidden(h, woven, tag):
-            h_w = tile("h_w%d" % h, [P, HALF], U32, tag=tag)
-            h_s = tile("h_s%d" % h, [P, HALF], U8)
+        def hidden_tiles(h):
+            act = tile("act%d" % h, [P, PACK, PACK, P], F32, tag="ws_raw0")
+            pairs = tile("h_planes%d" % h, [P, 2, HALF, 2], BF16)
+            return act, pairs
+
+        def quantise_hidden(name, woven, tag=None):
+            width = woven.shape[1]
+            h_w = tile("h_w" + name, [P, width], U32, tag=tag)
+            h_s = tile("h_s" + name, [P, width], U8)
             nc.vector.quantize_mx(out=h_w[:].bitcast(FP8X4), scales=h_s[:], in_=woven[:].rearrange("p c t -> p (c t)"))
             return h_w, h_s
 
-        def second_stage(h, t, hidden):
-            bank = PACK + ORDER.index(t)
-            acc = psum.tile([P, HALF], F32, name="y%d%d" % (h, t), tag="bank%d" % bank)
+        def second_stage(name, t, parts, y):
+            acc = psum.tile([P, y.shape[1]], F32, name=name, tag="bank%d" % (PACK + ORDER.index(t)))
             m_cols = slice(t * P, (t + 1) * P)
-            nc.tensor.matmul_mx(
-                out=acc[:],
-                lhsT=wd_w[:, m_cols].bitcast(FP8X4),
-                lhsT_scale=wd_s[:, m_cols],
-                rhs=hidden[0][:].bitcast(FP8X4),
-                rhs_scale=hidden[1][:],
-                start=True,
-                stop=True,
-            )
-            return acc
+            start = 0
+            for h_w, h_s in parts:
+                stop = start + h_w.shape[1]
+                nc.tensor.matmul_mx(
+                    out=acc[:, start:stop],
+                    lhsT=wd_w[:, m_cols].bitcast(FP8X4),
+                    lhsT_scale=wd_s[:, m_cols],
+                    rhs=h_w[:].bitcast(FP8X4),
+                    rhs_scale=h_s[:],
+                    start=True,
+                    stop=True,
+                )
+                start = stop
+            nc.scalar.copy(out=y, in_=acc[:])
 
         factors = {}
 
         def gather_gate(t, tag=None):
             factors[t] = tile("factor%d" % t, [P, J], F32, tag=tag)
-            nc.vector.tensor_tensor(factors[t][:], gates[t][:].indirect(src_list[:]), wgo_t[:], MULT)
+            nc.vector.tensor_tensor(factors[t][:], gates[t][:].indirect(src_list[:]), wgo_t[:].rearrange("c p i -> c (p i)"), MULT)
 
         out_rows = out_0.rearrange("(p t) c -> t p c", t=PACK)
         out_bf = [tile("out_bf%d" % c, [P, SIDE, PACK], BF16) for c in range(2)]
-        twins = [tile("twins%d" % c, [P, 2, SIDE, 2], BF16, tag=tag) for c, tag in enumerate(("ws_raw0", "pairs0"))]
+        twins = [tile("twins%d" % c, [P, 2, SIDE, 2], BF16, tag=tag) for c, tag in enumerate(("act", "pairs0"))]
         starts = [sum(OUT_CHUNKS[:i]) for i in range(len(OUT_CHUNKS) + 1)]
         chunks = [slice(starts[i], starts[i + 1]) for i in range(len(OUT_CHUNKS))]
 
@@ -237,21 +248,20 @@ def tile_list_msg_gelu_gateP_kernel(tc, tab_words, tab_scales, ws, wt_words, wt_
             side, start = divmod(cols.start, SIDE)
             return out_bf[side][:, start : start + cols.stop - cols.start, :]
 
-        def copy_out(name, accs, tag=None):
-            y = tile(name, [P, len(accs) * HALF], F32, tag=tag)
-            for i, acc in enumerate(accs):
-                nc.scalar.copy(out=y[:, i * HALF : (i + 1) * HALF], in_=acc[:])
+        def messages(name, t, parts, tag=None):
+            y = tile(name, [P, sum(h_w.shape[1] for h_w, h_s in parts)], F32, tag=tag)
+            second_stage(name + "_sum", t, parts, y[:])
             return y
 
-        def scatter(t, y, h=None):
-            offsets = dst_list[:] if h is None else dst_list[:, list_cols(h)]
-            factor = factors[t][:] if h is None else factors[t][:, h * HALF : (h + 1) * HALF]
-            nc.vector.tensor_tensor(pages[t][:].indirect(offsets), y[:], factor, MULT)
+        def scatter(t, y, start):
+            stop = start + y.shape[1]
+            offsets = dst_list[:, start // LIST_ROWS : stop // LIST_ROWS]
+            nc.vector.tensor_tensor(pages[t][:].indirect(offsets), y[:], factors[t][:, start:stop], MULT)
 
-        def weave_twins(c, part):
-            nc.scalar.copy(
-                out=out_bf[c][:, part, :].bitcast(U32),
-                in_=twins[c][:, :, part, :].bitcast(U32).rearrange("p u c o -> p c (u o)"),
+        def weave_twins(c, part, copy, words):
+            copy(
+                out=out_bf[c][:, part, :].bitcast(words),
+                in_=twins[c][:, :, part, :].bitcast(words).rearrange("p u c o -> p c (u o)"),
             )
 
         def finish_page(t):
@@ -263,58 +273,74 @@ def tile_list_msg_gelu_gateP_kernel(tc, tab_words, tab_scales, ws, wt_words, wt_
                 else:
                     nc.scalar.copy(out=twins[c][:, t // 2, :, t % 2], in_=source)
                 if (t, c) == (third, 0):
-                    weave_twins(0, slice(0, SIDE))
+                    weave_twins(0, slice(0, SIDE), nc.scalar.copy, U32)
 
-        clear_page(first, nc.gpsimd, "wd_bf")
-        planes0 = turn_and_smooth(0, first_stage(0))
-        woven0 = weave(0, planes0, nc.scalar.copy)
+        for i, t in enumerate((first, second)):
+            clear_page(t, placed.tile([P, T], F32, name="page%d" % t, align_bytes=64, offset=4 * T * i))
+        act0, h_pairs0 = hidden_tiles(0)
+        woven0 = [tile("h_bf0%d" % g, [P, GROUP, PACK], BF16) for g in range(2)]
+        sums_and_gelu(0, 0, act0)
+        turn_and_smooth(0, 0, act0, h_pairs0)
+        weave(0, h_pairs0, woven0[0][:])
+        sums_and_gelu(0, 1, act0)
+        turn_and_smooth(0, 1, act0, h_pairs0)
+        weave(1, h_pairs0, woven0[1][:])
         gather_gate(first)
-        load_gate(last, "packed")
+        load_gate(last, "pairs0")
         gather_gate(second)
-        clear_page(second, nc.gpsimd, "ws_raw1")
         gather_gate(third)
-        hidden0 = quantise_hidden(0, woven0, "ws_bf")
-        gather_gate(last, "h_bf0")
-        act1 = first_stage(1)
-        y_first0 = copy_out("y_first0", [second_stage(0, first, hidden0)])
-        y_second0 = copy_out("y_second0", [second_stage(0, second, hidden0)])
-        scatter(first, y_first0, 0)
-        clear_page(third, nc.gpsimd, "y_first0")
-        scatter(second, y_second0, 0)
-        planes1 = turn_and_smooth(1, act1)
-        woven1 = weave(1, planes1, nc.scalar.copy)
-        hidden1 = quantise_hidden(1, woven1, None)
-        y_third0 = copy_out("y_third0", [second_stage(0, third, hidden0)], "h_planes1")
-        scatter(third, y_third0, 0)
-        later = {t: copy_out("y_later%d" % t, [second_stage(1, t, hidden1)]) for t in (first, second, third)}
-        y_last = tile("y_last", [P, J], F32, tag="act")
+        hidden0 = [quantise_hidden("00", woven0[0], "ws_bf")]
+        gather_gate(last, "h_bf00")
+        hidden0.append(quantise_hidden("01", woven0[1], "pairs0"))
+        act1, h_pairs1 = hidden_tiles(1)
+        woven1 = tile("h_bf1", [P, HALF, PACK], BF16)
+        for g in range(2):
+            sums_and_gelu(1, g, act1)
+        for g in range(2):
+            early = {t: messages("y_early%d%d" % (g, t), t, hidden0[g : g + 1]) for t in (first, second)}
+            for t in (first, second):
+                scatter(t, early[t], g * GROUP)
+        clear_page(third, tile("page%d" % third, [P, T], F32, tag="y_early0%d" % first))
+        for g in range(2):
+            turn_and_smooth(1, g, act1, h_pairs1)
+        for g in range(2):
+            weave(g, h_pairs1, woven1[:, g * GROUP : (g + 1) * GROUP, :])
+        hidden1 = [quantise_hidden("1", woven1)]
+        scatter(third, messages("y_third0", third, hidden0, "h_planes1"), 0)
+        later = {t: messages("y_later%d" % t, t, hidden1) for t in (first, second, third)}
+        y_last = tile("y_last", [P, J], F32, tag="ws_raw0")
         for h, hidden in enumerate((hidden0, hidden1)):
-            nc.scalar.copy(out=y_last[:, h * HALF : (h + 1) * HALF], in_=second_stage(h, last, hidden)[:])
+            second_stage("y_last_sum%d" % h, last, hidden, y_last[:, h * HALF : (h + 1) * HALF])
         for t in (first, second, third):
-            scatter(t, later[t], 1)
+            scatter(t, later[t], HALF)
             finish_page(t)
         pages[last] = pages[first]
-        scatter(last, y_last)
+        scatter(last, y_last, 0)
         finish_page(last)
-        for cols in chunks[VECTOR_CHUNKS:]:
-            part = slice(cols.start - SIDE, cols.stop - SIDE)
+        upper = [slice(cols.start - SIDE, cols.stop - SIDE) for cols in chunks[VECTOR_CHUNKS:]]
+        for cols, part in zip(chunks[VECTOR_CHUNKS:], upper):
             nc.scalar.copy(out=twins[1][:, last // 2, part, last % 2], in_=pages[last][:, cols])
-            weave_twins(1, part)
+        for part in upper[1:]:
+            weave_twins(1, part, nc.scalar.copy, U32)
 
         out_w = tile("out_w", [P, T], U32)
         out_s = tile("out_s", [P, T], U8)
         code_rows = out_1[0].rearrange("p t i -> p (t i)").bitcast(I32)
-        for i in range(len(chunks) + 1):
-            if i < VECTOR_CHUNKS:
-                nc.vector.tensor_copy(woven_out(chunks[i])[:, :, last], pages[last][:, chunks[i]])
-            if i > 0:
-                cols = chunks[i - 1]
-                nc.vector.quantize_mx(
-                    out=out_w[:, cols].bitcast(FP8X4),
-                    scales=out_s[:, cols],
-                    in_=woven_out(cols).rearrange("p c t -> p (c t)"),
-                )
-                nc.sync.dma_start(out=code_rows[:, cols], in_=out_w[:, cols].bitcast(I32))
+
+        def quantise_out(cols):
+            nc.vector.quantize_mx(
+                out=out_w[:, cols].bitcast(FP8X4),
+                scales=out_s[:, cols],
+                in_=woven_out(cols).rearrange("p c t -> p (c t)"),
+            )
+            nc.sync.dma_start(out=code_rows[:, cols], in_=out_w[:, cols].bitcast(I32))
+
+        for cols in chunks[:VECTOR_CHUNKS]:
+            nc.vector.tensor_copy(woven_out(cols)[:, :, last], pages[last][:, cols])
+        quantise_out(chunks[0])
+        weave_twins(1, upper[0], nc.vector.tensor_copy, I32)
+        for cols in chunks[1:]:
+            quantise_out(cols)
         for q in range(QUADS):
             queue = nc.scalar if q % 2 else nc.sync
             queue.dma_start(out=out_2[0, 4 * q : 4 * q + 4, :].bitcast(I32), in_=out_s[32 * q : 32 * q + 4, :].bitcast(I32))

@@ -62,14 +62,13 @@ def tile_list_msg_gelu_gateP_kernel(tc, tab_words, tab_scales, ws, wt_words, wt_
         identity = tile("identity", [P, P], F32)
         make_identity(nc, identity[:])
 
-        def load_ws(a):
-            raw = tile("ws_raw%d" % a, [P, PACK, R], F32)
+        def load_ws(a, raw):
             nc.sync.dma_start(out=raw[:], in_=ws[512 * a : 512 * (a + 1), :].rearrange("(p j) r -> p j r", j=PACK))
             return raw
 
         wgo_runs = tile("wgo_runs", [P, RUN], F32)
         nc.sync.dma_start(out=wgo_runs[:], in_=wgo[0].rearrange("(p i) -> p i", i=RUN))
-        ws_raw = [load_ws(0)]
+        ws_raw = [load_ws(0, tile("ws_raw0", [P, PACK, R], F32))]
         tab_w = tile("tab_w", [P, T], I32)
         nc.sync.dma_start(out=tab_w[:], in_=tab_words[0].rearrange("p t i -> p (t i)").bitcast(I32))
         sm_t = tile("sm_t", [P, PACK], F32)
@@ -79,7 +78,7 @@ def tile_list_msg_gelu_gateP_kernel(tc, tab_words, tab_scales, ws, wt_words, wt_
                 out=wt_s[32 * q : 32 * q + 4, :, :].bitcast(I32),
                 in_=wt_scales[:, 4 * q : 4 * q + 4, :].bitcast(I32).rearrange("a q r -> q a r"),
             )
-        ws_raw.append(load_ws(1))
+        ws_raw.append(load_ws(1, placed.tile([P, PACK, R], F32, name="ws_raw1", align_bytes=64, offset=8 * T)))
 
         wgo_t = tile("wgo_t", [P, P, RUN], F32)
         for b in range(RUN // PACK):
@@ -89,7 +88,7 @@ def tile_list_msg_gelu_gateP_kernel(tc, tab_words, tab_scales, ws, wt_words, wt_
                 nc.tensor.transpose(spread[:, i, :], column.to_broadcast([P, P]), identity[:])
             nc.scalar.copy(out=wgo_t[:, :, PACK * b : PACK * (b + 1)], in_=spread[:].rearrange("c i p -> c p i"))
 
-        moved = tile("moved", [P, 2, 2 * J], U8)
+        moved = tile("moved", [P, 2, J], U8)
         nc.vector.memset(moved[:].rearrange("p a c -> p (a c)").bitcast(I32), 0)
         pages = {}
 
@@ -103,49 +102,57 @@ def tile_list_msg_gelu_gateP_kernel(tc, tab_words, tab_scales, ws, wt_words, wt_
         def gather_words(u, h, pairs):
             nc.vector.tensor_copy(pairs, tab_w[:].bitcast(U32).indirect(lists[u][:, list_cols(h)]))
 
-        def part_words(u, h, pairs):
-            parted = tile("v_w%d%d" % (u, h), [P, 2, 2 * HALF], U8)
+        def part_words(pairs, parted):
             nc.vector.tensor_copy(parted[:].bitcast(U16), pairs.bitcast(U16).rearrange("p (n d) -> p d n", d=2))
             return parted
 
-        packed = tile("packed", [P, 2 * J], U8)
-        for u in range(2):
-            nc.vector.tensor_copy(packed[:, u * J : (u + 1) * J], tab_s[:].indirect(lists[u][:]))
-        for q in range(QUADS):
-            nc.sync.dma_start(
-                out=moved[32 * q : 32 * q + 4, :, :].bitcast(I32),
-                in_=packed[96 + 8 * q : 104 + 8 * q, :].bitcast(I32),
-            )
+        packed = [tile("packed%d" % h, [P, J], U8) for h in range(2)]
+        for h in range(2):
+            for u in range(2):
+                nc.vector.tensor_copy(packed[h][:, u * HALF : (u + 1) * HALF], tab_s[:].indirect(lists[u][:, list_cols(h)]))
+
+        def move_scales(h):
+            for q in range(QUADS):
+                nc.sync.dma_start(
+                    out=moved[32 * q : 32 * q + 4, :, :].bitcast(I32),
+                    in_=packed[h][96 + 8 * q : 104 + 8 * q, :].bitcast(I32),
+                )
+
+        move_scales(0)
         wt_w = tile("wt_w", [P, 2, R], I32, tag="act")
         nc.sync.dma_start(out=wt_w[:], in_=wt_words.rearrange("a p r i -> p a (r i)").bitcast(I32))
-        v_s = [[moved[:, a, u * J : (u + 1) * J] for a in range(2)] for u in range(2)]
+        v_s = [[moved[:, a, u * HALF : (u + 1) * HALF] for a in range(2)] for u in range(2)]
 
         v_w = {}
         pairs0 = tile("pairs0", [P, 2, HALF], U32)
         for u in (1, 0):
             gather_words(u, 0, pairs0[:, u, :])
         for u in (1, 0):
-            v_w[u, 0] = part_words(u, 0, pairs0[:, u, :])
+            v_w[u, 0] = part_words(pairs0[:, u, :], tile("v_w%d0" % u, [P, 2, 2 * HALF], U8))
 
         ws_w = tile("ws_w", [P, 2, R], U32)
         ws_s = tile("ws_s", [P, 2, R], U8)
-        ws_bf = tile("ws_bf", [P, 2, PACK * R], BF16)
+        ws_bf = [tile("ws_bf%d" % a, [P, PACK * R], BF16) for a in range(2)]
         for a in range(2):
             nc.scalar.copy(
-                out=ws_bf[:, a, :].rearrange("p (c i j) -> p c j i", i=4, j=PACK),
+                out=ws_bf[a][:].rearrange("p (c i j) -> p c j i", i=4, j=PACK),
                 in_=ws_raw[a][:].rearrange("p j (c i) -> p c j i", i=4),
             )
         wd_raw = tile("wd_raw", [P, 2, PACK, N // 2], F32, tag="ws_raw0")
         for b in range(2):
             nc.sync.dma_start(out=wd_raw[:, b, :, :], in_=wd[:, b * N // 2 : (b + 1) * N // 2].rearrange("(p j) n -> p j n", j=PACK))
-        for a in range(2):
-            nc.vector.quantize_mx(out=ws_w[:, a, :].bitcast(FP8X4), scales=ws_s[:, a, :], in_=ws_bf[:, a, :])
 
-        pairs1 = tile("pairs1", [P, 2, HALF], U32, tag="ws_bf")
-        for u in (1, 0):
-            gather_words(u, 1, pairs1[:, u, :])
-        for u in (1, 0):
-            v_w[u, 1] = part_words(u, 1, pairs1[:, u, :])
+        def quantise_ws(a):
+            nc.vector.quantize_mx(out=ws_w[:, a, :].bitcast(FP8X4), scales=ws_s[:, a, :], in_=ws_bf[a][:])
+
+        quantise_ws(0)
+        dst_pairs1 = tile("dst_pairs1", [P, HALF], U32)
+        gather_words(1, 1, dst_pairs1[:])
+        quantise_ws(1)
+        src_pairs1 = placed.tile([P, HALF], U32, name="src_pairs1", align_bytes=64, offset=8 * T)
+        gather_words(0, 1, src_pairs1[:])
+        v_w[1, 1] = part_words(dst_pairs1[:], placed.tile([P, 2, 2 * HALF], U8, name="v_w11", align_bytes=64, offset=8 * T + 4 * HALF))
+        v_w[0, 1] = part_words(src_pairs1[:], tile("v_w01", [P, 2, 2 * HALF], U8))
 
         wd_bf = placed.tile([P, PACK * N], BF16, name="wd_bf", align_bytes=64, offset=4 * T - PACK * N)
         for b in range(2):
@@ -160,12 +167,13 @@ def tile_list_msg_gelu_gateP_kernel(tc, tab_words, tab_scales, ws, wt_words, wt_
         gates = {}
         g_rows = gT.rearrange("(p t) c -> t p c", t=PACK)
 
-        def load_gate(t, tag):
-            gates[t] = tile("gate%d" % t, [P, T], F32, tag=tag)
-            nc.sync.dma_start(out=gates[t][:], in_=g_rows[t])
+        def load_gate(t, gate):
+            gates[t] = gate
+            nc.sync.dma_start(out=gate[:], in_=g_rows[t])
 
-        for t, tag in zip(ORDER[:3], ("pairs0", "ws_raw1", "ws_bf")):
-            load_gate(t, tag)
+        load_gate(first, tile("gate_first", [P, T], F32, tag="pairs0"))
+        load_gate(second, placed.tile([P, T], F32, name="gate_second", align_bytes=64, offset=8 * T + 8 * HALF))
+        load_gate(third, tile("gate_third", [P, T], F32, tag="dst_pairs1"))
 
         def sums_and_gelu(h, g, act):
             blocks = (2 * g, 2 * g + 1)
@@ -176,7 +184,7 @@ def tile_list_msg_gelu_gateP_kernel(tc, tab_words, tab_scales, ws, wt_words, wt_
                         nc.tensor.matmul_mx(
                             out=accs[i][:],
                             lhsT=v_w[u, h][:, a, 2 * i * P : 2 * (i + 1) * P].bitcast(FP4X4),
-                            lhsT_scale=v_s[u][a][:, h * HALF + i * P : h * HALF + (i + 1) * P],
+                            lhsT_scale=v_s[u][a][:, i * P : (i + 1) * P],
                             rhs=w_w[:, a, :].bitcast(FP8X4),
                             rhs_scale=w_s[:, a, :],
                             start=(u, a) == (1, 0),
@@ -186,7 +194,6 @@ def tile_list_msg_gelu_gateP_kernel(tc, tab_words, tab_scales, ws, wt_words, wt_
                 nc.scalar.activation(out=act[:, i, :, :], in_=accs[i][:].rearrange("p (m t) -> p t m", t=PACK), func=GELU)
 
         def turn_and_smooth(h, g, act, pairs):
-            cols = slice(2 * g * P, 2 * (g + 1) * P)
             for u in range(2):
                 turned = psum.tile([P, 2, 2, P], F32, name="t%d%d%d" % (h, g, u), tag="bank%d" % (PACK * (1 - h) + 2 * g + u))
                 for o in range(2):
@@ -195,16 +202,15 @@ def tile_list_msg_gelu_gateP_kernel(tc, tab_words, tab_scales, ws, wt_words, wt_
                 for o in range(2):
                     t = 2 * u + o
                     nc.scalar.activation(
-                        out=pairs[:, u, cols, o], in_=turned[:, o, :, :].rearrange("p i m -> p (i m)"), func=COPY, scale=sm_t[:, t : t + 1]
+                        out=pairs[g][:, u, :, o], in_=turned[:, o, :, :].rearrange("p i m -> p (i m)"), func=COPY, scale=sm_t[:, t : t + 1]
                     )
 
         def weave(g, pairs, woven):
-            cols = slice(g * GROUP, (g + 1) * GROUP)
-            nc.scalar.copy(out=woven.bitcast(U32), in_=pairs[:, :, cols, :].bitcast(U32).rearrange("p u c o -> p c (u o)"))
+            nc.scalar.copy(out=woven.bitcast(U32), in_=pairs[g][:].bitcast(U32).rearrange("p u c o -> p c (u o)"))
 
         def hidden_tiles(h):
             act = tile("act%d" % h, [P, PACK, PACK, P], F32, tag="ws_raw0")
-            pairs = tile("h_planes%d" % h, [P, 2, HALF, 2], BF16)
+            pairs = [tile("h_pairs%d%d" % (h, g), [P, 2, GROUP, 2], BF16) for g in range(2)]
             return act, pairs
 
         def quantise_hidden(name, woven, tag=None):
@@ -240,7 +246,7 @@ def tile_list_msg_gelu_gateP_kernel(tc, tab_words, tab_scales, ws, wt_words, wt_
 
         out_rows = out_0.rearrange("(p t) c -> t p c", t=PACK)
         out_bf = [tile("out_bf%d" % c, [P, SIDE, PACK], BF16) for c in range(2)]
-        twins = [tile("twins%d" % c, [P, 2, SIDE, 2], BF16, tag=tag) for c, tag in enumerate(("act", "pairs0"))]
+        twins = [tile("twins%d" % c, [P, 2, SIDE, 2], BF16, tag=tag) for c, tag in enumerate(("y_early0%d" % second, "pairs0"))]
         starts = [sum(OUT_CHUNKS[:i]) for i in range(len(OUT_CHUNKS) + 1)]
         chunks = [slice(starts[i], starts[i + 1]) for i in range(len(OUT_CHUNKS))]
 
@@ -268,10 +274,7 @@ def tile_list_msg_gelu_gateP_kernel(tc, tab_words, tab_scales, ws, wt_words, wt_
             nc.sync.dma_start(out=out_rows[t], in_=pages[t][:])
             for c in range(2 if t != last else 0):
                 source = pages[t][:, c * SIDE : (c + 1) * SIDE]
-                if (t, c) == (first, 0):
-                    nc.scalar.copy(out=twins[c][:, 1, :, :], in_=source.unsqueeze(2).to_broadcast([P, SIDE, 2]))
-                else:
-                    nc.scalar.copy(out=twins[c][:, t // 2, :, t % 2], in_=source)
+                nc.scalar.copy(out=twins[c][:, t // 2, :, t % 2], in_=source)
                 if (t, c) == (third, 0):
                     weave_twins(0, slice(0, SIDE), nc.scalar.copy, U32)
 
@@ -283,14 +286,15 @@ def tile_list_msg_gelu_gateP_kernel(tc, tab_words, tab_scales, ws, wt_words, wt_
         turn_and_smooth(0, 0, act0, h_pairs0)
         weave(0, h_pairs0, woven0[0][:])
         sums_and_gelu(0, 1, act0)
+        move_scales(1)
         turn_and_smooth(0, 1, act0, h_pairs0)
         weave(1, h_pairs0, woven0[1][:])
         gather_gate(first)
-        load_gate(last, "pairs0")
+        load_gate(last, tile("gate_last", [P, T], F32, tag="pairs0"))
         gather_gate(second)
         gather_gate(third)
-        hidden0 = [quantise_hidden("00", woven0[0], "ws_bf")]
-        gather_gate(last, "h_bf00")
+        hidden0 = [quantise_hidden("00", woven0[0], "packed1")]
+        gather_gate(last, "h_pairs00")
         hidden0.append(quantise_hidden("01", woven0[1], "pairs0"))
         act1, h_pairs1 = hidden_tiles(1)
         woven1 = tile("h_bf1", [P, HALF, PACK], BF16)
@@ -301,12 +305,13 @@ def tile_list_msg_gelu_gateP_kernel(tc, tab_words, tab_scales, ws, wt_words, wt_
             for t in (first, second):
                 scatter(t, early[t], g * GROUP)
         clear_page(third, tile("page%d" % third, [P, T], F32, tag="y_early0%d" % first))
+        nc.gpsimd.memset(twins[0][:, last // 2, :, :].rearrange("p c o -> p (c o)").bitcast(I32), 0)
         for g in range(2):
             turn_and_smooth(1, g, act1, h_pairs1)
         for g in range(2):
             weave(g, h_pairs1, woven1[:, g * GROUP : (g + 1) * GROUP, :])
         hidden1 = [quantise_hidden("1", woven1)]
-        scatter(third, messages("y_third0", third, hidden0, "h_planes1"), 0)
+        scatter(third, messages("y_third0", third, hidden0, "h_pairs11"), 0)
         later = {t: messages("y_later%d" % t, t, hidden1) for t in (first, second, third)}
         y_last = tile("y_last", [P, J], F32, tag="ws_raw0")
         for h, hidden in enumerate((hidden0, hidden1)):

@@ -88,8 +88,8 @@ def tile_list_msg_gelu_gateP_kernel(tc, tab_words, tab_scales, ws, wt_words, wt_
                 nc.tensor.transpose(spread[:, i, :], column.to_broadcast([P, P]), identity[:])
             nc.scalar.copy(out=wgo_t[:, :, PACK * b : PACK * (b + 1)], in_=spread[:].rearrange("c i p -> c p i"))
 
-        moved = tile("moved", [P, 2, J], U8)
-        nc.vector.memset(moved[:].rearrange("p a c -> p (a c)").bitcast(I32), 0)
+        moved = [tile("moved0", [P, 2, J], U8)]
+        nc.vector.memset(moved[0][:].rearrange("p a c -> p (a c)").bitcast(I32), 0)
         pages = {}
 
         def clear_page(t, page):
@@ -114,14 +114,13 @@ def tile_list_msg_gelu_gateP_kernel(tc, tab_words, tab_scales, ws, wt_words, wt_
         def move_scales(h):
             for q in range(QUADS):
                 nc.sync.dma_start(
-                    out=moved[32 * q : 32 * q + 4, :, :].bitcast(I32),
+                    out=moved[h][32 * q : 32 * q + 4, :, :].bitcast(I32),
                     in_=packed[h][96 + 8 * q : 104 + 8 * q, :].bitcast(I32),
                 )
 
         move_scales(0)
         wt_w = tile("wt_w", [P, 2, R], I32, tag="act")
         nc.sync.dma_start(out=wt_w[:], in_=wt_words.rearrange("a p r i -> p a (r i)").bitcast(I32))
-        v_s = [[moved[:, a, u * HALF : (u + 1) * HALF] for a in range(2)] for u in range(2)]
 
         v_w = {}
         pairs0 = tile("pairs0", [P, 2, HALF], U32)
@@ -149,6 +148,8 @@ def tile_list_msg_gelu_gateP_kernel(tc, tab_words, tab_scales, ws, wt_words, wt_
         dst_pairs1 = tile("dst_pairs1", [P, HALF], U32)
         gather_words(1, 1, dst_pairs1[:])
         quantise_ws(1)
+        moved.append(tile("moved1", [P, 2, J], U8, tag="ws_bf1"))
+        nc.gpsimd.memset(moved[1][:].rearrange("p a c -> p (a c)").bitcast(I32), 0)
         src_pairs1 = placed.tile([P, HALF], U32, name="src_pairs1", align_bytes=64, offset=8 * T)
         gather_words(0, 1, src_pairs1[:])
         v_w[1, 1] = part_words(dst_pairs1[:], placed.tile([P, 2, 2 * HALF], U8, name="v_w11", align_bytes=64, offset=8 * T + 4 * HALF))
@@ -173,6 +174,7 @@ def tile_list_msg_gelu_gateP_kernel(tc, tab_words, tab_scales, ws, wt_words, wt_
 
         load_gate(first, tile("gate_first", [P, T], F32, tag="pairs0"))
         load_gate(second, placed.tile([P, T], F32, name="gate_second", align_bytes=64, offset=8 * T + 8 * HALF))
+        move_scales(1)
         load_gate(third, tile("gate_third", [P, T], F32, tag="dst_pairs1"))
 
         def sums_and_gelu(h, g, act):
@@ -184,7 +186,7 @@ def tile_list_msg_gelu_gateP_kernel(tc, tab_words, tab_scales, ws, wt_words, wt_
                         nc.tensor.matmul_mx(
                             out=accs[i][:],
                             lhsT=v_w[u, h][:, a, 2 * i * P : 2 * (i + 1) * P].bitcast(FP4X4),
-                            lhsT_scale=v_s[u][a][:, i * P : (i + 1) * P],
+                            lhsT_scale=moved[h][:, a, u * HALF + i * P : u * HALF + (i + 1) * P],
                             rhs=w_w[:, a, :].bitcast(FP8X4),
                             rhs_scale=w_s[:, a, :],
                             start=(u, a) == (1, 0),
@@ -286,14 +288,13 @@ def tile_list_msg_gelu_gateP_kernel(tc, tab_words, tab_scales, ws, wt_words, wt_
         turn_and_smooth(0, 0, act0, h_pairs0)
         weave(0, h_pairs0, woven0[0][:])
         sums_and_gelu(0, 1, act0)
-        move_scales(1)
         turn_and_smooth(0, 1, act0, h_pairs0)
         weave(1, h_pairs0, woven0[1][:])
         gather_gate(first)
         load_gate(last, tile("gate_last", [P, T], F32, tag="pairs0"))
         gather_gate(second)
         gather_gate(third)
-        hidden0 = [quantise_hidden("00", woven0[0], "packed1")]
+        hidden0 = [quantise_hidden("00", woven0[0], "dst_pairs1")]
         gather_gate(last, "h_pairs00")
         hidden0.append(quantise_hidden("01", woven0[1], "pairs0"))
         act1, h_pairs1 = hidden_tiles(1)

@@ -24,11 +24,12 @@ QUADS = 4
 HALF = 512
 GROUP = HALF // 2
 LIST_ROWS = 16
-OUT_CHUNKS = (512, 512, 256, 512, 256)
+OUT_CHUNKS = (512, 512, 512, 256, 256)
 VECTOR_CHUNKS = 2
 SIDE = T // 2
 RUN = J // P
 ORDER = (2, 0, 1, 3)
+TURN_BANKS = (4, 6, 6, 0)
 
 
 def tile_list_msg_gelu_gateP_kernel(tc, tab_words, tab_scales, ws, wt_words, wt_scales, sm, wd, gT, wgo, offs, offs2, out_0, out_1, out_2):
@@ -179,7 +180,7 @@ def tile_list_msg_gelu_gateP_kernel(tc, tab_words, tab_scales, ws, wt_words, wt_
 
         def sums_and_gelu(h, g, act):
             blocks = (2 * g, 2 * g + 1)
-            accs = {i: psum.tile([P, R], F32, name="a%d%d" % (h, i), tag="bank%d" % (PACK * h + i)) for i in blocks}
+            accs = {i: psum.tile([P, R], F32, name="a%d%d" % (h, i), tag="bank%d" % i) for i in blocks}
             for u, (w_w, w_s) in ((1, (wt_w, wt_s)), (0, (ws_w, ws_s))):
                 for i in blocks:
                     for a in range(2):
@@ -197,7 +198,7 @@ def tile_list_msg_gelu_gateP_kernel(tc, tab_words, tab_scales, ws, wt_words, wt_
 
         def turn_and_smooth(h, g, act, pairs):
             for u in range(2):
-                turned = psum.tile([P, 2, 2, P], F32, name="t%d%d%d" % (h, g, u), tag="bank%d" % (PACK * (1 - h) + 2 * g + u))
+                turned = psum.tile([P, 2, 2, P], F32, name="t%d%d%d" % (h, g, u), tag="bank%d" % (TURN_BANKS[2 * h + g] + u))
                 for o in range(2):
                     for i in range(2):
                         nc.tensor.transpose(turned[:, o, i, :], act[:, 2 * g + i, 2 * u + o, :], identity[:])
@@ -222,8 +223,8 @@ def tile_list_msg_gelu_gateP_kernel(tc, tab_words, tab_scales, ws, wt_words, wt_
             nc.vector.quantize_mx(out=h_w[:].bitcast(FP8X4), scales=h_s[:], in_=woven[:].rearrange("p c t -> p (c t)"))
             return h_w, h_s
 
-        def second_stage(name, t, parts, y):
-            acc = psum.tile([P, y.shape[1]], F32, name=name, tag="bank%d" % (PACK + ORDER.index(t)))
+        def second_stage(name, t, parts, y, bank):
+            acc = psum.tile([P, y.shape[1]], F32, name=name, tag="bank%d" % bank)
             m_cols = slice(t * P, (t + 1) * P)
             start = 0
             for h_w, h_s in parts:
@@ -256,9 +257,9 @@ def tile_list_msg_gelu_gateP_kernel(tc, tab_words, tab_scales, ws, wt_words, wt_
             side, start = divmod(cols.start, SIDE)
             return out_bf[side][:, start : start + cols.stop - cols.start, :]
 
-        def messages(name, t, parts, tag=None):
+        def messages(name, t, parts, bank, tag=None):
             y = tile(name, [P, sum(h_w.shape[1] for h_w, h_s in parts)], F32, tag=tag)
-            second_stage(name + "_sum", t, parts, y[:])
+            second_stage(name + "_sum", t, parts, y[:], bank)
             return y
 
         def scatter(t, y, start):
@@ -301,22 +302,26 @@ def tile_list_msg_gelu_gateP_kernel(tc, tab_words, tab_scales, ws, wt_words, wt_
         woven1 = tile("h_bf1", [P, HALF, PACK], BF16)
         for g in range(2):
             sums_and_gelu(1, g, act1)
-        for g in range(2):
-            early = {t: messages("y_early%d%d" % (g, t), t, hidden0[g : g + 1]) for t in (first, second)}
+
+        def early_messages(g):
+            early = {t: messages("y_early%d%d" % (g, t), t, hidden0[g : g + 1], 4 + 2 * g + i) for i, t in enumerate((first, second))}
             for t in (first, second):
                 scatter(t, early[t], g * GROUP)
+
+        early_messages(0)
         clear_page(third, tile("page%d" % third, [P, T], F32, tag="y_early0%d" % first))
         nc.gpsimd.memset(twins[0][:, last // 2, :, :].rearrange("p c o -> p (c o)").bitcast(I32), 0)
-        for g in range(2):
-            turn_and_smooth(1, g, act1, h_pairs1)
+        turn_and_smooth(1, 0, act1, h_pairs1)
+        early_messages(1)
+        turn_and_smooth(1, 1, act1, h_pairs1)
         for g in range(2):
             weave(g, h_pairs1, woven1[:, g * GROUP : (g + 1) * GROUP, :])
         hidden1 = [quantise_hidden("1", woven1)]
-        scatter(third, messages("y_third0", third, hidden0, "h_pairs11"), 0)
-        later = {t: messages("y_later%d" % t, t, hidden1) for t in (first, second, third)}
+        scatter(third, messages("y_third0", third, hidden0, 0, "h_pairs11"), 0)
+        later = {t: messages("y_later%d" % t, t, hidden1, 2 + i) for i, t in enumerate((first, second, third))}
         y_last = tile("y_last", [P, J], F32, tag="ws_raw0")
         for h, hidden in enumerate((hidden0, hidden1)):
-            second_stage("y_last_sum%d" % h, last, hidden, y_last[:, h * HALF : (h + 1) * HALF])
+            second_stage("y_last_sum%d" % h, last, hidden, y_last[:, h * HALF : (h + 1) * HALF], 1 + PACK * h)
         for t in (first, second, third):
             scatter(t, later[t], HALF)
             finish_page(t)
@@ -324,29 +329,38 @@ def tile_list_msg_gelu_gateP_kernel(tc, tab_words, tab_scales, ws, wt_words, wt_
         scatter(last, y_last, 0)
         finish_page(last)
         upper = [slice(cols.start - SIDE, cols.stop - SIDE) for cols in chunks[VECTOR_CHUNKS:]]
-        for cols, part in zip(chunks[VECTOR_CHUNKS:], upper):
-            nc.scalar.copy(out=twins[1][:, last // 2, part, last % 2], in_=pages[last][:, cols])
-        for part in upper[1:]:
-            weave_twins(1, part, nc.scalar.copy, U32)
+
+        def round_upper(i):
+            nc.scalar.copy(out=twins[1][:, last // 2, upper[i], last % 2], in_=pages[last][:, chunks[VECTOR_CHUNKS + i]])
+
+        round_upper(0)
+        for i in range(len(upper)):
+            if i + 1 < len(upper):
+                round_upper(i + 1)
+            weave_twins(1, upper[i], nc.scalar.copy, U32)
 
         out_w = tile("out_w", [P, T], U32)
-        out_s = tile("out_s", [P, T], U8)
+        out_s = tile("out_s", [P, HALF], U8)
         code_rows = out_1[0].rearrange("p t i -> p (t i)").bitcast(I32)
 
         def quantise_out(cols):
-            nc.vector.quantize_mx(
-                out=out_w[:, cols].bitcast(FP8X4),
-                scales=out_s[:, cols],
-                in_=woven_out(cols).rearrange("p c t -> p (c t)"),
-            )
+            for start in range(cols.start, cols.stop, GROUP):
+                piece = slice(start, start + GROUP)
+                plane, place = divmod(start, HALF)
+                nc.vector.quantize_mx(
+                    out=out_w[:, piece].bitcast(FP8X4),
+                    scales=out_s[4 * plane : P, place : place + GROUP],
+                    in_=woven_out(piece).rearrange("p c t -> p (c t)"),
+                )
             nc.sync.dma_start(out=code_rows[:, cols], in_=out_w[:, cols].bitcast(I32))
 
         for cols in chunks[:VECTOR_CHUNKS]:
             nc.vector.tensor_copy(woven_out(cols)[:, :, last], pages[last][:, cols])
-        quantise_out(chunks[0])
-        weave_twins(1, upper[0], nc.vector.tensor_copy, I32)
-        for cols in chunks[1:]:
+        for cols in chunks:
             quantise_out(cols)
         for q in range(QUADS):
             queue = nc.scalar if q % 2 else nc.sync
-            queue.dma_start(out=out_2[0, 4 * q : 4 * q + 4, :].bitcast(I32), in_=out_s[32 * q : 32 * q + 4, :].bitcast(I32))
+            queue.dma_start(
+                out=out_2[0, 4 * q : 4 * q + 4, :].bitcast(I32).rearrange("r (a c) -> a r c", a=T // HALF),
+                in_=out_s[32 * q : 32 * q + 16, :].bitcast(I32),
+            )

@@ -173,10 +173,10 @@ def tile_list_msg_gelu_gateP_kernel(tc, tab_words, tab_scales, ws, wt_words, wt_
             gates[t] = gate
             nc.sync.dma_start(out=gate[:], in_=g_rows[t])
 
-        load_gate(first, tile("gate_first", [P, T], F32, tag="pairs0"))
-        load_gate(second, placed.tile([P, T], F32, name="gate_second", align_bytes=64, offset=8 * T + 8 * HALF))
+        load_gate(second, tile("gate_a", [P, T], F32, tag="pairs0"))
+        load_gate(third, placed.tile([P, T], F32, name="gate_b", align_bytes=64, offset=8 * T + 8 * HALF))
         move_scales(1)
-        load_gate(third, tile("gate_third", [P, T], F32, tag="dst_pairs1"))
+        load_gate(last, tile("gate_c", [P, T], F32, tag="dst_pairs1"))
 
         def sums_and_gelu(h, g, act):
             blocks = (2 * g, 2 * g + 1)
@@ -249,7 +249,7 @@ def tile_list_msg_gelu_gateP_kernel(tc, tab_words, tab_scales, ws, wt_words, wt_
 
         out_rows = out_0.rearrange("(p t) c -> t p c", t=PACK)
         out_bf = [tile("out_bf%d" % c, [P, SIDE, PACK], BF16) for c in range(2)]
-        twins = [tile("twins%d" % c, [P, 2, SIDE, 2], BF16, tag=tag) for c, tag in enumerate(("y_early0%d" % second, "pairs0"))]
+        twins = [tile("twins%d" % c, [P, 2, SIDE, 2], BF16, tag=tag) for c, tag in enumerate(("h_bf0", "pairs0"))]
         starts = [sum(OUT_CHUNKS[:i]) for i in range(len(OUT_CHUNKS) + 1)]
         chunks = [slice(starts[i], starts[i + 1]) for i in range(len(OUT_CHUNKS))]
 
@@ -284,36 +284,27 @@ def tile_list_msg_gelu_gateP_kernel(tc, tab_words, tab_scales, ws, wt_words, wt_
         for i, t in enumerate((first, second)):
             clear_page(t, placed.tile([P, T], F32, name="page%d" % t, align_bytes=64, offset=4 * T * i))
         act0, h_pairs0 = hidden_tiles(0)
-        woven0 = [tile("h_bf0%d" % g, [P, GROUP, PACK], BF16) for g in range(2)]
-        sums_and_gelu(0, 0, act0)
-        turn_and_smooth(0, 0, act0, h_pairs0)
-        weave(0, h_pairs0, woven0[0][:])
-        sums_and_gelu(0, 1, act0)
-        turn_and_smooth(0, 1, act0, h_pairs0)
-        weave(1, h_pairs0, woven0[1][:])
-        gather_gate(first)
-        load_gate(last, tile("gate_last", [P, T], F32, tag="pairs0"))
+        woven0 = tile("h_bf0", [P, HALF, PACK], BF16)
+        for g in range(2):
+            sums_and_gelu(0, g, act0)
+            turn_and_smooth(0, g, act0, h_pairs0)
+            weave(g, h_pairs0, woven0[:, g * GROUP : (g + 1) * GROUP, :])
         gather_gate(second)
+        load_gate(first, tile("gate_d", [P, T], F32, tag="pairs0"))
         gather_gate(third)
-        hidden0 = [quantise_hidden("00", woven0[0], "dst_pairs1")]
-        gather_gate(last, "h_pairs00")
-        hidden0.append(quantise_hidden("01", woven0[1], "pairs0"))
+        gather_gate(last)
+        hidden0 = [quantise_hidden("0", woven0, "dst_pairs1")]
+        gather_gate(first)
+        nc.gpsimd.memset(twins[0][:, last // 2, :, :].rearrange("p c o -> p (c o)").bitcast(I32), 0)
         act1, h_pairs1 = hidden_tiles(1)
         woven1 = tile("h_bf1", [P, HALF, PACK], BF16)
+        scatter(first, messages("y_first0", first, hidden0, 4), 0)
+        clear_page(third, tile("page%d" % third, [P, T], F32, tag="y_first0"))
+        scatter(second, messages("y_second0", second, hidden0, 5, "pairs0"), 0)
         for g in range(2):
             sums_and_gelu(1, g, act1)
-
-        def early_messages(g):
-            early = {t: messages("y_early%d%d" % (g, t), t, hidden0[g : g + 1], 4 + 2 * g + i) for i, t in enumerate((first, second))}
-            for t in (first, second):
-                scatter(t, early[t], g * GROUP)
-
-        early_messages(0)
-        clear_page(third, tile("page%d" % third, [P, T], F32, tag="y_early0%d" % first))
-        nc.gpsimd.memset(twins[0][:, last // 2, :, :].rearrange("p c o -> p (c o)").bitcast(I32), 0)
-        turn_and_smooth(1, 0, act1, h_pairs1)
-        early_messages(1)
-        turn_and_smooth(1, 1, act1, h_pairs1)
+        for g in range(2):
+            turn_and_smooth(1, g, act1, h_pairs1)
         for g in range(2):
             weave(g, h_pairs1, woven1[:, g * GROUP : (g + 1) * GROUP, :])
         hidden1 = [quantise_hidden("1", woven1)]

@@ -173,10 +173,10 @@ def tile_list_msg_gelu_gateP_kernel(tc, tab_words, tab_scales, ws, wt_words, wt_
             gates[t] = gate
             nc.sync.dma_start(out=gate[:], in_=g_rows[t])
 
-        load_gate(second, tile("gate_a", [P, T], F32, tag="pairs0"))
-        load_gate(third, placed.tile([P, T], F32, name="gate_b", align_bytes=64, offset=8 * T + 8 * HALF))
+        load_gate(first, tile("gate_a", [P, T], F32, tag="pairs0"))
+        load_gate(second, placed.tile([P, T], F32, name="gate_b", align_bytes=64, offset=8 * T + 8 * HALF))
         move_scales(1)
-        load_gate(last, tile("gate_c", [P, T], F32, tag="dst_pairs1"))
+        load_gate(third, tile("gate_c", [P, T], F32, tag="dst_pairs1"))
 
         def sums_and_gelu(h, g, act):
             blocks = (2 * g, 2 * g + 1)
@@ -289,20 +289,20 @@ def tile_list_msg_gelu_gateP_kernel(tc, tab_words, tab_scales, ws, wt_words, wt_
             sums_and_gelu(0, g, act0)
             turn_and_smooth(0, g, act0, h_pairs0)
             weave(g, h_pairs0, woven0[:, g * GROUP : (g + 1) * GROUP, :])
-        gather_gate(second)
-        load_gate(first, tile("gate_d", [P, T], F32, tag="pairs0"))
-        gather_gate(third)
-        gather_gate(last)
-        hidden0 = [quantise_hidden("0", woven0, "dst_pairs1")]
         gather_gate(first)
+        load_gate(last, tile("gate_d", [P, T], F32, tag="pairs0"))
+        gather_gate(second)
+        gather_gate(third)
+        hidden0 = [quantise_hidden("0", woven0, "dst_pairs1")]
+        gather_gate(last)
         nc.gpsimd.memset(twins[0][:, last // 2, :, :].rearrange("p c o -> p (c o)").bitcast(I32), 0)
         act1, h_pairs1 = hidden_tiles(1)
         woven1 = tile("h_bf1", [P, HALF, PACK], BF16)
-        scatter(first, messages("y_first0", first, hidden0, 4), 0)
-        clear_page(third, tile("page%d" % third, [P, T], F32, tag="y_first0"))
-        scatter(second, messages("y_second0", second, hidden0, 5, "pairs0"), 0)
         for g in range(2):
             sums_and_gelu(1, g, act1)
+        scatter(first, messages("y_first0", first, hidden0, 4), 0)
+        clear_page(third, tile("page%d" % third, [P, T], F32, tag="y_first0"))
+        scatter(second, messages("y_second0", second, hidden0, 5), 0)
         for g in range(2):
             turn_and_smooth(1, g, act1, h_pairs1)
         for g in range(2):

@@ -124,11 +124,11 @@ def tile_list_msg_gelu_gateP_kernel(tc, tab_words, tab_scales, ws, wt_words, wt_
         nc.sync.dma_start(out=wt_w[:], in_=wt_words.rearrange("a p r i -> p a (r i)").bitcast(I32))
 
         v_w = {}
-        pairs0 = tile("pairs0", [P, 2, HALF], U32)
+        pairs0 = [tile("pairs0", [P, HALF], U32), tile("dst_pairs0", [P, HALF], U32)]
         for u in (1, 0):
-            gather_words(u, 0, pairs0[:, u, :])
+            gather_words(u, 0, pairs0[u][:])
         for u in (1, 0):
-            v_w[u, 0] = part_words(pairs0[:, u, :], tile("v_w%d0" % u, [P, 2, 2 * HALF], U8))
+            v_w[u, 0] = part_words(pairs0[u][:], tile("v_w%d0" % u, [P, 2, 2 * HALF], U8))
 
         ws_w = tile("ws_w", [P, 2, R], U32)
         ws_s = tile("ws_s", [P, 2, R], U8)

@@ -19,6 +19,7 @@ GELU = mybir.ActivationFunctionType.Gelu_apprx_tanh
 COPY = mybir.ActivationFunctionType.Copy
 
 P = 128
+ALIGN = 256
 PACK = 4
 QUADS = 4
 HALF = 512
@@ -41,7 +42,7 @@ def tile_list_msg_gelu_gateP_kernel(tc, tab_words, tab_scales, ws, wt_words, wt_
         psum = ctx.enter_context(tc.psum_pool(name="psum", bufs=1))
 
         def tile(name, shape, dtype, tag=None):
-            return keep.tile(shape, dtype, name=name, tag=tag or name, align_bytes=64)
+            return keep.tile(shape, dtype, name=name, tag=tag or name, align_bytes=ALIGN)
 
         src_list = tile("src_list", [P, J // LIST_ROWS], U16)
         dst_list = tile("dst_list", [P, J // LIST_ROWS], U16)
@@ -79,7 +80,7 @@ def tile_list_msg_gelu_gateP_kernel(tc, tab_words, tab_scales, ws, wt_words, wt_
                 out=wt_s[32 * q : 32 * q + 4, :, :].bitcast(I32),
                 in_=wt_scales[:, 4 * q : 4 * q + 4, :].bitcast(I32).rearrange("a q r -> q a r"),
             )
-        ws_raw.append(load_ws(1, placed.tile([P, PACK, R], F32, name="ws_raw1", align_bytes=64, offset=8 * T)))
+        ws_raw.append(load_ws(1, placed.tile([P, PACK, R], F32, name="ws_raw1", align_bytes=ALIGN, offset=8 * T)))
 
         wgo_t = tile("wgo_t", [P, P, RUN], F32)
         for b in range(RUN // PACK):
@@ -151,12 +152,12 @@ def tile_list_msg_gelu_gateP_kernel(tc, tab_words, tab_scales, ws, wt_words, wt_
         quantise_ws(1)
         moved.append(tile("moved1", [P, 2, J], U8, tag="ws_bf1"))
         nc.gpsimd.memset(moved[1][:].rearrange("p a c -> p (a c)").bitcast(I32), 0)
-        src_pairs1 = placed.tile([P, HALF], U32, name="src_pairs1", align_bytes=64, offset=8 * T)
+        src_pairs1 = placed.tile([P, HALF], U32, name="src_pairs1", align_bytes=ALIGN, offset=8 * T)
         gather_words(0, 1, src_pairs1[:])
-        v_w[1, 1] = part_words(dst_pairs1[:], placed.tile([P, 2, 2 * HALF], U8, name="v_w11", align_bytes=64, offset=8 * T + 4 * HALF))
+        v_w[1, 1] = part_words(dst_pairs1[:], placed.tile([P, 2, 2 * HALF], U8, name="v_w11", align_bytes=ALIGN, offset=8 * T + 4 * HALF))
         v_w[0, 1] = part_words(src_pairs1[:], tile("v_w01", [P, 2, 2 * HALF], U8))
 
-        wd_bf = placed.tile([P, PACK * N], BF16, name="wd_bf", align_bytes=64, offset=4 * T - PACK * N)
+        wd_bf = placed.tile([P, PACK * N], BF16, name="wd_bf", align_bytes=ALIGN, offset=4 * T - PACK * N)
         for b in range(2):
             nc.scalar.copy(
                 out=wd_bf[:].rearrange("p (t b m j) -> p b m j t", t=PACK, b=2, j=PACK)[:, b],
@@ -174,7 +175,7 @@ def tile_list_msg_gelu_gateP_kernel(tc, tab_words, tab_scales, ws, wt_words, wt_
             nc.sync.dma_start(out=gate[:], in_=g_rows[t])
 
         load_gate(first, tile("gate_a", [P, T], F32, tag="pairs0"))
-        load_gate(second, placed.tile([P, T], F32, name="gate_b", align_bytes=64, offset=8 * T + 8 * HALF))
+        load_gate(second, placed.tile([P, T], F32, name="gate_b", align_bytes=ALIGN, offset=8 * T + 8 * HALF))
         move_scales(1)
         load_gate(third, tile("gate_c", [P, T], F32, tag="dst_pairs1"))
 
@@ -282,7 +283,7 @@ def tile_list_msg_gelu_gateP_kernel(tc, tab_words, tab_scales, ws, wt_words, wt_
                     weave_twins(0, slice(0, SIDE), nc.scalar.copy, U32)
 
         for i, t in enumerate((first, second)):
-            clear_page(t, placed.tile([P, T], F32, name="page%d" % t, align_bytes=64, offset=4 * T * i))
+            clear_page(t, placed.tile([P, T], F32, name="page%d" % t, align_bytes=ALIGN, offset=4 * T * i))
         act0, h_pairs0 = hidden_tiles(0)
         woven0 = tile("h_bf0", [P, HALF, PACK], BF16)
         for g in range(2):

@@ -70,7 +70,8 @@ def tile_list_msg_gelu_gateP_kernel(tc, tab_words, tab_scales, ws, wt_words, wt_
 
         wgo_runs = tile("wgo_runs", [P, RUN], F32)
         nc.sync.dma_start(out=wgo_runs[:], in_=wgo[0].rearrange("(p i) -> p i", i=RUN))
-        ws_raw = [load_ws(0, tile("ws_raw0", [P, PACK, R], F32))]
+        stage_at = 14 * T
+        ws_raw = [load_ws(0, placed.tile([P, PACK, R], F32, name="ws_raw0", align_bytes=ALIGN, offset=stage_at + ALIGN))]
         tab_w = tile("tab_w", [P, T], I32)
         nc.sync.dma_start(out=tab_w[:], in_=tab_words[0].rearrange("p t i -> p (t i)").bitcast(I32))
         sm_t = tile("sm_t", [P, PACK], F32)
@@ -81,14 +82,6 @@ def tile_list_msg_gelu_gateP_kernel(tc, tab_words, tab_scales, ws, wt_words, wt_
                 in_=wt_scales[:, 4 * q : 4 * q + 4, :].bitcast(I32).rearrange("a q r -> q a r"),
             )
         ws_raw.append(load_ws(1, placed.tile([P, PACK, R], F32, name="ws_raw1", align_bytes=ALIGN, offset=8 * T)))
-
-        wgo_t = tile("wgo_t", [P, P, RUN], F32)
-        for b in range(RUN // PACK):
-            spread = psum.tile([P, PACK, P], F32, name="spread%d" % b, tag="bank%d" % (PACK + b))
-            for i in range(PACK):
-                column = wgo_runs[:, PACK * b + i : PACK * b + i + 1]
-                nc.tensor.transpose(spread[:, i, :], column.to_broadcast([P, P]), identity[:])
-            nc.scalar.copy(out=wgo_t[:, :, PACK * b : PACK * (b + 1)], in_=spread[:].rearrange("c i p -> c p i"))
 
         moved = [tile("moved0", [P, 2, J], U8)]
         nc.vector.memset(moved[0][:].rearrange("p a c -> p (a c)").bitcast(I32), 0)
@@ -134,12 +127,24 @@ def tile_list_msg_gelu_gateP_kernel(tc, tab_words, tab_scales, ws, wt_words, wt_
         ws_w = tile("ws_w", [P, 2, R], U32)
         ws_s = tile("ws_s", [P, 2, R], U8)
         ws_bf = [tile("ws_bf%d" % a, [P, PACK * R], BF16) for a in range(2)]
-        for a in range(2):
+
+        def round_ws(a):
             nc.scalar.copy(
                 out=ws_bf[a][:].rearrange("p (c i j) -> p c j i", i=4, j=PACK),
                 in_=ws_raw[a][:].rearrange("p j (c i) -> p c j i", i=4),
             )
-        wd_raw = tile("wd_raw", [P, 2, PACK, N // 2], F32, tag="ws_raw0")
+
+        round_ws(0)
+        wgo_t = placed.tile([P, P, RUN], F32, name="wgo_t", align_bytes=ALIGN, offset=stage_at + 4 * T)
+        for b in range(RUN // PACK):
+            spread = psum.tile([P, PACK, P], F32, name="spread%d" % b, tag="bank%d" % (PACK + b))
+            for i in range(PACK):
+                column = wgo_runs[:, PACK * b + i : PACK * b + i + 1]
+                nc.tensor.transpose(spread[:, i, :], column.to_broadcast([P, P]), identity[:])
+            nc.scalar.copy(out=wgo_t[:, :, PACK * b : PACK * (b + 1)], in_=spread[:].rearrange("c i p -> c p i"))
+
+        round_ws(1)
+        wd_raw = placed.tile([P, 2, PACK, N // 2], F32, name="wd_raw", align_bytes=ALIGN, offset=stage_at)
         for b in range(2):
             nc.sync.dma_start(out=wd_raw[:, b, :, :], in_=wd[:, b * N // 2 : (b + 1) * N // 2].rearrange("(p j) n -> p j n", j=PACK))
 
@@ -213,7 +218,7 @@ def tile_list_msg_gelu_gateP_kernel(tc, tab_words, tab_scales, ws, wt_words, wt_
             nc.scalar.copy(out=woven.bitcast(U32), in_=pairs[g][:].bitcast(U32).rearrange("p u c o -> p c (u o)"))
 
         def hidden_tiles(h):
-            act = tile("act%d" % h, [P, PACK, PACK, P], F32, tag="ws_raw0")
+            act = placed.tile([P, PACK, PACK, P], F32, name="act%d" % h, align_bytes=ALIGN, offset=stage_at)
             pairs = [tile("h_pairs%d%d" % (h, g), [P, 2, GROUP, 2], BF16) for g in range(2)]
             return act, pairs
 
@@ -311,7 +316,7 @@ def tile_list_msg_gelu_gateP_kernel(tc, tab_words, tab_scales, ws, wt_words, wt_
         hidden1 = [quantise_hidden("1", woven1)]
         scatter(third, messages("y_third0", third, hidden0, 0, "h_pairs11"), 0)
         later = {t: messages("y_later%d" % t, t, hidden1, 2 + i) for i, t in enumerate((first, second, third))}
-        y_last = tile("y_last", [P, J], F32, tag="ws_raw0")
+        y_last = placed.tile([P, J], F32, name="y_last", align_bytes=ALIGN, offset=stage_at)
         for h, hidden in enumerate((hidden0, hidden1)):
             second_stage("y_last_sum%d" % h, last, hidden, y_last[:, h * HALF : (h + 1) * HALF], 1 + PACK * h)
         for t in (first, second, third):

@@ -56,7 +56,6 @@ def tile_list_msg_gelu_gateP_kernel(tc, tab_words, tab_scales, ws, wt_words, wt_
             out=tab_s[96:128, :].bitcast(I32),
             in_=tab_scales.bitcast(I32).rearrange("a b t -> b a t"),
         )
-        nc.sync.dma_start(dst_list[:], offs2)
         nc.vector.memset(tab_s[0:96, :].bitcast(I32), 0)
         warm = tile("warm", [P, 2], F32)
         nc.gpsimd.memset(warm[:, 0:1], 0.0)
@@ -68,10 +67,11 @@ def tile_list_msg_gelu_gateP_kernel(tc, tab_words, tab_scales, ws, wt_words, wt_
             nc.sync.dma_start(out=raw[:], in_=ws[512 * a : 512 * (a + 1), :].rearrange("(p j) r -> p j r", j=PACK))
             return raw
 
-        wgo_runs = tile("wgo_runs", [P, RUN], F32)
-        nc.sync.dma_start(out=wgo_runs[:], in_=wgo[0].rearrange("(p i) -> p i", i=RUN))
         stage_at = 14 * T
         ws_raw = [load_ws(0, placed.tile([P, PACK, R], F32, name="ws_raw0", align_bytes=ALIGN, offset=stage_at + ALIGN))]
+        nc.sync.dma_start(dst_list[:], offs2)
+        wgo_runs = tile("wgo_runs", [P, RUN], F32)
+        nc.sync.dma_start(out=wgo_runs[:], in_=wgo[0].rearrange("(p i) -> p i", i=RUN))
         tab_w = tile("tab_w", [P, T], I32)
         nc.sync.dma_start(out=tab_w[:], in_=tab_words[0].rearrange("p t i -> p (t i)").bitcast(I32))
         sm_t = tile("sm_t", [P, PACK], F32)
@@ -101,16 +101,15 @@ def tile_list_msg_gelu_gateP_kernel(tc, tab_words, tab_scales, ws, wt_words, wt_
             nc.vector.tensor_copy(parted[:].bitcast(U16), pairs.bitcast(U16).rearrange("p (n d) -> p d n", d=2))
             return parted
 
-        packed = [tile("packed%d" % h, [P, J], U8) for h in range(2)]
-        for h in range(2):
-            for u in range(2):
-                nc.vector.tensor_copy(packed[h][:, u * HALF : (u + 1) * HALF], tab_s[:].indirect(lists[u][:, list_cols(h)]))
+        packed = tile("packed", [P, 2, J], U8)
+        for u in range(2):
+            nc.vector.tensor_copy(packed[:, u, :], tab_s[:].indirect(lists[u][:]))
 
         def move_scales(h):
             for q in range(QUADS):
                 nc.sync.dma_start(
-                    out=moved[h][32 * q : 32 * q + 4, :, :].bitcast(I32),
-                    in_=packed[h][96 + 8 * q : 104 + 8 * q, :].bitcast(I32),
+                    out=moved[h][32 * q : 32 * q + 4, :, :].bitcast(I32).rearrange("p a (u c) -> p (a u) c", u=2),
+                    in_=packed[96 + 8 * q : 104 + 8 * q, :, h * HALF : (h + 1) * HALF].bitcast(I32),
                 )
 
         move_scales(0)

from contextlib import ExitStack

import concourse.mybir as mybir
from concourse.masks import make_identity

K, R, N, T, J = 1024, 512, 512, 2048, 1024
FLOPS = 2 * J * R * (2 * K + N)

F32 = mybir.dt.float32
BF16 = mybir.dt.bfloat16
I32 = mybir.dt.int32
U32 = mybir.dt.uint32
U16 = mybir.dt.uint16
U8 = mybir.dt.uint8
FP8X4 = mybir.dt.float8_e4m3fn_x4
FP4X4 = mybir.dt.float4_e2m1fn_x4
MULT = mybir.AluOpType.mult
GELU = mybir.ActivationFunctionType.Gelu_apprx_tanh
COPY = mybir.ActivationFunctionType.Copy

P = 128
ALIGN = 256
PACK = 4
QUADS = 4
HALF = 512
GROUP = HALF // 2
LIST_ROWS = 16
OUT_CHUNKS = (512, 512, 512, 256, 256)
VECTOR_CHUNKS = 2
SIDE = T // 2
RUN = J // P
ORDER = (2, 0, 1, 3)
TURN_BANKS = (4, 6, 6, 0)


def tile_list_msg_gelu_gateP_kernel(tc, tab_words, tab_scales, ws, wt_words, wt_scales, sm, wd, gT, wgo, offs, offs2, out_0, out_1, out_2):
    nc = tc.nc

    with ExitStack() as ctx:
        keep = ctx.enter_context(tc.tile_pool(name="keep", bufs=1))
        placed = ctx.enter_context(tc.tile_pool(name="placed", bufs=1))
        psum = ctx.enter_context(tc.psum_pool(name="psum", bufs=1))

        def tile(name, shape, dtype, tag=None):
            return keep.tile(shape, dtype, name=name, tag=tag or name, align_bytes=ALIGN)

        src_list = tile("src_list", [P, J // LIST_ROWS], U16)
        dst_list = tile("dst_list", [P, J // LIST_ROWS], U16)
        lists = (src_list, dst_list)
        first, second, third, last = ORDER
        wt_s = tile("wt_s", [P, 2, R], U8)
        nc.vector.memset(wt_s[:].rearrange("p a r -> p (a r)").bitcast(I32), 0)
        tab_s = tile("tab_s", [P, T], U8, tag="act")
        nc.sync.dma_start(src_list[:], offs)
        nc.sync.dma_start(
            out=tab_s[96:128, :].bitcast(I32),
            in_=tab_scales.bitcast(I32).rearrange("a b t -> b a t"),
        )
        nc.vector.memset(tab_s[0:96, :].bitcast(I32), 0)
        warm = tile("warm", [P, 2], F32)
        nc.gpsimd.memset(warm[:, 0:1], 0.0)
        nc.scalar.activation(out=warm[:, 1:2], in_=warm[:, 0:1], func=GELU)
        identity = tile("identity", [P, P], F32)
        make_identity(nc, identity[:])

        def load_ws(a, raw):
            nc.sync.dma_start(out=raw[:], in_=ws[512 * a : 512 * (a + 1), :].rearrange("(p j) r -> p j r", j=PACK))
            return raw

        stage_at = 14 * T
        ws_raw = [load_ws(0, placed.tile([P, PACK, R], F32, name="ws_raw0", align_bytes=ALIGN, offset=stage_at + ALIGN))]
        nc.sync.dma_start(dst_list[:], offs2)
        wgo_runs = tile("wgo_runs", [P, RUN], F32)
        nc.sync.dma_start(out=wgo_runs[:], in_=wgo[0].rearrange("(p i) -> p i", i=RUN))
        tab_w = tile("tab_w", [P, T], I32)
        nc.sync.dma_start(out=tab_w[:], in_=tab_words[0].rearrange("p t i -> p (t i)").bitcast(I32))
        sm_t = tile("sm_t", [P, PACK], F32)
        nc.sync.dma_start(out=sm_t[:], in_=sm.rearrange("(p t) -> p t", t=PACK))
        for q in range(QUADS):
            nc.sync.dma_start(
                out=wt_s[32 * q : 32 * q + 4, :, :].bitcast(I32),
                in_=wt_scales[:, 4 * q : 4 * q + 4, :].bitcast(I32).rearrange("a q r -> q a r"),
            )
        ws_raw.append(load_ws(1, placed.tile([P, PACK, R], F32, name="ws_raw1", align_bytes=ALIGN, offset=8 * T)))

        moved = [tile("moved0", [P, 2, J], U8)]
        nc.vector.memset(moved[0][:].rearrange("p a c -> p (a c)").bitcast(I32), 0)
        pages = {}

        def clear_page(t, page):
            pages[t] = page
            nc.gpsimd.memset(page[:], 0.0)

        def list_cols(h):
            return slice(h * HALF // LIST_ROWS, (h + 1) * HALF // LIST_ROWS)

        def gather_words(u, h, pairs):
            nc.vector.tensor_copy(pairs, tab_w[:].bitcast(U32).indirect(lists[u][:, list_cols(h)]))

        def part_words(pairs, parted):
            nc.vector.tensor_copy(parted[:].bitcast(U16), pairs.bitcast(U16).rearrange("p (n d) -> p d n", d=2))
            return parted

        packed = tile("packed", [P, 2, J], U8)
        for u in range(2):
            nc.vector.tensor_copy(packed[:, u, :], tab_s[:].indirect(lists[u][:]))

        def move_scales(h):
            for q in range(QUADS):
                nc.sync.dma_start(
                    out=moved[h][32 * q : 32 * q + 4, :, :].bitcast(I32).rearrange("p a (u c) -> p (a u) c", u=2),
                    in_=packed[96 + 8 * q : 104 + 8 * q, :, h * HALF : (h + 1) * HALF].bitcast(I32),
                )

        move_scales(0)
        wt_w = tile("wt_w", [P, 2, R], I32, tag="act")
        nc.sync.dma_start(out=wt_w[:], in_=wt_words.rearrange("a p r i -> p a (r i)").bitcast(I32))

        v_w = {}
        pairs0 = [tile("pairs0", [P, HALF], U32), tile("dst_pairs0", [P, HALF], U32)]
        for u in (1, 0):
            gather_words(u, 0, pairs0[u][:])
        for u in (1, 0):
            v_w[u, 0] = part_words(pairs0[u][:], tile("v_w%d0" % u, [P, 2, 2 * HALF], U8))

        ws_w = tile("ws_w", [P, 2, R], U32)
        ws_s = tile("ws_s", [P, 2, R], U8)
        ws_bf = [tile("ws_bf%d" % a, [P, PACK * R], BF16) for a in range(2)]

        def round_ws(a):
            nc.scalar.copy(
                out=ws_bf[a][:].rearrange("p (c i j) -> p c j i", i=4, j=PACK),
                in_=ws_raw[a][:].rearrange("p j (c i) -> p c j i", i=4),
            )

        round_ws(0)
        wgo_t = placed.tile([P, P, RUN], F32, name="wgo_t", align_bytes=ALIGN, offset=stage_at + 4 * T)
        for b in range(RUN // PACK):
            spread = psum.tile([P, PACK, P], F32, name="spread%d" % b, tag="bank%d" % (PACK + b))
            for i in range(PACK):
                column = wgo_runs[:, PACK * b + i : PACK * b + i + 1]
                nc.tensor.transpose(spread[:, i, :], column.to_broadcast([P, P]), identity[:])
            nc.scalar.copy(out=wgo_t[:, :, PACK * b : PACK * (b + 1)], in_=spread[:].rearrange("c i p -> c p i"))

        round_ws(1)
        wd_raw = placed.tile([P, 2, PACK, N // 2], F32, name="wd_raw", align_bytes=ALIGN, offset=stage_at)
        for b in range(2):
            nc.sync.dma_start(out=wd_raw[:, b, :, :], in_=wd[:, b * N // 2 : (b + 1) * N // 2].rearrange("(p j) n -> p j n", j=PACK))

        def quantise_ws(a):
            nc.vector.quantize_mx(out=ws_w[:, a, :].bitcast(FP8X4), scales=ws_s[:, a, :], in_=ws_bf[a][:])

        quantise_ws(0)
        dst_pairs1 = tile("dst_pairs1", [P, HALF], U32)
        gather_words(1, 1, dst_pairs1[:])
        quantise_ws(1)
        moved.append(tile("moved1", [P, 2, J], U8, tag="ws_bf1"))
        nc.gpsimd.memset(moved[1][:].rearrange("p a c -> p (a c)").bitcast(I32), 0)
        src_pairs1 = placed.tile([P, HALF], U32, name="src_pairs1", align_bytes=ALIGN, offset=8 * T)
        gather_words(0, 1, src_pairs1[:])
        v_w[1, 1] = part_words(dst_pairs1[:], placed.tile([P, 2, 2 * HALF], U8, name="v_w11", align_bytes=ALIGN, offset=8 * T + 4 * HALF))
        v_w[0, 1] = part_words(src_pairs1[:], tile("v_w01", [P, 2, 2 * HALF], U8))

        wd_bf = placed.tile([P, PACK * N], BF16, name="wd_bf", align_bytes=ALIGN, offset=4 * T - PACK * N)
        for b in range(2):
            nc.scalar.copy(
                out=wd_bf[:].rearrange("p (t b m j) -> p b m j t", t=PACK, b=2, j=PACK)[:, b],
                in_=wd_raw[:, b, :, :].rearrange("p j (m t) -> p m j t", t=PACK),
            )
        wd_w = tile("wd_w", [P, N], U32)
        wd_s = tile("wd_s", [P, N], U8)
        nc.vector.quantize_mx(out=wd_w[:].bitcast(FP8X4), scales=wd_s[:], in_=wd_bf[:])

        gates = {}
        g_rows = gT.rearrange("(p t) c -> t p c", t=PACK)

        def load_gate(t, gate):
            gates[t] = gate
            nc.sync.dma_start(out=gate[:], in_=g_rows[t])

        load_gate(first, tile("gate_a", [P, T], F32, tag="pairs0"))
        load_gate(second, placed.tile([P, T], F32, name="gate_b", align_bytes=ALIGN, offset=8 * T + 8 * HALF))
        move_scales(1)
        load_gate(third, tile("gate_c", [P, T], F32, tag="dst_pairs1"))

        def sums_and_gelu(h, g, act):
            blocks = (2 * g, 2 * g + 1)
            accs = {i: psum.tile([P, R], F32, name="a%d%d" % (h, i), tag="bank%d" % i) for i in blocks}
            for u, (w_w, w_s) in ((1, (wt_w, wt_s)), (0, (ws_w, ws_s))):
                for i in blocks:
                    for a in range(2):
                        nc.tensor.matmul_mx(
                            out=accs[i][:],
                            lhsT=v_w[u, h][:, a, 2 * i * P : 2 * (i + 1) * P].bitcast(FP4X4),
                            lhsT_scale=moved[h][:, a, u * HALF + i * P : u * HALF + (i + 1) * P],
                            rhs=w_w[:, a, :].bitcast(FP8X4),
                            rhs_scale=w_s[:, a, :],
                            start=(u, a) == (1, 0),
                            stop=(u, a) == (0, 1),
                        )
            for i in blocks:
                nc.scalar.activation(out=act[:, i, :, :], in_=accs[i][:].rearrange("p (m t) -> p t m", t=PACK), func=GELU)

        def turn_and_smooth(h, g, act, pairs):
            for u in range(2):
                turned = psum.tile([P, 2, 2, P], F32, name="t%d%d%d" % (h, g, u), tag="bank%d" % (TURN_BANKS[2 * h + g] + u))
                for o in range(2):
                    for i in range(2):
                        nc.tensor.transpose(turned[:, o, i, :], act[:, 2 * g + i, 2 * u + o, :], identity[:])
                for o in range(2):
                    t = 2 * u + o
                    nc.scalar.activation(
                        out=pairs[g][:, u, :, o], in_=turned[:, o, :, :].rearrange("p i m -> p (i m)"), func=COPY, scale=sm_t[:, t : t + 1]
                    )

        def weave(g, pairs, woven):
            nc.scalar.copy(out=woven.bitcast(U32), in_=pairs[g][:].bitcast(U32).rearrange("p u c o -> p c (u o)"))

        def hidden_tiles(h):
            act = placed.tile([P, PACK, PACK, P], F32, name="act%d" % h, align_bytes=ALIGN, offset=stage_at)
            pairs = [tile("h_pairs%d%d" % (h, g), [P, 2, GROUP, 2], BF16) for g in range(2)]
            return act, pairs

        def quantise_hidden(name, woven, tag=None):
            width = woven.shape[1]
            h_w = tile("h_w" + name, [P, width], U32, tag=tag)
            h_s = tile("h_s" + name, [P, width], U8)
            nc.vector.quantize_mx(out=h_w[:].bitcast(FP8X4), scales=h_s[:], in_=woven[:].rearrange("p c t -> p (c t)"))
            return h_w, h_s

        def second_stage(name, t, parts, y, bank):
            acc = psum.tile([P, y.shape[1]], F32, name=name, tag="bank%d" % bank)
            m_cols = slice(t * P, (t + 1) * P)
            start = 0
            for h_w, h_s in parts:
                stop = start + h_w.shape[1]
                nc.tensor.matmul_mx(
                    out=acc[:, start:stop],
                    lhsT=wd_w[:, m_cols].bitcast(FP8X4),
                    lhsT_scale=wd_s[:, m_cols],
                    rhs=h_w[:].bitcast(FP8X4),
                    rhs_scale=h_s[:],
                    start=True,
                    stop=True,
                )
                start = stop
            nc.scalar.copy(out=y, in_=acc[:])

        factors = {}

        def gather_gate(t, tag=None):
            factors[t] = tile("factor%d" % t, [P, J], F32, tag=tag)
            nc.vector.tensor_tensor(factors[t][:], gates[t][:].indirect(src_list[:]), wgo_t[:].rearrange("c p i -> c (p i)"), MULT)

        out_rows = out_0.rearrange("(p t) c -> t p c", t=PACK)
        out_bf = [tile("out_bf%d" % c, [P, SIDE, PACK], BF16) for c in range(2)]
        twins = [tile("twins%d" % c, [P, 2, SIDE, 2], BF16, tag=tag) for c, tag in enumerate(("h_bf0", "pairs0"))]
        starts = [sum(OUT_CHUNKS[:i]) for i in range(len(OUT_CHUNKS) + 1)]
        chunks = [slice(starts[i], starts[i + 1]) for i in range(len(OUT_CHUNKS))]

        def woven_out(cols):
            side, start = divmod(cols.start, SIDE)
            return out_bf[side][:, start : start + cols.stop - cols.start, :]

        def messages(name, t, parts, bank, tag=None):
            y = tile(name, [P, sum(h_w.shape[1] for h_w, h_s in parts)], F32, tag=tag)
            second_stage(name + "_sum", t, parts, y[:], bank)
            return y

        def scatter(t, y, start):
            stop = start + y.shape[1]
            offsets = dst_list[:, start // LIST_ROWS : stop // LIST_ROWS]
            nc.vector.tensor_tensor(pages[t][:].indirect(offsets), y[:], factors[t][:, start:stop], MULT)

        def weave_twins(c, part, copy, words):
            copy(
                out=out_bf[c][:, part, :].bitcast(words),
                in_=twins[c][:, :, part, :].bitcast(words).rearrange("p u c o -> p c (u o)"),
            )

        def finish_page(t):
            nc.sync.dma_start(out=out_rows[t], in_=pages[t][:])
            for c in range(2 if t != last else 0):
                source = pages[t][:, c * SIDE : (c + 1) * SIDE]
                nc.scalar.copy(out=twins[c][:, t // 2, :, t % 2], in_=source)
                if (t, c) == (third, 0):
                    weave_twins(0, slice(0, SIDE), nc.scalar.copy, U32)

        for i, t in enumerate((first, second)):
            clear_page(t, placed.tile([P, T], F32, name="page%d" % t, align_bytes=ALIGN, offset=4 * T * i))
        act0, h_pairs0 = hidden_tiles(0)
        woven0 = tile("h_bf0", [P, HALF, PACK], BF16)
        for g in range(2):
            sums_and_gelu(0, g, act0)
            turn_and_smooth(0, g, act0, h_pairs0)
            weave(g, h_pairs0, woven0[:, g * GROUP : (g + 1) * GROUP, :])
        gather_gate(first)
        load_gate(last, tile("gate_d", [P, T], F32, tag="pairs0"))
        gather_gate(second)
        gather_gate(third)
        hidden0 = [quantise_hidden("0", woven0, "dst_pairs1")]
        gather_gate(last)
        nc.gpsimd.memset(twins[0][:, last // 2, :, :].rearrange("p c o -> p (c o)").bitcast(I32), 0)
        act1, h_pairs1 = hidden_tiles(1)
        woven1 = tile("h_bf1", [P, HALF, PACK], BF16)
        for g in range(2):
            sums_and_gelu(1, g, act1)
        scatter(first, messages("y_first0", first, hidden0, 4), 0)
        clear_page(third, tile("page%d" % third, [P, T], F32, tag="y_first0"))
        scatter(second, messages("y_second0", second, hidden0, 5), 0)
        for g in range(2):
            turn_and_smooth(1, g, act1, h_pairs1)
        for g in range(2):
            weave(g, h_pairs1, woven1[:, g * GROUP : (g + 1) * GROUP, :])
        hidden1 = [quantise_hidden("1", woven1)]
        scatter(third, messages("y_third0", third, hidden0, 0, "h_pairs11"), 0)
        later = {t: messages("y_later%d" % t, t, hidden1, 2 + i) for i, t in enumerate((first, second, third))}
        y_last = placed.tile([P, J], F32, name="y_last", align_bytes=ALIGN, offset=stage_at)
        for h, hidden in enumerate((hidden0, hidden1)):
            second_stage("y_last_sum%d" % h, last, hidden, y_last[:, h * HALF : (h + 1) * HALF], 1 + PACK * h)
        for t in (first, second, third):
            scatter(t, later[t], HALF)
            finish_page(t)
        pages[last] = pages[first]
        scatter(last, y_last, 0)
        finish_page(last)
        upper = [slice(cols.start - SIDE, cols.stop - SIDE) for cols in chunks[VECTOR_CHUNKS:]]

        def round_upper(i):
            nc.scalar.copy(out=twins[1][:, last // 2, upper[i], last % 2], in_=pages[last][:, chunks[VECTOR_CHUNKS + i]])

        round_upper(0)
        for i in range(len(upper)):
            if i + 1 < len(upper):
                round_upper(i + 1)
            weave_twins(1, upper[i], nc.scalar.copy, U32)

        out_w = tile("out_w", [P, T], U32)
        out_s = tile("out_s", [P, HALF], U8)
        code_rows = out_1[0].rearrange("p t i -> p (t i)").bitcast(I32)

        def quantise_out(cols):
            for start in range(cols.start, cols.stop, GROUP):
                piece = slice(start, start + GROUP)
                plane, place = divmod(start, HALF)
                nc.vector.quantize_mx(
                    out=out_w[:, piece].bitcast(FP8X4),
                    scales=out_s[4 * plane : P, place : place + GROUP],
                    in_=woven_out(piece).rearrange("p c t -> p (c t)"),
                )
            nc.sync.dma_start(out=code_rows[:, cols], in_=out_w[:, cols].bitcast(I32))

        for cols in chunks[:VECTOR_CHUNKS]:
            nc.vector.tensor_copy(woven_out(cols)[:, :, last], pages[last][:, cols])
        for cols in chunks:
            quantise_out(cols)
        for q in range(QUADS):
            queue = nc.scalar if q % 2 else nc.sync
            queue.dma_start(
                out=out_2[0, 4 * q : 4 * q + 4, :].bitcast(I32).rearrange("r (a c) -> a r c", a=T // HALF),
                in_=out_s[32 * q : 32 * q + 16, :].bitcast(I32),
            )
